import numpy as np
import ml_dtypes


def mxq(x, axis, fmt="e4m3"):
    dtype, down = {"e4m3": (ml_dtypes.float8_e4m3fn, 7), "e5m2": (ml_dtypes.float8_e5m2, 14)}[fmt]
    v = np.moveaxis(np.asarray(x, np.float32).astype(ml_dtypes.bfloat16).astype(np.float64), axis, -1)
    blocks = v.reshape(v.shape[:-1] + (-1, 32))
    amax = np.abs(blocks).max(-1, keepdims=True)
    byte = np.maximum(np.where(amax > 0, np.frexp(amax)[1] - 1 + 127, 0) - down, 1)
    scale = np.exp2(byte - 127.0)
    codes = (blocks / scale).astype(np.float32).astype(dtype).astype(np.float64)
    return np.moveaxis((codes * scale).reshape(v.shape), -1, axis)


WIDE = False


def mx_kscale(k):
    if not WIDE:
        return np.ones(k)
    levels = np.array([10, -10, 5, -5, 0])
    if k % 512:
        return np.exp2(np.random.permutation(np.resize(levels, k // 32))).repeat(32)
    a = np.empty((k // 512, 16))
    for p in range(k // 512):
        a[p, :8] = np.random.permutation(np.resize(levels, 8))
        for g in range(8):
            far = levels[np.abs(levels - a[p, g]) >= 10]
            a[p, g + 8] = far[np.random.randint(len(far))]
    return np.exp2(a.ravel()).repeat(32)


def f64(x):
    return np.asarray(x).astype(np.float64)


def striped(idx):
    return np.tile(idx.reshape(-1, 16).T, (8, 1)).astype(np.uint16)


def unstriped(offs):
    return offs[:16].T.reshape(-1).astype(np.int64)


def striped8(idx):
    return np.concatenate([x.reshape(-1, 16).T for x in idx]).astype(np.uint16)


def runs(offs, k):
    lists = np.stack([offs[16 * r : 16 * r + 16].T.reshape(-1) for r in range(8)]).astype(np.int64)
    return lists[np.arange(k) % 512 // 64]


def pack_weight(w):
    k, n = w.shape
    w = f64(np.asarray(w, np.float32).astype(ml_dtypes.bfloat16)).reshape(k // 32, 32, n)
    amax = np.abs(w).max(1)
    byte = np.clip(np.where(amax > 0, np.frexp(amax)[1] - 1 + 127 - 7, 1), 1, 254)
    scaled = (w * np.exp2(127.0 - byte)[:, None, :]).reshape(k, n).astype(np.float32)
    words = np.ascontiguousarray(scaled.reshape(k // 512, 128, 4, n).transpose(0, 1, 3, 2)).astype(ml_dtypes.float8_e4m3fn).view(np.uint8)
    return words, np.ascontiguousarray(byte.astype(np.uint8).reshape(k // 512, 16, n))


def unpack_weight(words, scales):
    g, p, n, _ = words.shape
    vals = np.ascontiguousarray(words).view(ml_dtypes.float8_e4m3fn).astype(np.float64) * np.repeat(np.exp2(scales.astype(np.float64) - 127.0), 8, axis=1)[..., None]
    return vals.transpose(0, 1, 3, 2).reshape(g * 512, n)


def gelu(v):
    return 0.5 * v * (1.0 + np.tanh(np.sqrt(2.0 / np.pi) * (v + 0.044715 * v**3)))


K, T, S, V, N, H = 512, 2048, 512, 256, 512, 512


def setup_inputs():
    n = np.random.standard_normal
    s = mx_kscale(K)[:, None]
    u = mx_kscale(H)
    packed_xT = pack_weight(n((K, T)) * s)
    return {
        "x_words": packed_xT[0],
        "x_scales": packed_xT[1],
        "w1": (n((K, H)) / np.sqrt(K) / s * u).astype(np.float32),
        "wt": np.repeat(np.random.uniform(0.3, 1.2, (8, V)), 64, axis=0).astype(np.float32),
        "w2": (n((H, N)) / np.sqrt(H) / u[:, None]).astype(np.float32),
        "offs": striped(np.random.permutation(T)[:S]),
        "take": striped8(np.stack([np.random.permutation(S)[:V] for _ in range(8)])),
    }


def reference(x_words, x_scales, w1, wt, w2, offs, take):
    xq = unpack_weight(x_words, x_scales)[:, unstriped(offs)]
    y = mxq(f64(w1), 0, "e4m3").T @ xq
    e = (gelu(y[np.arange(H)[:, None], runs(take, H)])) * f64(wt)
    d = np.zeros((H, S))
    d[np.arange(H)[:, None], runs(take, H)] = e
    z = y + d
    return mxq(f64(w2), 0, "e4m3").T @ mxq(z, 0, "e4m3")

@@ -1,0 +1,178 @@
+from contextlib import ExitStack
+
+import concourse.mybir as mybir
+
+K, T, S, V, N, H = 512, 2048, 512, 256, 512, 512
+FLOPS = 2 * K * H * S + 2 * H * N * S
+
+F32 = mybir.dt.float32
+BF16 = mybir.dt.bfloat16
+I32 = mybir.dt.int32
+U32 = mybir.dt.uint32
+U16 = mybir.dt.uint16
+U8 = mybir.dt.uint8
+FP8X4 = mybir.dt.float8_e4m3fn_x4
+GELU = mybir.ActivationFunctionType.Gelu_apprx_tanh
+ADD = mybir.AluOpType.add
+MULT = mybir.AluOpType.mult
+
+P = 128
+PACK = 4
+HALF = S // 2
+QUARTER = S // 4
+
+
+def tile_picked_headmod_gelu_p_kernel(tc, x_words, x_scales, w1, wt, w2, offs, take, out):
+    nc = tc.nc
+    with ExitStack() as ctx:
+        keep = ctx.enter_context(tc.tile_pool(name="keep", bufs=1))
+        psum = ctx.enter_context(tc.psum_pool(name="psum", bufs=1))
+
+        offs_t = keep.tile([P, S // 16], U16, name="offs_t")
+        take_t = keep.tile([P, V // 16], U16, name="take_t")
+        xs_win = keep.tile([P, T], U8, name="xs_win", tag="scale_slot", align_bytes=64)
+        xw_win = keep.tile([P, T], I32, name="xw_win", align_bytes=64)
+        w1_raw = keep.tile([P, PACK, H], F32, name="w1_raw", tag="w_raw")
+        wt_t = keep.tile([P, V], F32, name="wt_t")
+
+        nc.vector.memset(xs_win[:].bitcast(I32), 0)
+        nc.sync.dma_start(out=w1_raw[:], in_=w1.rearrange("(p j) c -> p j c", j=PACK))
+        for q in range(4):
+            nc.sync.dma_start(
+                out=xs_win[32 * q : 32 * q + 4, :].bitcast(I32),
+                in_=x_scales[0, 4 * q : 4 * q + 4, :].bitcast(I32),
+            )
+        nc.sync.dma_start(offs_t[:], offs)
+        nc.sync.dma_start(out=xw_win[:], in_=x_words[0].rearrange("p c r -> p (c r)").bitcast(I32))
+        nc.sync.dma_start(take_t[:], take)
+        nc.sync.dma_start(out=wt_t[:], in_=wt.rearrange("(p f) v -> p f v", f=PACK)[:, 0, :])
+
+        warm = keep.tile([P, 8], F32, name="warm")
+        warm_out = keep.tile([P, 8], F32, name="warm_out")
+        nc.vector.memset(warm[:], 0.0)
+        nc.scalar.activation(warm_out[:], warm[:], GELU)
+
+        xs = keep.tile([P, S], U8, name="xs", align_bytes=64)
+        nc.vector.tensor_copy(xs[:], xs_win[:].indirect(offs_t[:]))
+
+        w1_view = w1_raw[:].rearrange("p j (m t) -> p m j t", t=PACK)
+        w1_codes = keep.tile([P, H], U32, name="w1_codes", tag="scale_slot", align_bytes=64)
+        w1_scales = keep.tile([P, H], U8, name="w1_scales", align_bytes=64)
+        for u in range(2):
+            grouped = keep.tile([P, 2, P, PACK], BF16, name=f"w1_grouped{u}", align_bytes=64)
+            dst = grouped[:].rearrange("p e m j -> p m j e")
+            src = w1_view[:, :, :, 2 * u : 2 * u + 2]
+            if u == 0:
+                nc.vector.tensor_copy(out=dst, in_=src)
+            else:
+                nc.scalar.copy(out=dst, in_=src)
+            cols = slice(2 * P * u, 2 * P * (u + 1))
+            nc.vector.quantize_mx(
+                out=w1_codes[:, cols].bitcast(FP8X4), scales=w1_scales[:, cols], in_=grouped[:].rearrange("p e m j -> p (e m j)")
+            )
+
+        w2_raw = keep.tile([P, PACK, N], F32, name="w2_raw", tag="w_raw")
+        nc.sync.dma_start(out=w2_raw[:], in_=w2.rearrange("(p j) c -> p j c", j=PACK))
+
+        xw = keep.tile([P, S], U32, name="xw", align_bytes=64)
+        for h in range(2):
+            nc.vector.tensor_copy(
+                xw[:, h * HALF : (h + 1) * HALF],
+                xw_win[:].bitcast(U32).indirect(offs_t[:, h * HALF // 16 : (h + 1) * HALF // 16]),
+            )
+
+        def first_layer(t, cols, bank):
+            width = cols.stop - cols.start
+            acc = psum.tile([P, S], F32, name=f"y_acc{bank}", tag=f"bank{bank}")
+            stat = slice(t * P, (t + 1) * P)
+            nc.tensor.matmul_mx(
+                out=acc[:, 0:width],
+                lhsT=w1_codes[:, stat].bitcast(FP8X4),
+                lhsT_scale=w1_scales[:, stat],
+                rhs=xw[:, cols].bitcast(FP8X4),
+                rhs_scale=xs[:, cols],
+                start=True,
+                stop=True,
+            )
+            nc.scalar.copy(out=rows[t][:, cols], in_=acc[:, 0:width])
+
+        rows = [keep.tile([P, S], F32, name=f"rows{t}") for t in range(PACK)]
+        first_layer(0, slice(0, HALF), 0)
+        first_layer(0, slice(HALF, S), 1)
+        for t in range(1, PACK):
+            first_layer(t, slice(0, S), t + 1)
+
+        picked = [keep.tile([P, 2, V], F32, name=f"picked{u}") for u in range(2)]
+        for t in range(PACK):
+            nc.vector.tensor_copy(picked[t // 2][:, t % 2, :], rows[t][:].indirect(take_t[:]))
+        weighted = []
+        for u in range(2):
+            act = keep.tile([P, 2, V], F32, name=f"act{u}")
+            nc.scalar.activation(act[:], picked[u][:], GELU)
+            e = keep.tile([P, 2, V], F32, name=f"weighted{u}")
+            nc.vector.tensor_tensor(e[:], act[:], wt_t[:].unsqueeze(1).to_broadcast([P, 2, V]), MULT)
+            weighted.append(e)
+
+        w2_grouped = keep.tile([P, N, PACK], BF16, name="w2_grouped", align_bytes=64)
+        w2_codes = keep.tile([P, N], U32, name="w2_codes", align_bytes=64)
+        w2_scales = keep.tile([P, N], U8, name="w2_scales", align_bytes=64)
+        for b in range(4):
+            cols = slice(b * P, (b + 1) * P)
+            nc.scalar.copy(
+                out=w2_grouped[:, cols, :].rearrange("p (c i) j -> p c j i", i=4),
+                in_=w2_raw[:, :, cols].rearrange("p j (c i) -> p c j i", i=4),
+            )
+
+        z = [keep.tile([P, HALF, PACK], BF16, name=f"z{h}", align_bytes=64) for h in range(2)]
+        for t in range(PACK):
+            nc.vector.tensor_tensor(
+                rows[t][:].indirect(take_t[:]), picked[t // 2][:, t % 2, :], weighted[t // 2][:, t % 2, :], ADD
+            )
+            if t == 1:
+                nc.vector.quantize_mx(
+                    out=w2_codes[:].bitcast(FP8X4), scales=w2_scales[:], in_=w2_grouped[:].rearrange("p c j -> p (c j)")
+                )
+            if t < 2:
+                for h in range(2):
+                    nc.scalar.copy(out=z[h][:, :, t], in_=rows[t][:, h * HALF : (h + 1) * HALF])
+            else:
+                nc.scalar.copy(out=z[1][:, :, t], in_=rows[t][:, HALF:S])
+                for c in range(2):
+                    cols = slice(c * QUARTER, (c + 1) * QUARTER)
+                    nc.vector.tensor_copy(out=z[0][:, cols, t], in_=rows[t][:, cols])
+
+        z_codes = [keep.tile([P, HALF], U32, name=f"z_codes{h}", align_bytes=64) for h in range(2)]
+        z_scales = [keep.tile([P, HALF], U8, name=f"z_scales{h}", align_bytes=64) for h in range(2)]
+        for c in range(2):
+            cols = slice(c * QUARTER, (c + 1) * QUARTER)
+            nc.vector.quantize_mx(
+                out=z_codes[0][:, cols].bitcast(FP8X4),
+                scales=z_scales[0][:, cols],
+                in_=z[0][:, cols, :].rearrange("p c j -> p (c j)"),
+            )
+        nc.vector.quantize_mx(
+            out=z_codes[1][:].bitcast(FP8X4), scales=z_scales[1][:], in_=z[1][:].rearrange("p c j -> p (c j)")
+        )
+
+        out_view = out.rearrange("(b p) s -> p b s", p=P)
+        for h in range(2):
+            for pair in range(2):
+                bank = (5 + 2 * h + pair) % 8
+                acc = psum.tile([P, 2, HALF], F32, name=f"out_acc{h}{pair}", tag=f"bank{bank}")
+                for i in range(2):
+                    stat = slice((2 * pair + i) * P, (2 * pair + i + 1) * P)
+                    nc.tensor.matmul_mx(
+                        out=acc[:, i, :],
+                        lhsT=w2_codes[:, stat].bitcast(FP8X4),
+                        lhsT_scale=w2_scales[:, stat],
+                        rhs=z_codes[h][:].bitcast(FP8X4),
+                        rhs_scale=z_scales[h][:],
+                        start=True,
+                        stop=True,
+                    )
+                res = keep.tile([P, 2, HALF], F32, name=f"res{h}{pair}")
+                if pair == 0:
+                    nc.scalar.copy(out=res[:], in_=acc[:])
+                else:
+                    nc.vector.tensor_copy(out=res[:], in_=acc[:])
+                nc.sync.dma_start(out=out_view[:, 2 * pair : 2 * pair + 2, h * HALF : (h + 1) * HALF], in_=res[:])

@@ -26,13 +26,14 @@ def tile_picked_headmod_gelu_p_kernel(tc, x_words, x_scales, w1, wt, w2, offs, t
     nc = tc.nc
     with ExitStack() as ctx:
         keep = ctx.enter_context(tc.tile_pool(name="keep", bufs=1))
+        shared = ctx.enter_context(tc.tile_pool(name="shared", bufs=1))
         psum = ctx.enter_context(tc.psum_pool(name="psum", bufs=1))
 
         offs_t = keep.tile([P, S // 16], U16, name="offs_t")
         take_t = keep.tile([P, V // 16], U16, name="take_t")
         xs_win = keep.tile([P, T], U8, name="xs_win", tag="scale_slot", align_bytes=64)
         xw_win = keep.tile([P, T], I32, name="xw_win", align_bytes=64)
-        w1_raw = keep.tile([P, PACK, H], F32, name="w1_raw", tag="w_raw")
+        w1_raw = keep.tile([P, PACK, H], F32, name="w1_raw")
         wt_t = keep.tile([P, V], F32, name="wt_t")
 
         nc.vector.memset(xs_win[:].bitcast(I32), 0)
@@ -46,6 +47,8 @@ def tile_picked_headmod_gelu_p_kernel(tc, x_words, x_scales, w1, wt, w2, offs, t
         nc.sync.dma_start(out=xw_win[:], in_=x_words[0].rearrange("p c r -> p (c r)").bitcast(I32))
         nc.sync.dma_start(take_t[:], take)
         nc.sync.dma_start(out=wt_t[:], in_=wt.rearrange("(p f) v -> p f v", f=PACK)[:, 0, :])
+        w2_raw = shared.tile([P, PACK, N], F32, name="w2_raw", offset=0, align_bytes=64)
+        nc.sync.dma_start(out=w2_raw[:], in_=w2.rearrange("(p j) c -> p j c", j=PACK))
 
         warm = keep.tile([P, 8], F32, name="warm")
         warm_out = keep.tile([P, 8], F32, name="warm_out")
@@ -70,9 +73,6 @@ def tile_picked_headmod_gelu_p_kernel(tc, x_words, x_scales, w1, wt, w2, offs, t
             nc.vector.quantize_mx(
                 out=w1_codes[:, cols].bitcast(FP8X4), scales=w1_scales[:, cols], in_=grouped[:].rearrange("p e m j -> p (e m j)")
             )
-
-        w2_raw = keep.tile([P, PACK, N], F32, name="w2_raw", tag="w_raw")
-        nc.sync.dma_start(out=w2_raw[:], in_=w2.rearrange("(p j) c -> p j c", j=PACK))
 
         xw = keep.tile([P, S], U32, name="xw", align_bytes=64)
         for h in range(2):
@@ -107,15 +107,13 @@ def tile_picked_headmod_gelu_p_kernel(tc, x_words, x_scales, w1, wt, w2, offs, t
             nc.vector.tensor_copy(picked[t // 2][:, t % 2, :], rows[t][:].indirect(take_t[:]))
         weighted = []
         for u in range(2):
-            act = keep.tile([P, 2, V], F32, name=f"act{u}")
+            act = keep.tile([P, 2, V], F32, name=f"act{u}", tag=f"act_slot{u}", align_bytes=64)
             nc.scalar.activation(act[:], picked[u][:], GELU)
-            e = keep.tile([P, 2, V], F32, name=f"weighted{u}")
-            nc.vector.tensor_tensor(e[:], act[:], wt_t[:].unsqueeze(1).to_broadcast([P, 2, V]), MULT)
-            weighted.append(e)
+            product = keep.tile([P, 2, V], F32, name=f"weighted{u}")
+            nc.vector.tensor_tensor(product[:], act[:], wt_t[:].unsqueeze(1).to_broadcast([P, 2, V]), MULT)
+            weighted.append(product)
 
-        w2_grouped = keep.tile([P, N, PACK], BF16, name="w2_grouped", align_bytes=64)
-        w2_codes = keep.tile([P, N], U32, name="w2_codes", align_bytes=64)
-        w2_scales = keep.tile([P, N], U8, name="w2_scales", align_bytes=64)
+        w2_grouped = keep.tile([P, N, PACK], BF16, name="w2_grouped", tag="act_slot1", align_bytes=64)
         for b in range(4):
             cols = slice(b * P, (b + 1) * P)
             nc.scalar.copy(
@@ -123,56 +121,58 @@ def tile_picked_headmod_gelu_p_kernel(tc, x_words, x_scales, w1, wt, w2, offs, t
                 in_=w2_raw[:, :, cols].rearrange("p j (c i) -> p c j i", i=4),
             )
 
-        z = [keep.tile([P, HALF, PACK], BF16, name=f"z{h}", align_bytes=64) for h in range(2)]
+        z = [shared.tile([P, HALF, PACK], BF16, name=f"z{h}", offset=h * HALF * PACK * 2, align_bytes=64) for h in range(2)]
+
         for t in range(PACK):
             nc.vector.tensor_tensor(
                 rows[t][:].indirect(take_t[:]), picked[t // 2][:, t % 2, :], weighted[t // 2][:, t % 2, :], ADD
             )
-            if t == 1:
-                nc.vector.quantize_mx(
-                    out=w2_codes[:].bitcast(FP8X4), scales=w2_scales[:], in_=w2_grouped[:].rearrange("p c j -> p (c j)")
-                )
-            if t < 2:
-                for h in range(2):
-                    nc.scalar.copy(out=z[h][:, :, t], in_=rows[t][:, h * HALF : (h + 1) * HALF])
-            else:
-                nc.scalar.copy(out=z[1][:, :, t], in_=rows[t][:, HALF:S])
-                for c in range(2):
-                    cols = slice(c * QUARTER, (c + 1) * QUARTER)
-                    nc.vector.tensor_copy(out=z[0][:, cols, t], in_=rows[t][:, cols])
+            for h in range(2 if t < 2 else 1):
+                nc.scalar.copy(out=z[h][:, :, t], in_=rows[t][:, h * HALF : (h + 1) * HALF])
 
+        w2_codes = keep.tile([P, N], U32, name="w2_codes", align_bytes=64)
+        w2_scales = keep.tile([P, N], U8, name="w2_scales", align_bytes=64)
+        nc.vector.quantize_mx(
+            out=w2_codes[:].bitcast(FP8X4), scales=w2_scales[:], in_=w2_grouped[:].rearrange("p c j -> p (c j)")
+        )
         z_codes = [keep.tile([P, HALF], U32, name=f"z_codes{h}", align_bytes=64) for h in range(2)]
         z_scales = [keep.tile([P, HALF], U8, name=f"z_scales{h}", align_bytes=64) for h in range(2)]
-        for c in range(2):
-            cols = slice(c * QUARTER, (c + 1) * QUARTER)
+
+        def quantize_z(h, cols):
             nc.vector.quantize_mx(
-                out=z_codes[0][:, cols].bitcast(FP8X4),
-                scales=z_scales[0][:, cols],
-                in_=z[0][:, cols, :].rearrange("p c j -> p (c j)"),
+                out=z_codes[h][:, cols].bitcast(FP8X4),
+                scales=z_scales[h][:, cols],
+                in_=z[h][:, cols, :].rearrange("p c j -> p (c j)"),
             )
-        nc.vector.quantize_mx(
-            out=z_codes[1][:].bitcast(FP8X4), scales=z_scales[1][:], in_=z[1][:].rearrange("p c j -> p (c j)")
-        )
+
+        quantize_z(0, slice(0, HALF))
+        nc.vector.tensor_copy(out=z[1][:, :, 2], in_=rows[2][:, HALF:S])
+        for c in range(2):
+            nc.vector.tensor_copy(
+                out=z[1][:, c * QUARTER : (c + 1) * QUARTER, 3],
+                in_=rows[3][:, HALF + c * QUARTER : HALF + (c + 1) * QUARTER],
+            )
+        for c in range(2):
+            quantize_z(1, slice(c * QUARTER, (c + 1) * QUARTER))
 
         out_view = out.rearrange("(b p) s -> p b s", p=P)
-        for h in range(2):
-            for pair in range(2):
-                bank = (5 + 2 * h + pair) % 8
-                acc = psum.tile([P, 2, HALF], F32, name=f"out_acc{h}{pair}", tag=f"bank{bank}")
-                for i in range(2):
-                    stat = slice((2 * pair + i) * P, (2 * pair + i + 1) * P)
-                    nc.tensor.matmul_mx(
-                        out=acc[:, i, :],
-                        lhsT=w2_codes[:, stat].bitcast(FP8X4),
-                        lhsT_scale=w2_scales[:, stat],
-                        rhs=z_codes[h][:].bitcast(FP8X4),
-                        rhs_scale=z_scales[h][:],
-                        start=True,
-                        stop=True,
-                    )
-                res = keep.tile([P, 2, HALF], F32, name=f"res{h}{pair}")
-                if pair == 0:
-                    nc.scalar.copy(out=res[:], in_=acc[:])
-                else:
-                    nc.vector.tensor_copy(out=res[:], in_=acc[:])
-                nc.sync.dma_start(out=out_view[:, 2 * pair : 2 * pair + 2, h * HALF : (h + 1) * HALF], in_=res[:])
+        pieces = [(0, 0, 2), (0, 2, 4), (1, 0, 2), (1, 2, 3), (1, 3, 4)]
+        for n, (h, b0, b1) in enumerate(pieces):
+            acc = psum.tile([P, b1 - b0, HALF], F32, name=f"out_acc{n}", tag=f"bank{(5 + n) % 8}")
+            for b in range(b0, b1):
+                stat = slice(b * P, (b + 1) * P)
+                nc.tensor.matmul_mx(
+                    out=acc[:, b - b0, :],
+                    lhsT=w2_codes[:, stat].bitcast(FP8X4),
+                    lhsT_scale=w2_scales[:, stat],
+                    rhs=z_codes[h][:].bitcast(FP8X4),
+                    rhs_scale=z_scales[h][:],
+                    start=True,
+                    stop=True,
+                )
+            res = keep.tile([P, b1 - b0, HALF], F32, name=f"res{n}")
+            if n in (2, 4):
+                nc.vector.tensor_copy(out=res[:], in_=acc[:])
+            else:
+                nc.scalar.copy(out=res[:], in_=acc[:])
+            nc.sync.dma_start(out=out_view[:, b0:b1, h * HALF : (h + 1) * HALF], in_=res[:])

@@ -32,7 +32,7 @@ def tile_picked_headmod_gelu_p_kernel(tc, x_words, x_scales, w1, wt, w2, offs, t
         offs_t = keep.tile([P, S // 16], U16, name="offs_t")
         take_t = keep.tile([P, V // 16], U16, name="take_t")
         xs_win = keep.tile([P, T], U8, name="xs_win", tag="scale_slot", align_bytes=64)
-        xw_win = keep.tile([P, T], I32, name="xw_win", align_bytes=64)
+        xw_win = keep.tile([P, T], I32, name="xw_win", tag="word_slot", align_bytes=64)
         w1_raw = keep.tile([P, PACK, H], F32, name="w1_raw")
         wt_t = keep.tile([P, V], F32, name="wt_t")
 
@@ -59,61 +59,53 @@ def tile_picked_headmod_gelu_p_kernel(tc, x_words, x_scales, w1, wt, w2, offs, t
         nc.vector.tensor_copy(xs[:], xs_win[:].indirect(offs_t[:]))
 
         w1_view = w1_raw[:].rearrange("p j (m t) -> p m j t", t=PACK)
-        w1_codes = keep.tile([P, H], U32, name="w1_codes", tag="scale_slot", align_bytes=64)
-        w1_scales = keep.tile([P, H], U8, name="w1_scales", align_bytes=64)
-        for u in range(2):
-            grouped = keep.tile([P, 2, P, PACK], BF16, name=f"w1_grouped{u}", align_bytes=64)
-            dst = grouped[:].rearrange("p e m j -> p m j e")
-            src = w1_view[:, :, :, 2 * u : 2 * u + 2]
-            if u == 0:
-                nc.vector.tensor_copy(out=dst, in_=src)
-            else:
-                nc.scalar.copy(out=dst, in_=src)
-            cols = slice(2 * P * u, 2 * P * (u + 1))
-            nc.vector.quantize_mx(
-                out=w1_codes[:, cols].bitcast(FP8X4), scales=w1_scales[:, cols], in_=grouped[:].rearrange("p e m j -> p (e m j)")
-            )
+        w1_grouped = [keep.tile([P, 2, P, PACK], BF16, name=f"w1_grouped{u}", align_bytes=64) for u in range(2)]
+        nc.vector.tensor_copy(out=w1_grouped[0][:].rearrange("p e m j -> p m j e"), in_=w1_view[:, :, :, 0:2])
+        nc.scalar.copy(out=w1_grouped[1][:].rearrange("p e m j -> p m j e"), in_=w1_view[:, :, :, 2:4])
 
+        def quantize_w1(u, slot):
+            codes = keep.tile([P, 2 * P], U32, name=f"w1_codes{u}", tag=slot, align_bytes=64)
+            scales = keep.tile([P, 2 * P], U8, name=f"w1_scales{u}", align_bytes=64)
+            nc.vector.quantize_mx(
+                out=codes[:].bitcast(FP8X4), scales=scales[:], in_=w1_grouped[u][:].rearrange("p e m j -> p (e m j)")
+            )
+            return codes, scales
+
+        w1_mx = [quantize_w1(0, "scale_slot")]
         xw = keep.tile([P, S], U32, name="xw", align_bytes=64)
         for h in range(2):
             nc.vector.tensor_copy(
                 xw[:, h * HALF : (h + 1) * HALF],
                 xw_win[:].bitcast(U32).indirect(offs_t[:, h * HALF // 16 : (h + 1) * HALF // 16]),
             )
+        w1_mx.append(quantize_w1(1, "word_slot"))
 
-        def first_layer(t, cols, bank):
-            width = cols.stop - cols.start
-            acc = psum.tile([P, S], F32, name=f"y_acc{bank}", tag=f"bank{bank}")
-            stat = slice(t * P, (t + 1) * P)
+        rows = [keep.tile([P, S], F32, name=f"rows{t}") for t in range(PACK)]
+        first = [(t, slice(h * HALF, (h + 1) * HALF)) for h in range(2) for t in range(2)]
+        first.extend((t, slice(0, S)) for t in range(2, PACK))
+        for bank, (t, cols) in enumerate(first):
+            acc = psum.tile([P, cols.stop - cols.start], F32, name=f"y_acc{bank}", tag=f"bank{bank}")
+            codes, scales = w1_mx[t // 2]
+            stat = slice((t % 2) * P, (t % 2 + 1) * P)
             nc.tensor.matmul_mx(
-                out=acc[:, 0:width],
-                lhsT=w1_codes[:, stat].bitcast(FP8X4),
-                lhsT_scale=w1_scales[:, stat],
+                out=acc[:],
+                lhsT=codes[:, stat].bitcast(FP8X4),
+                lhsT_scale=scales[:, stat],
                 rhs=xw[:, cols].bitcast(FP8X4),
                 rhs_scale=xs[:, cols],
                 start=True,
                 stop=True,
             )
-            nc.scalar.copy(out=rows[t][:, cols], in_=acc[:, 0:width])
-
-        rows = [keep.tile([P, S], F32, name=f"rows{t}") for t in range(PACK)]
-        first_layer(0, slice(0, HALF), 0)
-        first_layer(0, slice(HALF, S), 1)
-        for t in range(1, PACK):
-            first_layer(t, slice(0, S), t + 1)
+            nc.scalar.copy(out=rows[t][:, cols], in_=acc[:])
 
         picked = [keep.tile([P, 2, V], F32, name=f"picked{u}") for u in range(2)]
         for t in range(PACK):
             nc.vector.tensor_copy(picked[t // 2][:, t % 2, :], rows[t][:].indirect(take_t[:]))
-        weighted = []
+        act = [keep.tile([P, 2, V], F32, name=f"act{u}") for u in range(2)]
         for u in range(2):
-            act = keep.tile([P, 2, V], F32, name=f"act{u}", tag=f"act_slot{u}", align_bytes=64)
-            nc.scalar.activation(act[:], picked[u][:], GELU)
-            product = keep.tile([P, 2, V], F32, name=f"weighted{u}")
-            nc.vector.tensor_tensor(product[:], act[:], wt_t[:].unsqueeze(1).to_broadcast([P, 2, V]), MULT)
-            weighted.append(product)
+            nc.scalar.activation(act[u][:], picked[u][:], GELU)
 
-        w2_grouped = keep.tile([P, N, PACK], BF16, name="w2_grouped", tag="act_slot1", align_bytes=64)
+        w2_grouped = keep.tile([P, N, PACK], BF16, name="w2_grouped", align_bytes=64)
         for b in range(4):
             cols = slice(b * P, (b + 1) * P)
             nc.scalar.copy(
@@ -121,58 +113,64 @@ def tile_picked_headmod_gelu_p_kernel(tc, x_words, x_scales, w1, wt, w2, offs, t
                 in_=w2_raw[:, :, cols].rearrange("p j (c i) -> p c j i", i=4),
             )
 
-        z = [shared.tile([P, HALF, PACK], BF16, name=f"z{h}", offset=h * HALF * PACK * 2, align_bytes=64) for h in range(2)]
+        bounds = [0, QUARTER, HALF, S]
+        pieces = [slice(a, b) for a, b in zip(bounds, bounds[1:])]
+        z = [
+            shared.tile([P, c.stop - c.start, PACK], BF16, name=f"z{c.start}", offset=c.start * PACK * 2, align_bytes=64)
+            for c in pieces
+        ]
+        weighted = keep.tile([P, PACK, V], F32, name="weighted")
 
+        def weigh(t):
+            nc.vector.tensor_tensor(weighted[:, t, :], act[t // 2][:, t % 2, :], wt_t[:], MULT)
+
+        weigh(0)
+        weigh(1)
         for t in range(PACK):
-            nc.vector.tensor_tensor(
-                rows[t][:].indirect(take_t[:]), picked[t // 2][:, t % 2, :], weighted[t // 2][:, t % 2, :], ADD
-            )
-            for h in range(2 if t < 2 else 1):
-                nc.scalar.copy(out=z[h][:, :, t], in_=rows[t][:, h * HALF : (h + 1) * HALF])
+            nc.vector.tensor_tensor(rows[t][:].indirect(take_t[:]), picked[t // 2][:, t % 2, :], weighted[:, t, :], ADD)
+            if t == 0:
+                weigh(2)
+                weigh(3)
+            for piece, cols in zip(z, pieces):
+                nc.scalar.copy(out=piece[:, :, t], in_=rows[t][:, cols])
 
         w2_codes = keep.tile([P, N], U32, name="w2_codes", align_bytes=64)
         w2_scales = keep.tile([P, N], U8, name="w2_scales", align_bytes=64)
         nc.vector.quantize_mx(
             out=w2_codes[:].bitcast(FP8X4), scales=w2_scales[:], in_=w2_grouped[:].rearrange("p c j -> p (c j)")
         )
-        z_codes = [keep.tile([P, HALF], U32, name=f"z_codes{h}", align_bytes=64) for h in range(2)]
-        z_scales = [keep.tile([P, HALF], U8, name=f"z_scales{h}", align_bytes=64) for h in range(2)]
-
-        def quantize_z(h, cols):
+        z_mx = []
+        for piece, cols in zip(z, pieces):
+            width = cols.stop - cols.start
+            codes = keep.tile([P, width], U32, name=f"z_codes{cols.start}", align_bytes=64)
+            scales = keep.tile([P, width], U8, name=f"z_scales{cols.start}", align_bytes=64)
             nc.vector.quantize_mx(
-                out=z_codes[h][:, cols].bitcast(FP8X4),
-                scales=z_scales[h][:, cols],
-                in_=z[h][:, cols, :].rearrange("p c j -> p (c j)"),
+                out=codes[:].bitcast(FP8X4), scales=scales[:], in_=piece[:].rearrange("p c j -> p (c j)")
             )
-
-        quantize_z(0, slice(0, HALF))
-        nc.vector.tensor_copy(out=z[1][:, :, 2], in_=rows[2][:, HALF:S])
-        for c in range(2):
-            nc.vector.tensor_copy(
-                out=z[1][:, c * QUARTER : (c + 1) * QUARTER, 3],
-                in_=rows[3][:, HALF + c * QUARTER : HALF + (c + 1) * QUARTER],
-            )
-        for c in range(2):
-            quantize_z(1, slice(c * QUARTER, (c + 1) * QUARTER))
+            z_mx.append((codes, scales))
 
         out_view = out.rearrange("(b p) s -> p b s", p=P)
-        pieces = [(0, 0, 2), (0, 2, 4), (1, 0, 2), (1, 2, 3), (1, 3, 4)]
-        for n, (h, b0, b1) in enumerate(pieces):
-            acc = psum.tile([P, b1 - b0, HALF], F32, name=f"out_acc{n}", tag=f"bank{(5 + n) % 8}")
-            for b in range(b0, b1):
-                stat = slice(b * P, (b + 1) * P)
-                nc.tensor.matmul_mx(
-                    out=acc[:, b - b0, :],
-                    lhsT=w2_codes[:, stat].bitcast(FP8X4),
-                    lhsT_scale=w2_scales[:, stat],
-                    rhs=z_codes[h][:].bitcast(FP8X4),
-                    rhs_scale=z_scales[h][:],
-                    start=True,
-                    stop=True,
-                )
-            res = keep.tile([P, b1 - b0, HALF], F32, name=f"res{n}")
-            if n in (2, 4):
-                nc.vector.tensor_copy(out=res[:], in_=acc[:])
-            else:
-                nc.scalar.copy(out=res[:], in_=acc[:])
-            nc.sync.dma_start(out=out_view[:, b0:b1, h * HALF : (h + 1) * HALF], in_=res[:])
+        bank = 0
+        for n, ((codes, scales), cols) in enumerate(zip(z_mx, pieces)):
+            width = cols.stop - cols.start
+            blocks = HALF // width
+            for b0 in range(0, N // P, blocks):
+                acc = psum.tile([P, blocks, width], F32, name=f"out_acc{bank}", tag=f"bank{(6 + bank) % 8}")
+                for i in range(blocks):
+                    stat = slice((b0 + i) * P, (b0 + i + 1) * P)
+                    nc.tensor.matmul_mx(
+                        out=acc[:, i, :],
+                        lhsT=w2_codes[:, stat].bitcast(FP8X4),
+                        lhsT_scale=w2_scales[:, stat],
+                        rhs=codes[:].bitcast(FP8X4),
+                        rhs_scale=scales[:],
+                        start=True,
+                        stop=True,
+                    )
+                res = keep.tile([P, blocks, width], F32, name=f"res{bank}")
+                if bank in (2, 3, 5, 7):
+                    nc.vector.tensor_copy(out=res[:], in_=acc[:])
+                else:
+                    nc.scalar.copy(out=res[:], in_=acc[:])
+                nc.sync.dma_start(out=out_view[:, b0 : b0 + blocks, cols], in_=res[:])
+                bank = bank + 1

@@ -46,9 +46,12 @@ def tile_picked_headmod_gelu_p_kernel(tc, x_words, x_scales, w1, wt, w2, offs, t
         nc.sync.dma_start(offs_t[:], offs)
         nc.sync.dma_start(out=xw_win[:], in_=x_words[0].rearrange("p c r -> p (c r)").bitcast(I32))
         nc.sync.dma_start(take_t[:], take)
+        w2_view = w2.rearrange("(p j) c -> p j c", j=PACK)
+        w2_early = keep.tile([P, PACK, P], F32, name="w2_early")
+        nc.sync.dma_start(out=w2_early[:], in_=w2_view[:, :, 0:P])
         nc.sync.dma_start(out=wt_t[:], in_=wt.rearrange("(p f) v -> p f v", f=PACK)[:, 0, :])
-        w2_raw = shared.tile([P, PACK, N], F32, name="w2_raw", offset=0, align_bytes=64)
-        nc.sync.dma_start(out=w2_raw[:], in_=w2.rearrange("(p j) c -> p j c", j=PACK))
+        w2_raw = shared.tile([P, PACK, N - P], F32, name="w2_raw", offset=0, align_bytes=64)
+        nc.sync.dma_start(out=w2_raw[:], in_=w2_view[:, :, P:N])
 
         warm = keep.tile([P, 8], F32, name="warm")
         warm_out = keep.tile([P, 8], F32, name="warm_out")
@@ -108,9 +111,10 @@ def tile_picked_headmod_gelu_p_kernel(tc, x_words, x_scales, w1, wt, w2, offs, t
         w2_grouped = keep.tile([P, N, PACK], BF16, name="w2_grouped", align_bytes=64)
         for b in range(4):
             cols = slice(b * P, (b + 1) * P)
+            src = w2_early[:] if b == 0 else w2_raw[:, :, (b - 1) * P : b * P]
             nc.scalar.copy(
                 out=w2_grouped[:, cols, :].rearrange("p (c i) j -> p c j i", i=4),
-                in_=w2_raw[:, :, cols].rearrange("p j (c i) -> p c j i", i=4),
+                in_=src.rearrange("p j (c i) -> p c j i", i=4),
             )
 
         bounds = [0, QUARTER, HALF, S]

@@ -26,31 +26,33 @@ def tile_picked_headmod_gelu_p_kernel(tc, x_words, x_scales, w1, wt, w2, offs, t
     nc = tc.nc
     with ExitStack() as ctx:
         keep = ctx.enter_context(tc.tile_pool(name="keep", bufs=1))
-        shared = ctx.enter_context(tc.tile_pool(name="shared", bufs=1))
+        order = ctx.enter_context(tc.tile_pool(name="order", bufs=1))
         psum = ctx.enter_context(tc.psum_pool(name="psum", bufs=1))
 
         offs_t = keep.tile([P, S // 16], U16, name="offs_t")
         take_t = keep.tile([P, V // 16], U16, name="take_t")
         xs_win = keep.tile([P, T], U8, name="xs_win", tag="scale_slot", align_bytes=64)
-        xw_win = keep.tile([P, T], I32, name="xw_win", tag="word_slot", align_bytes=64)
+        xw_win = keep.tile([P, T], I32, name="xw_win", align_bytes=64)
         w1_raw = keep.tile([P, PACK, H], F32, name="w1_raw")
         wt_t = keep.tile([P, V], F32, name="wt_t")
 
         nc.vector.memset(xs_win[:].bitcast(I32), 0)
-        nc.sync.dma_start(out=w1_raw[:], in_=w1.rearrange("(p j) c -> p j c", j=PACK))
+        w1_rows = w1.rearrange("(p j) c -> p j c", j=PACK)
+        nc.sync.dma_start(out=w1_raw[:, 0:2, :], in_=w1_rows[:, 0:2, :])
         for q in range(4):
             nc.sync.dma_start(
                 out=xs_win[32 * q : 32 * q + 4, :].bitcast(I32),
                 in_=x_scales[0, 4 * q : 4 * q + 4, :].bitcast(I32),
             )
         nc.sync.dma_start(offs_t[:], offs)
+        nc.sync.dma_start(out=w1_raw[:, 2:4, :], in_=w1_rows[:, 2:4, :])
         nc.sync.dma_start(out=xw_win[:], in_=x_words[0].rearrange("p c r -> p (c r)").bitcast(I32))
         nc.sync.dma_start(take_t[:], take)
         w2_view = w2.rearrange("(p j) c -> p j c", j=PACK)
         w2_early = keep.tile([P, PACK, P], F32, name="w2_early")
-        nc.sync.dma_start(out=w2_early[:], in_=w2_view[:, :, 0:P])
         nc.sync.dma_start(out=wt_t[:], in_=wt.rearrange("(p f) v -> p f v", f=PACK)[:, 0, :])
-        w2_raw = shared.tile([P, PACK, N - P], F32, name="w2_raw", offset=0, align_bytes=64)
+        nc.sync.dma_start(out=w2_early[:], in_=w2_view[:, :, 0:P])
+        w2_raw = keep.tile([P, PACK, N - P], F32, name="w2_raw")
         nc.sync.dma_start(out=w2_raw[:], in_=w2_view[:, :, P:N])
 
         warm = keep.tile([P, 8], F32, name="warm")
@@ -62,31 +64,30 @@ def tile_picked_headmod_gelu_p_kernel(tc, x_words, x_scales, w1, wt, w2, offs, t
         nc.vector.tensor_copy(xs[:], xs_win[:].indirect(offs_t[:]))
 
         w1_view = w1_raw[:].rearrange("p j (m t) -> p m j t", t=PACK)
-        w1_grouped = [keep.tile([P, 2, P, PACK], BF16, name=f"w1_grouped{u}", align_bytes=64) for u in range(2)]
+        w1_grouped = [
+            keep.tile([P, 2, P, PACK], BF16, name="w1_grouped0", tag="scale_slot", align_bytes=64),
+            keep.tile([P, 2, P, PACK], BF16, name="w1_grouped1", align_bytes=64),
+        ]
         nc.vector.tensor_copy(out=w1_grouped[0][:].rearrange("p e m j -> p m j e"), in_=w1_view[:, :, :, 0:2])
         nc.scalar.copy(out=w1_grouped[1][:].rearrange("p e m j -> p m j e"), in_=w1_view[:, :, :, 2:4])
 
-        def quantize_w1(u, slot):
-            codes = keep.tile([P, 2 * P], U32, name=f"w1_codes{u}", tag=slot, align_bytes=64)
+        def quantize_w1(u):
+            codes = keep.tile([P, 2 * P], U32, name=f"w1_codes{u}", align_bytes=64)
             scales = keep.tile([P, 2 * P], U8, name=f"w1_scales{u}", align_bytes=64)
             nc.vector.quantize_mx(
                 out=codes[:].bitcast(FP8X4), scales=scales[:], in_=w1_grouped[u][:].rearrange("p e m j -> p (e m j)")
             )
             return codes, scales
 
-        w1_mx = [quantize_w1(0, "scale_slot")]
+        w1_mx = [quantize_w1(u) for u in range(2)]
         xw = keep.tile([P, S], U32, name="xw", align_bytes=64)
         for h in range(2):
             nc.vector.tensor_copy(
                 xw[:, h * HALF : (h + 1) * HALF],
                 xw_win[:].bitcast(U32).indirect(offs_t[:, h * HALF // 16 : (h + 1) * HALF // 16]),
             )
-        w1_mx.append(quantize_w1(1, "word_slot"))
 
-        rows = [keep.tile([P, S], F32, name=f"rows{t}") for t in range(PACK)]
-        first = [(t, slice(h * HALF, (h + 1) * HALF)) for h in range(2) for t in range(2)]
-        first.extend((t, slice(0, S)) for t in range(2, PACK))
-        for bank, (t, cols) in enumerate(first):
+        def first_layer(t, cols, bank):
             acc = psum.tile([P, cols.stop - cols.start], F32, name=f"y_acc{bank}", tag=f"bank{bank}")
             codes, scales = w1_mx[t // 2]
             stat = slice((t % 2) * P, (t % 2 + 1) * P)
@@ -99,63 +100,93 @@ def tile_picked_headmod_gelu_p_kernel(tc, x_words, x_scales, w1, wt, w2, offs, t
                 start=True,
                 stop=True,
             )
-            nc.scalar.copy(out=rows[t][:, cols], in_=acc[:])
+            return acc
 
-        picked = [keep.tile([P, 2, V], F32, name=f"picked{u}") for u in range(2)]
-        for t in range(PACK):
-            nc.vector.tensor_copy(picked[t // 2][:, t % 2, :], rows[t][:].indirect(take_t[:]))
-        act = [keep.tile([P, 2, V], F32, name=f"act{u}") for u in range(2)]
-        for u in range(2):
-            nc.scalar.activation(act[u][:], picked[u][:], GELU)
+        halves = [slice(0, HALF), slice(HALF, S)]
+        whole = slice(0, S)
+        rows = [keep.tile([P, S], F32, name=f"rows{t}") for t in range(PACK)]
+        gelu_rows = [
+            keep.tile([P, S], F32, name="gelu_rows0", tag="plane0_slot"),
+            order.tile([P, S], F32, name="gelu_rows1", offset=2048, align_bytes=64),
+        ]
+        for h, cols in enumerate(halves):
+            for t in (2, 3):
+                nc.scalar.copy(out=rows[t][:, cols], in_=first_layer(t, cols, 2 * h + t - 2)[:])
+        dense = [first_layer(t, whole, 4 + t) for t in range(2)]
+        for t in range(2):
+            nc.scalar.activation(gelu_rows[t][:], dense[t][:], GELU)
 
-        w2_grouped = keep.tile([P, N, PACK], BF16, name="w2_grouped", align_bytes=64)
-        for b in range(4):
+        picked = keep.tile([P, 2, V], F32, name="picked")
+        act = keep.tile([P, 2, V], F32, name="act")
+        routed = [keep.tile([P, V], F32, name=f"routed{t}") for t in range(2)]
+        for t in (2, 3):
+            nc.vector.tensor_copy(picked[:, t - 2, :], rows[t][:].indirect(take_t[:]))
+        for t in range(2):
+            nc.vector.tensor_tensor(routed[t][:], gelu_rows[t][:].indirect(take_t[:]), wt_t[:], MULT)
+        nc.scalar.activation(act[:], picked[:], GELU)
+        for t in range(2):
+            nc.scalar.copy(out=rows[t][:], in_=dense[t][:])
+
+        placed = [
+            keep.tile([P, S], F32, name="placed0", tag="plane0_slot"),
+            keep.tile([P, S], F32, name="placed1"),
+        ]
+        for t in range(2):
+            nc.gpsimd.memset(placed[t][:], 0.0)
+
+        def four_at_a_time(grouped, raw):
+            return grouped.rearrange("p (c i) j -> p c j i", i=4), raw.rearrange("p j (c i) -> p c j i", i=4)
+
+        w2_grouped = [
+            keep.tile([P, P, PACK], BF16, name="w2_grouped0", align_bytes=64),
+            order.tile([P, N - P, PACK], BF16, name="w2_grouped1", offset=0, align_bytes=64),
+        ]
+        nc.scalar.copy(*four_at_a_time(w2_grouped[0][:], w2_early[:]))
+        for b in range(3):
             cols = slice(b * P, (b + 1) * P)
-            src = w2_early[:] if b == 0 else w2_raw[:, :, (b - 1) * P : b * P]
-            nc.scalar.copy(
-                out=w2_grouped[:, cols, :].rearrange("p (c i) j -> p c j i", i=4),
-                in_=src.rearrange("p j (c i) -> p c j i", i=4),
-            )
+            nc.scalar.copy(*four_at_a_time(w2_grouped[1][:, cols, :], w2_raw[:, :, cols]))
 
         bounds = [0, QUARTER, HALF, S]
         pieces = [slice(a, b) for a, b in zip(bounds, bounds[1:])]
-        z = [
-            shared.tile([P, c.stop - c.start, PACK], BF16, name=f"z{c.start}", offset=c.start * PACK * 2, align_bytes=64)
-            for c in pieces
-        ]
-        weighted = keep.tile([P, PACK, V], F32, name="weighted")
+        z_all = order.tile([P, S, PACK], BF16, name="z_all", offset=4096, align_bytes=64)
+        z = [z_all[:, c, :] for c in pieces]
 
-        def weigh(t):
-            nc.vector.tensor_tensor(weighted[:, t, :], act[t // 2][:, t % 2, :], wt_t[:], MULT)
-
-        weigh(0)
-        weigh(1)
-        for t in range(PACK):
-            nc.vector.tensor_tensor(rows[t][:].indirect(take_t[:]), picked[t // 2][:, t % 2, :], weighted[:, t, :], ADD)
-            if t == 0:
-                weigh(2)
-                weigh(3)
-            for piece, cols in zip(z, pieces):
-                nc.scalar.copy(out=piece[:, :, t], in_=rows[t][:, cols])
-
-        w2_codes = keep.tile([P, N], U32, name="w2_codes", align_bytes=64)
-        w2_scales = keep.tile([P, N], U8, name="w2_scales", align_bytes=64)
-        nc.vector.quantize_mx(
-            out=w2_codes[:].bitcast(FP8X4), scales=w2_scales[:], in_=w2_grouped[:].rearrange("p c j -> p (c j)")
-        )
-        z_mx = []
+        for t in range(2):
+            nc.vector.tensor_copy(placed[t][:].indirect(take_t[:]), routed[t][:])
+        weighted = order.tile([P, 2, V], F32, name="weighted", offset=3072, align_bytes=64)
+        summed = keep.tile([P, 2, V], F32, name="summed", tag="summed_slot", align_bytes=64)
+        nc.gpsimd.tensor_tensor(weighted[:], act[:], wt_t[:].unsqueeze(1).to_broadcast([P, 2, V]), MULT)
+        nc.gpsimd.tensor_tensor(summed[:], weighted[:], picked[:], ADD)
+        for t in (1, 0):
+            nc.gpsimd.tensor_tensor(z_all[:, :, t], rows[t][:], placed[t][:], ADD)
+        nc.vector.tensor_copy(rows[2][:].indirect(take_t[:]), summed[:, 0, :])
+        nc.scalar.copy(out=z_all[:, :, 2], in_=rows[2][:])
+        nc.vector.tensor_copy(rows[3][:].indirect(take_t[:]), summed[:, 1, :])
         for piece, cols in zip(z, pieces):
+            nc.scalar.copy(out=piece[:, :, 3], in_=rows[3][:, cols])
+
+        w2_codes = keep.tile([P, N], U32, name="w2_codes", tag="summed_slot", align_bytes=64)
+        w2_scales = keep.tile([P, N], U8, name="w2_scales", align_bytes=64)
+        w2_parts = (w2_grouped[0][:], w2_grouped[1][:, 0:P, :], w2_grouped[1][:, P:, :])
+        for grouped, cols in zip(w2_parts, (slice(0, P), slice(P, 2 * P), slice(2 * P, N))):
+            nc.vector.quantize_mx(
+                out=w2_codes[:, cols].bitcast(FP8X4), scales=w2_scales[:, cols], in_=grouped.rearrange("p c j -> p (c j)")
+            )
+
+        def quantize_z(piece, cols):
             width = cols.stop - cols.start
-            codes = keep.tile([P, width], U32, name=f"z_codes{cols.start}", align_bytes=64)
+            slot = "z_codes_second" if cols.start == QUARTER else "z_codes_first_and_last"
+            codes = keep.tile([P, width], U32, name=f"z_codes{cols.start}", tag=slot, align_bytes=64)
             scales = keep.tile([P, width], U8, name=f"z_scales{cols.start}", align_bytes=64)
             nc.vector.quantize_mx(
-                out=codes[:].bitcast(FP8X4), scales=scales[:], in_=piece[:].rearrange("p c j -> p (c j)")
+                out=codes[:].bitcast(FP8X4), scales=scales[:], in_=piece.rearrange("p c j -> p (c j)")
             )
-            z_mx.append((codes, scales))
+            return codes, scales
 
         out_view = out.rearrange("(b p) s -> p b s", p=P)
         bank = 0
-        for n, ((codes, scales), cols) in enumerate(zip(z_mx, pieces)):
+        for piece, cols in zip(z, pieces):
+            codes, scales = quantize_z(piece, cols)
             width = cols.stop - cols.start
             blocks = HALF // width
             for b0 in range(0, N // P, blocks):
@@ -172,7 +203,7 @@ def tile_picked_headmod_gelu_p_kernel(tc, x_words, x_scales, w1, wt, w2, offs, t
                         stop=True,
                     )
                 res = keep.tile([P, blocks, width], F32, name=f"res{bank}")
-                if bank in (2, 3, 5, 7):
+                if bank in (0, 3, 5, 7):
                     nc.vector.tensor_copy(out=res[:], in_=acc[:])
                 else:
                     nc.scalar.copy(out=res[:], in_=acc[:])

@@ -39,19 +39,23 @@ def tile_picked_headmod_gelu_p_kernel(tc, x_words, x_scales, w1, wt, w2, offs, t
         nc.vector.memset(xs_win[:].bitcast(I32), 0)
         w1_rows = w1.rearrange("(p j) c -> p j c", j=PACK)
         nc.sync.dma_start(out=w1_raw[:, 0:2, :], in_=w1_rows[:, 0:2, :])
-        for q in range(4):
-            nc.sync.dma_start(
-                out=xs_win[32 * q : 32 * q + 4, :].bitcast(I32),
-                in_=x_scales[0, 4 * q : 4 * q + 4, :].bitcast(I32),
-            )
+        nc.sync.dma_start(out=xs_win[4:P:8, :].bitcast(I32), in_=x_scales[0].bitcast(I32))
         nc.sync.dma_start(offs_t[:], offs)
         nc.sync.dma_start(out=w1_raw[:, 2:4, :], in_=w1_rows[:, 2:4, :])
         nc.sync.dma_start(out=xw_win[:], in_=x_words[0].rearrange("p c r -> p (c r)").bitcast(I32))
-        nc.sync.dma_start(take_t[:], take)
+        xs_spread = keep.tile([P, S], U8, name="xs_spread", align_bytes=64)
+        nc.vector.tensor_copy(xs_spread[:], xs_win[:].indirect(offs_t[:]))
+        xs = keep.tile([P, S], U8, name="xs", align_bytes=64)
+        nc.vector.memset(xs[:].bitcast(I32), 0)
+        for q in range(4):
+            nc.sync.dma_start(
+                out=xs[32 * q : 32 * q + 4, :].bitcast(I32), in_=xs_spread[32 * q + 4 : 32 * q + 32 : 8, :].bitcast(I32)
+            )
         w2_view = w2.rearrange("(p j) c -> p j c", j=PACK)
         w2_early = keep.tile([P, PACK, P], F32, name="w2_early")
-        nc.sync.dma_start(out=wt_t[:], in_=wt.rearrange("(p f) v -> p f v", f=PACK)[:, 0, :])
         nc.sync.dma_start(out=w2_early[:], in_=w2_view[:, :, 0:P])
+        nc.sync.dma_start(take_t[:], take)
+        nc.sync.dma_start(out=wt_t[:], in_=wt.rearrange("(p f) v -> p f v", f=PACK)[:, 0, :])
         w2_raw = keep.tile([P, PACK, N - P], F32, name="w2_raw")
         nc.sync.dma_start(out=w2_raw[:], in_=w2_view[:, :, P:N])
 
@@ -60,8 +64,6 @@ def tile_picked_headmod_gelu_p_kernel(tc, x_words, x_scales, w1, wt, w2, offs, t
         nc.vector.memset(warm[:], 0.0)
         nc.scalar.activation(warm_out[:], warm[:], GELU)
 
-        xs = keep.tile([P, S], U8, name="xs", align_bytes=64)
-        nc.vector.tensor_copy(xs[:], xs_win[:].indirect(offs_t[:]))
 
         w1_view = w1_raw[:].rearrange("p j (m t) -> p m j t", t=PACK)
         w1_grouped = [
@@ -110,13 +112,27 @@ def tile_picked_headmod_gelu_p_kernel(tc, x_words, x_scales, w1, wt, w2, offs, t
             order.tile([P, S], F32, name="gelu_rows1", offset=2048, align_bytes=64),
         ]
         for h, cols in enumerate(halves):
-            for t in (2, 3):
-                nc.scalar.copy(out=rows[t][:, cols], in_=first_layer(t, cols, 2 * h + t - 2)[:])
+            nc.scalar.copy(out=rows[2][:, cols], in_=first_layer(2, cols, 2 * h)[:])
+            nc.scalar.copy(out=rows[3][:, cols], in_=first_layer(3, cols, 2 * h + 1)[:])
         dense = [first_layer(t, whole, 4 + t) for t in range(2)]
         for t in range(2):
             nc.scalar.activation(gelu_rows[t][:], dense[t][:], GELU)
 
-        picked = keep.tile([P, 2, V], F32, name="picked")
+        def four_at_a_time(grouped, raw):
+            return grouped.rearrange("p (c i) j -> p c j i", i=4), raw.rearrange("p j (c i) -> p c j i", i=4)
+
+        def quantize(name, grouped, width, slot):
+            codes = keep.tile([P, width], U32, name=f"{name}_codes", tag=slot, align_bytes=64)
+            scales = keep.tile([P, width], U8, name=f"{name}_scales", align_bytes=64)
+            nc.vector.quantize_mx(out=codes[:].bitcast(FP8X4), scales=scales[:], in_=grouped.rearrange("p c j -> p (c j)"))
+            return codes, scales
+
+        w2_first = keep.tile([P, P, PACK], BF16, name="w2_first", tag="w2_first_slot", align_bytes=64)
+        nc.vector.tensor_copy(*four_at_a_time(w2_first[:], w2_early[:]))
+        codes, scales = quantize("w2_first", w2_first[:], P, "w2_first_codes")
+        w2_blocks = [(codes[:], scales[:])]
+
+        picked = keep.tile([P, 2, V], F32, name="picked", tag="w2_first_slot", align_bytes=64)
         act = keep.tile([P, 2, V], F32, name="act")
         routed = [keep.tile([P, V], F32, name=f"routed{t}") for t in range(2)]
         for t in (2, 3):
@@ -134,24 +150,17 @@ def tile_picked_headmod_gelu_p_kernel(tc, x_words, x_scales, w1, wt, w2, offs, t
         for t in range(2):
             nc.gpsimd.memset(placed[t][:], 0.0)
 
-        def four_at_a_time(grouped, raw):
-            return grouped.rearrange("p (c i) j -> p c j i", i=4), raw.rearrange("p j (c i) -> p c j i", i=4)
-
-        w2_grouped = [
-            keep.tile([P, P, PACK], BF16, name="w2_grouped0", align_bytes=64),
-            order.tile([P, N - P, PACK], BF16, name="w2_grouped1", offset=0, align_bytes=64),
-        ]
-        nc.scalar.copy(*four_at_a_time(w2_grouped[0][:], w2_early[:]))
+        w2_late = order.tile([P, N - P, PACK], BF16, name="w2_late", offset=0, align_bytes=64)
         for b in range(3):
             cols = slice(b * P, (b + 1) * P)
-            nc.scalar.copy(*four_at_a_time(w2_grouped[1][:, cols, :], w2_raw[:, :, cols]))
+            nc.scalar.copy(*four_at_a_time(w2_late[:, cols, :], w2_raw[:, :, cols]))
 
         bounds = [0, QUARTER, HALF, S]
         pieces = [slice(a, b) for a, b in zip(bounds, bounds[1:])]
         z_all = order.tile([P, S, PACK], BF16, name="z_all", offset=4096, align_bytes=64)
         z = [z_all[:, c, :] for c in pieces]
 
-        for t in range(2):
+        for t in (1, 0):
             nc.vector.tensor_copy(placed[t][:].indirect(take_t[:]), routed[t][:])
         weighted = order.tile([P, 2, V], F32, name="weighted", offset=3072, align_bytes=64)
         summed = keep.tile([P, 2, V], F32, name="summed", tag="summed_slot", align_bytes=64)
@@ -165,38 +174,31 @@ def tile_picked_headmod_gelu_p_kernel(tc, x_words, x_scales, w1, wt, w2, offs, t
         for piece, cols in zip(z, pieces):
             nc.scalar.copy(out=piece[:, :, 3], in_=rows[3][:, cols])
 
-        w2_codes = keep.tile([P, N], U32, name="w2_codes", tag="summed_slot", align_bytes=64)
-        w2_scales = keep.tile([P, N], U8, name="w2_scales", align_bytes=64)
-        w2_parts = (w2_grouped[0][:], w2_grouped[1][:, 0:P, :], w2_grouped[1][:, P:, :])
-        for grouped, cols in zip(w2_parts, (slice(0, P), slice(P, 2 * P), slice(2 * P, N))):
+        w2_codes = keep.tile([P, N - P], U32, name="w2_codes", tag="summed_slot", align_bytes=64)
+        w2_scales = keep.tile([P, N - P], U8, name="w2_scales", align_bytes=64)
+        for cols in (slice(0, P), slice(P, N - P)):
             nc.vector.quantize_mx(
-                out=w2_codes[:, cols].bitcast(FP8X4), scales=w2_scales[:, cols], in_=grouped.rearrange("p c j -> p (c j)")
+                out=w2_codes[:, cols].bitcast(FP8X4),
+                scales=w2_scales[:, cols],
+                in_=w2_late[:, cols, :].rearrange("p c j -> p (c j)"),
             )
-
-        def quantize_z(piece, cols):
-            width = cols.stop - cols.start
-            slot = "z_codes_second" if cols.start == QUARTER else "z_codes_first_and_last"
-            codes = keep.tile([P, width], U32, name=f"z_codes{cols.start}", tag=slot, align_bytes=64)
-            scales = keep.tile([P, width], U8, name=f"z_scales{cols.start}", align_bytes=64)
-            nc.vector.quantize_mx(
-                out=codes[:].bitcast(FP8X4), scales=scales[:], in_=piece.rearrange("p c j -> p (c j)")
-            )
-            return codes, scales
+        w2_blocks.extend((w2_codes[:, b * P : (b + 1) * P], w2_scales[:, b * P : (b + 1) * P]) for b in range(3))
 
         out_view = out.rearrange("(b p) s -> p b s", p=P)
         bank = 0
         for piece, cols in zip(z, pieces):
-            codes, scales = quantize_z(piece, cols)
             width = cols.stop - cols.start
+            slot = "z_codes_second" if cols.start == QUARTER else "z_codes_first_and_last"
+            codes, scales = quantize(f"z{cols.start}", piece, width, slot)
             blocks = HALF // width
             for b0 in range(0, N // P, blocks):
                 acc = psum.tile([P, blocks, width], F32, name=f"out_acc{bank}", tag=f"bank{(6 + bank) % 8}")
                 for i in range(blocks):
-                    stat = slice((b0 + i) * P, (b0 + i + 1) * P)
+                    w2_codes, w2_scales = w2_blocks[b0 + i]
                     nc.tensor.matmul_mx(
                         out=acc[:, i, :],
-                        lhsT=w2_codes[:, stat].bitcast(FP8X4),
-                        lhsT_scale=w2_scales[:, stat],
+                        lhsT=w2_codes.bitcast(FP8X4),
+                        lhsT_scale=w2_scales,
                         rhs=codes[:].bitcast(FP8X4),
                         rhs_scale=scales[:],
                         start=True,

@@ -31,18 +31,18 @@ def tile_picked_headmod_gelu_p_kernel(tc, x_words, x_scales, w1, wt, w2, offs, t
 
         offs_t = keep.tile([P, S // 16], U16, name="offs_t")
         take_t = keep.tile([P, V // 16], U16, name="take_t")
-        xs_win = keep.tile([P, T], U8, name="xs_win", tag="scale_slot", align_bytes=64)
+        xs_win = keep.tile([P, T], U8, name="xs_win", align_bytes=64)
         xw_win = keep.tile([P, T], I32, name="xw_win", align_bytes=64)
-        w1_raw = keep.tile([P, PACK, H], F32, name="w1_raw")
+        w1_raw = [keep.tile([P, 2, H], F32, name=f"w1_raw{u}") for u in range(2)]
         wt_t = keep.tile([P, V], F32, name="wt_t")
 
         nc.vector.memset(xs_win[:].bitcast(I32), 0)
         w1_rows = w1.rearrange("(p j) c -> p j c", j=PACK)
-        nc.sync.dma_start(out=w1_raw[:, 0:2, :], in_=w1_rows[:, 0:2, :])
+        nc.sync.dma_start(out=w1_raw[0][:], in_=w1_rows[:, 0:2, :])
         nc.sync.dma_start(out=xs_win[4:P:8, :].bitcast(I32), in_=x_scales[0].bitcast(I32))
         nc.sync.dma_start(offs_t[:], offs)
-        nc.sync.dma_start(out=w1_raw[:, 2:4, :], in_=w1_rows[:, 2:4, :])
         nc.sync.dma_start(out=xw_win[:], in_=x_words[0].rearrange("p c r -> p (c r)").bitcast(I32))
+        nc.sync.dma_start(out=w1_raw[1][:], in_=w1_rows[:, 2:4, :])
         xs_spread = keep.tile([P, S], U8, name="xs_spread", align_bytes=64)
         nc.vector.tensor_copy(xs_spread[:], xs_win[:].indirect(offs_t[:]))
         xs = keep.tile([P, S], U8, name="xs", align_bytes=64)
@@ -65,38 +65,38 @@ def tile_picked_headmod_gelu_p_kernel(tc, x_words, x_scales, w1, wt, w2, offs, t
         nc.scalar.activation(warm_out[:], warm[:], GELU)
 
 
-        w1_view = w1_raw[:].rearrange("p j (m t) -> p m j t", t=PACK)
-        w1_grouped = [
-            keep.tile([P, 2, P, PACK], BF16, name="w1_grouped0", tag="scale_slot", align_bytes=64),
-            keep.tile([P, 2, P, PACK], BF16, name="w1_grouped1", align_bytes=64),
-        ]
-        nc.vector.tensor_copy(out=w1_grouped[0][:].rearrange("p e m j -> p m j e"), in_=w1_view[:, :, :, 0:2])
-        nc.scalar.copy(out=w1_grouped[1][:].rearrange("p e m j -> p m j e"), in_=w1_view[:, :, :, 2:4])
-
-        def quantize_w1(u):
-            codes = keep.tile([P, 2 * P], U32, name=f"w1_codes{u}", align_bytes=64)
-            scales = keep.tile([P, 2 * P], U8, name=f"w1_scales{u}", align_bytes=64)
-            nc.vector.quantize_mx(
-                out=codes[:].bitcast(FP8X4), scales=scales[:], in_=w1_grouped[u][:].rearrange("p e m j -> p (e m j)")
-            )
-            return codes, scales
-
-        w1_mx = [quantize_w1(u) for u in range(2)]
         xw = keep.tile([P, S], U32, name="xw", align_bytes=64)
-        for h in range(2):
-            nc.vector.tensor_copy(
-                xw[:, h * HALF : (h + 1) * HALF],
-                xw_win[:].bitcast(U32).indirect(offs_t[:, h * HALF // 16 : (h + 1) * HALF // 16]),
+        nc.vector.tensor_copy(xw[:], xw_win[:].bitcast(U32).indirect(offs_t[:]))
+
+        w1_parts = [slice(2, 3), slice(0, 1), slice(3, 4), slice(1, 2)]
+        w1_grouped = [
+            keep.tile([P, part.stop - part.start, P, PACK], BF16, name=f"w1_grouped{part.start}", align_bytes=64)
+            for part in w1_parts
+        ]
+        for u in range(2):
+            dealt = w1_raw[u][:].rearrange("p j (m t) -> p m j t", t=PACK)
+            for n, (grouped, part) in enumerate(zip(w1_grouped, w1_parts)):
+                copy = nc.vector.tensor_copy if u == 1 and n < 2 else nc.scalar.copy
+                copy(out=grouped[:, :, :, 2 * u : 2 * u + 2].rearrange("p t m j -> p m j t"), in_=dealt[:, :, :, part])
+        w1_mx = {}
+        for grouped, part in zip(w1_grouped, w1_parts):
+            width = (part.stop - part.start) * P
+            codes = keep.tile([P, width], U32, name=f"w1_codes{part.start}", align_bytes=64)
+            scales = keep.tile([P, width], U8, name=f"w1_scales{part.start}", align_bytes=64)
+            nc.vector.quantize_mx(
+                out=codes[:].bitcast(FP8X4), scales=scales[:], in_=grouped[:].rearrange("p t m j -> p (t m j)")
             )
+            for t in range(part.start, part.stop):
+                cols = slice((t - part.start) * P, (t - part.start + 1) * P)
+                w1_mx[t] = (codes[:, cols], scales[:, cols])
 
         def first_layer(t, cols, bank):
             acc = psum.tile([P, cols.stop - cols.start], F32, name=f"y_acc{bank}", tag=f"bank{bank}")
-            codes, scales = w1_mx[t // 2]
-            stat = slice((t % 2) * P, (t % 2 + 1) * P)
+            codes, scales = w1_mx[t]
             nc.tensor.matmul_mx(
                 out=acc[:],
-                lhsT=codes[:, stat].bitcast(FP8X4),
-                lhsT_scale=scales[:, stat],
+                lhsT=codes.bitcast(FP8X4),
+                lhsT_scale=scales,
                 rhs=xw[:, cols].bitcast(FP8X4),
                 rhs_scale=xs[:, cols],
                 start=True,
@@ -111,12 +111,15 @@ def tile_picked_headmod_gelu_p_kernel(tc, x_words, x_scales, w1, wt, w2, offs, t
             keep.tile([P, S], F32, name="gelu_rows0", tag="plane0_slot"),
             order.tile([P, S], F32, name="gelu_rows1", offset=2048, align_bytes=64),
         ]
-        for h, cols in enumerate(halves):
-            nc.scalar.copy(out=rows[2][:, cols], in_=first_layer(2, cols, 2 * h)[:])
-            nc.scalar.copy(out=rows[3][:, cols], in_=first_layer(3, cols, 2 * h + 1)[:])
-        dense = [first_layer(t, whole, 4 + t) for t in range(2)]
-        for t in range(2):
-            nc.scalar.activation(gelu_rows[t][:], dense[t][:], GELU)
+        dense = {}
+        for n, t in enumerate((2, 0, 3, 1)):
+            for h, cols in enumerate(halves):
+                acc = first_layer(t, cols, 2 * n + h)
+                if t < 2:
+                    dense[t, h] = acc
+                    nc.scalar.activation(gelu_rows[t][:, cols], acc[:], GELU)
+                else:
+                    nc.scalar.copy(out=rows[t][:, cols], in_=acc[:])
 
         def four_at_a_time(grouped, raw):
             return grouped.rearrange("p (c i) j -> p c j i", i=4), raw.rearrange("p j (c i) -> p c j i", i=4)
@@ -135,13 +138,14 @@ def tile_picked_headmod_gelu_p_kernel(tc, x_words, x_scales, w1, wt, w2, offs, t
         picked = keep.tile([P, 2, V], F32, name="picked", tag="w2_first_slot", align_bytes=64)
         act = keep.tile([P, 2, V], F32, name="act")
         routed = [keep.tile([P, V], F32, name=f"routed{t}") for t in range(2)]
-        for t in (2, 3):
-            nc.vector.tensor_copy(picked[:, t - 2, :], rows[t][:].indirect(take_t[:]))
         for t in range(2):
+            nc.vector.tensor_copy(picked[:, t, :], rows[t + 2][:].indirect(take_t[:]))
             nc.vector.tensor_tensor(routed[t][:], gelu_rows[t][:].indirect(take_t[:]), wt_t[:], MULT)
-        nc.scalar.activation(act[:], picked[:], GELU)
         for t in range(2):
-            nc.scalar.copy(out=rows[t][:], in_=dense[t][:])
+            nc.scalar.activation(act[:, t, :], picked[:, t, :], GELU)
+        for t in range(2):
+            for h, cols in enumerate(halves):
+                nc.scalar.copy(out=rows[t][:, cols], in_=dense[t, h][:])
 
         placed = [
             keep.tile([P, S], F32, name="placed0", tag="plane0_slot"),
@@ -160,13 +164,13 @@ def tile_picked_headmod_gelu_p_kernel(tc, x_words, x_scales, w1, wt, w2, offs, t
         z_all = order.tile([P, S, PACK], BF16, name="z_all", offset=4096, align_bytes=64)
         z = [z_all[:, c, :] for c in pieces]
 
-        for t in (1, 0):
+        for t in range(2):
             nc.vector.tensor_copy(placed[t][:].indirect(take_t[:]), routed[t][:])
         weighted = order.tile([P, 2, V], F32, name="weighted", offset=3072, align_bytes=64)
         summed = keep.tile([P, 2, V], F32, name="summed", tag="summed_slot", align_bytes=64)
         nc.gpsimd.tensor_tensor(weighted[:], act[:], wt_t[:].unsqueeze(1).to_broadcast([P, 2, V]), MULT)
         nc.gpsimd.tensor_tensor(summed[:], weighted[:], picked[:], ADD)
-        for t in (1, 0):
+        for t in range(2):
             nc.gpsimd.tensor_tensor(z_all[:, :, t], rows[t][:], placed[t][:], ADD)
         nc.vector.tensor_copy(rows[2][:].indirect(take_t[:]), summed[:, 0, :])
         nc.scalar.copy(out=z_all[:, :, 2], in_=rows[2][:])
@@ -185,18 +189,22 @@ def tile_picked_headmod_gelu_p_kernel(tc, x_words, x_scales, w1, wt, w2, offs, t
         w2_blocks.extend((w2_codes[:, b * P : (b + 1) * P], w2_scales[:, b * P : (b + 1) * P]) for b in range(3))
 
         out_view = out.rearrange("(b p) s -> p b s", p=P)
-        bank = 0
-        for piece, cols in zip(z, pieces):
-            width = cols.stop - cols.start
-            slot = "z_codes_second" if cols.start == QUARTER else "z_codes_first_and_last"
-            codes, scales = quantize(f"z{cols.start}", piece, width, slot)
-            blocks = HALF // width
-            for b0 in range(0, N // P, blocks):
-                acc = psum.tile([P, blocks, width], F32, name=f"out_acc{bank}", tag=f"bank{(6 + bank) % 8}")
-                for i in range(blocks):
-                    w2_codes, w2_scales = w2_blocks[b0 + i]
+        z_mx = {}
+        groups = [((0,), 0, 1, True), ((0,), 1, 1, True), ((0,), 2, 2, False), ((1,), 0, 2, False), ((1,), 2, 2, True)]
+        groups.extend(((2,), b, 1, b % 2 == 1) for b in range(4))
+        for bank, (parts, b0, blocks, on_vector) in enumerate(groups):
+            first, last = pieces[parts[0]].start, pieces[parts[-1]].stop
+            acc = psum.tile([P, blocks, last - first], F32, name=f"out_acc{bank}", tag=f"bank{(6 + bank) % 8}")
+            for i in range(blocks):
+                w2_codes, w2_scales = w2_blocks[b0 + i]
+                for n in parts:
+                    cols = pieces[n]
+                    if n not in z_mx:
+                        slot = "z_codes_second" if n == 1 else "z_codes_first_and_last"
+                        z_mx[n] = quantize(f"z{n}", z[n], cols.stop - cols.start, slot)
+                    codes, scales = z_mx[n]
                     nc.tensor.matmul_mx(
-                        out=acc[:, i, :],
+                        out=acc[:, i, cols.start - first : cols.stop - first],
                         lhsT=w2_codes.bitcast(FP8X4),
                         lhsT_scale=w2_scales,
                         rhs=codes[:].bitcast(FP8X4),
@@ -204,10 +212,9 @@ def tile_picked_headmod_gelu_p_kernel(tc, x_words, x_scales, w1, wt, w2, offs, t
                         start=True,
                         stop=True,
                     )
-                res = keep.tile([P, blocks, width], F32, name=f"res{bank}")
-                if bank in (0, 3, 5, 7):
-                    nc.vector.tensor_copy(out=res[:], in_=acc[:])
-                else:
-                    nc.scalar.copy(out=res[:], in_=acc[:])
-                nc.sync.dma_start(out=out_view[:, b0 : b0 + blocks, cols], in_=res[:])
-                bank = bank + 1
+            res = keep.tile([P, blocks, last - first], F32, name=f"res{bank}")
+            if on_vector:
+                nc.vector.tensor_copy(out=res[:], in_=acc[:])
+            else:
+                nc.scalar.copy(out=res[:], in_=acc[:])
+            nc.sync.dma_start(out=out_view[:, b0 : b0 + blocks, first:last], in_=res[:])

@@ -159,7 +159,7 @@ def tile_picked_headmod_gelu_p_kernel(tc, x_words, x_scales, w1, wt, w2, offs, t
             cols = slice(b * P, (b + 1) * P)
             nc.scalar.copy(*four_at_a_time(w2_late[:, cols, :], w2_raw[:, :, cols]))
 
-        bounds = [0, QUARTER, HALF, S]
+        bounds = list(range(0, S + 1, QUARTER))
         pieces = [slice(a, b) for a, b in zip(bounds, bounds[1:])]
         z_all = order.tile([P, S, PACK], BF16, name="z_all", offset=4096, align_bytes=64)
         z = [z_all[:, c, :] for c in pieces]
@@ -188,10 +188,21 @@ def tile_picked_headmod_gelu_p_kernel(tc, x_words, x_scales, w1, wt, w2, offs, t
             )
         w2_blocks.extend((w2_codes[:, b * P : (b + 1) * P], w2_scales[:, b * P : (b + 1) * P]) for b in range(3))
 
+        warm_acc = psum.tile([P, S], F32, name="warm_acc", tag="bank5")
+        nc.tensor.matmul_mx(
+            out=warm_acc[:],
+            lhsT=w2_blocks[1][0].bitcast(FP8X4),
+            lhsT_scale=w2_blocks[1][1],
+            rhs=xw[:].bitcast(FP8X4),
+            rhs_scale=xs[:],
+            start=True,
+            stop=True,
+        )
+
         out_view = out.rearrange("(b p) s -> p b s", p=P)
         z_mx = {}
-        groups = [((0,), 0, 1, True), ((0,), 1, 1, True), ((0,), 2, 2, False), ((1,), 0, 2, False), ((1,), 2, 2, True)]
-        groups.extend(((2,), b, 1, b % 2 == 1) for b in range(4))
+        groups = [((0,), 0, 1, True), ((0,), 1, 1, False), ((0,), 2, 2, False), ((1,), 0, 2, True), ((1,), 2, 2, False)]
+        groups.extend(((2, 3), b, 1, b % 2 == 0) for b in range(4))
         for bank, (parts, b0, blocks, on_vector) in enumerate(groups):
             first, last = pieces[parts[0]].start, pieces[parts[-1]].stop
             acc = psum.tile([P, blocks, last - first], F32, name=f"out_acc{bank}", tag=f"bank{(6 + bank) % 8}")
@@ -200,7 +211,7 @@ def tile_picked_headmod_gelu_p_kernel(tc, x_words, x_scales, w1, wt, w2, offs, t
                 for n in parts:
                     cols = pieces[n]
                     if n not in z_mx:
-                        slot = "z_codes_second" if n == 1 else "z_codes_first_and_last"
+                        slot = f"z_codes_slot{n % 3}"
                         z_mx[n] = quantize(f"z{n}", z[n], cols.stop - cols.start, slot)
                     codes, scales = z_mx[n]
                     nc.tensor.matmul_mx(

@@ -31,18 +31,18 @@ def tile_picked_headmod_gelu_p_kernel(tc, x_words, x_scales, w1, wt, w2, offs, t
 
         offs_t = keep.tile([P, S // 16], U16, name="offs_t")
         take_t = keep.tile([P, V // 16], U16, name="take_t")
-        xs_win = keep.tile([P, T], U8, name="xs_win", align_bytes=64)
+        xs_win = keep.tile([P, T], U8, name="xs_win", tag="scale_slot", align_bytes=64)
         xw_win = keep.tile([P, T], I32, name="xw_win", align_bytes=64)
-        w1_raw = [keep.tile([P, 2, H], F32, name=f"w1_raw{u}") for u in range(2)]
+        w1_raw = keep.tile([P, PACK, H], F32, name="w1_raw")
         wt_t = keep.tile([P, V], F32, name="wt_t")
 
         nc.vector.memset(xs_win[:].bitcast(I32), 0)
         w1_rows = w1.rearrange("(p j) c -> p j c", j=PACK)
-        nc.sync.dma_start(out=w1_raw[0][:], in_=w1_rows[:, 0:2, :])
+        nc.sync.dma_start(out=w1_raw[:, 0:2, :], in_=w1_rows[:, 0:2, :])
         nc.sync.dma_start(out=xs_win[4:P:8, :].bitcast(I32), in_=x_scales[0].bitcast(I32))
         nc.sync.dma_start(offs_t[:], offs)
+        nc.sync.dma_start(out=w1_raw[:, 2:4, :], in_=w1_rows[:, 2:4, :])
         nc.sync.dma_start(out=xw_win[:], in_=x_words[0].rearrange("p c r -> p (c r)").bitcast(I32))
-        nc.sync.dma_start(out=w1_raw[1][:], in_=w1_rows[:, 2:4, :])
         xs_spread = keep.tile([P, S], U8, name="xs_spread", align_bytes=64)
         nc.vector.tensor_copy(xs_spread[:], xs_win[:].indirect(offs_t[:]))
         xs = keep.tile([P, S], U8, name="xs", align_bytes=64)
@@ -65,38 +65,38 @@ def tile_picked_headmod_gelu_p_kernel(tc, x_words, x_scales, w1, wt, w2, offs, t
         nc.scalar.activation(warm_out[:], warm[:], GELU)
 
 
-        xw = keep.tile([P, S], U32, name="xw", align_bytes=64)
-        nc.vector.tensor_copy(xw[:], xw_win[:].bitcast(U32).indirect(offs_t[:]))
-
-        w1_parts = [slice(2, 3), slice(0, 1), slice(3, 4), slice(1, 2)]
+        w1_view = w1_raw[:].rearrange("p j (m t) -> p m j t", t=PACK)
         w1_grouped = [
-            keep.tile([P, part.stop - part.start, P, PACK], BF16, name=f"w1_grouped{part.start}", align_bytes=64)
-            for part in w1_parts
+            keep.tile([P, 2, P, PACK], BF16, name="w1_grouped0", tag="scale_slot", align_bytes=64),
+            keep.tile([P, 2, P, PACK], BF16, name="w1_grouped1", align_bytes=64),
         ]
-        for u in range(2):
-            dealt = w1_raw[u][:].rearrange("p j (m t) -> p m j t", t=PACK)
-            for n, (grouped, part) in enumerate(zip(w1_grouped, w1_parts)):
-                copy = nc.vector.tensor_copy if u == 1 and n < 2 else nc.scalar.copy
-                copy(out=grouped[:, :, :, 2 * u : 2 * u + 2].rearrange("p t m j -> p m j t"), in_=dealt[:, :, :, part])
-        w1_mx = {}
-        for grouped, part in zip(w1_grouped, w1_parts):
-            width = (part.stop - part.start) * P
-            codes = keep.tile([P, width], U32, name=f"w1_codes{part.start}", align_bytes=64)
-            scales = keep.tile([P, width], U8, name=f"w1_scales{part.start}", align_bytes=64)
+        nc.vector.tensor_copy(out=w1_grouped[0][:].rearrange("p e m j -> p m j e"), in_=w1_view[:, :, :, 0:2])
+        nc.scalar.copy(out=w1_grouped[1][:].rearrange("p e m j -> p m j e"), in_=w1_view[:, :, :, 2:4])
+
+        def quantize_w1(u):
+            codes = keep.tile([P, 2 * P], U32, name=f"w1_codes{u}", align_bytes=64)
+            scales = keep.tile([P, 2 * P], U8, name=f"w1_scales{u}", align_bytes=64)
             nc.vector.quantize_mx(
-                out=codes[:].bitcast(FP8X4), scales=scales[:], in_=grouped[:].rearrange("p t m j -> p (t m j)")
+                out=codes[:].bitcast(FP8X4), scales=scales[:], in_=w1_grouped[u][:].rearrange("p e m j -> p (e m j)")
             )
-            for t in range(part.start, part.stop):
-                cols = slice((t - part.start) * P, (t - part.start + 1) * P)
-                w1_mx[t] = (codes[:, cols], scales[:, cols])
+            return codes, scales
+
+        w1_mx = [quantize_w1(u) for u in range(2)]
+        xw = keep.tile([P, S], U32, name="xw", align_bytes=64)
+        for h in range(2):
+            nc.vector.tensor_copy(
+                xw[:, h * HALF : (h + 1) * HALF],
+                xw_win[:].bitcast(U32).indirect(offs_t[:, h * HALF // 16 : (h + 1) * HALF // 16]),
+            )
 
         def first_layer(t, cols, bank):
             acc = psum.tile([P, cols.stop - cols.start], F32, name=f"y_acc{bank}", tag=f"bank{bank}")
-            codes, scales = w1_mx[t]
+            codes, scales = w1_mx[t // 2]
+            stat = slice((t % 2) * P, (t % 2 + 1) * P)
             nc.tensor.matmul_mx(
                 out=acc[:],
-                lhsT=codes.bitcast(FP8X4),
-                lhsT_scale=scales,
+                lhsT=codes[:, stat].bitcast(FP8X4),
+                lhsT_scale=scales[:, stat],
                 rhs=xw[:, cols].bitcast(FP8X4),
                 rhs_scale=xs[:, cols],
                 start=True,
@@ -112,14 +112,14 @@ def tile_picked_headmod_gelu_p_kernel(tc, x_words, x_scales, w1, wt, w2, offs, t
             order.tile([P, S], F32, name="gelu_rows1", offset=2048, align_bytes=64),
         ]
         dense = {}
-        for n, t in enumerate((2, 0, 3, 1)):
-            for h, cols in enumerate(halves):
-                acc = first_layer(t, cols, 2 * n + h)
-                if t < 2:
-                    dense[t, h] = acc
-                    nc.scalar.activation(gelu_rows[t][:, cols], acc[:], GELU)
-                else:
-                    nc.scalar.copy(out=rows[t][:, cols], in_=acc[:])
+        for bank, (t, h) in enumerate([(2, 0), (0, 0), (2, 1), (0, 1), (3, 0), (3, 1), (1, 0), (1, 1)]):
+            cols = halves[h]
+            acc = first_layer(t, cols, bank)
+            if t < 2:
+                dense[t, h] = acc
+                nc.scalar.activation(gelu_rows[t][:, cols], acc[:], GELU)
+            else:
+                nc.scalar.copy(out=rows[t][:, cols], in_=acc[:])
 
         def four_at_a_time(grouped, raw):
             return grouped.rearrange("p (c i) j -> p c j i", i=4), raw.rearrange("p j (c i) -> p c j i", i=4)
@@ -187,17 +187,6 @@ def tile_picked_headmod_gelu_p_kernel(tc, x_words, x_scales, w1, wt, w2, offs, t
                 in_=w2_late[:, cols, :].rearrange("p c j -> p (c j)"),
             )
         w2_blocks.extend((w2_codes[:, b * P : (b + 1) * P], w2_scales[:, b * P : (b + 1) * P]) for b in range(3))
-
-        warm_acc = psum.tile([P, S], F32, name="warm_acc", tag="bank5")
-        nc.tensor.matmul_mx(
-            out=warm_acc[:],
-            lhsT=w2_blocks[1][0].bitcast(FP8X4),
-            lhsT_scale=w2_blocks[1][1],
-            rhs=xw[:].bitcast(FP8X4),
-            rhs_scale=xs[:],
-            start=True,
-            stop=True,
-        )
 
         out_view = out.rearrange("(b p) s -> p b s", p=P)
         z_mx = {}

@@ -111,12 +111,12 @@ def tile_picked_headmod_gelu_p_kernel(tc, x_words, x_scales, w1, wt, w2, offs, t
             keep.tile([P, S], F32, name="gelu_rows0", tag="plane0_slot"),
             order.tile([P, S], F32, name="gelu_rows1", offset=2048, align_bytes=64),
         ]
-        dense = {}
-        for bank, (t, h) in enumerate([(2, 0), (0, 0), (2, 1), (0, 1), (3, 0), (3, 1), (1, 0), (1, 1)]):
-            cols = halves[h]
+        dense = []
+        passes = [(t, cols) for cols in halves for t in (2, 0)] + [(3, whole), (1, whole)]
+        for bank, (t, cols) in enumerate(passes):
             acc = first_layer(t, cols, bank)
             if t < 2:
-                dense[t, h] = acc
+                dense.append((t, cols, acc))
                 nc.scalar.activation(gelu_rows[t][:, cols], acc[:], GELU)
             else:
                 nc.scalar.copy(out=rows[t][:, cols], in_=acc[:])
@@ -143,13 +143,12 @@ def tile_picked_headmod_gelu_p_kernel(tc, x_words, x_scales, w1, wt, w2, offs, t
             nc.vector.tensor_tensor(routed[t][:], gelu_rows[t][:].indirect(take_t[:]), wt_t[:], MULT)
         for t in range(2):
             nc.scalar.activation(act[:, t, :], picked[:, t, :], GELU)
-        for t in range(2):
-            for h, cols in enumerate(halves):
-                nc.scalar.copy(out=rows[t][:, cols], in_=dense[t, h][:])
+        for t, cols, acc in dense:
+            nc.scalar.copy(out=rows[t][:, cols], in_=acc[:])
 
         placed = [
             keep.tile([P, S], F32, name="placed0", tag="plane0_slot"),
-            keep.tile([P, S], F32, name="placed1"),
+            keep.tile([P, S], F32, name="placed1", tag="plane1_slot", align_bytes=64),
         ]
         for t in range(2):
             nc.gpsimd.memset(placed[t][:], 0.0)
@@ -167,7 +166,7 @@ def tile_picked_headmod_gelu_p_kernel(tc, x_words, x_scales, w1, wt, w2, offs, t
         for t in range(2):
             nc.vector.tensor_copy(placed[t][:].indirect(take_t[:]), routed[t][:])
         weighted = order.tile([P, 2, V], F32, name="weighted", offset=3072, align_bytes=64)
-        summed = keep.tile([P, 2, V], F32, name="summed", tag="summed_slot", align_bytes=64)
+        summed = keep.tile([P, 2, V], F32, name="summed")
         nc.gpsimd.tensor_tensor(weighted[:], act[:], wt_t[:].unsqueeze(1).to_broadcast([P, 2, V]), MULT)
         nc.gpsimd.tensor_tensor(summed[:], weighted[:], picked[:], ADD)
         for t in range(2):
@@ -178,7 +177,8 @@ def tile_picked_headmod_gelu_p_kernel(tc, x_words, x_scales, w1, wt, w2, offs, t
         for piece, cols in zip(z, pieces):
             nc.scalar.copy(out=piece[:, :, 3], in_=rows[3][:, cols])
 
-        w2_codes = keep.tile([P, N - P], U32, name="w2_codes", tag="summed_slot", align_bytes=64)
+        z_mx = {0: quantize("z0", z[0], QUARTER, "z_codes_slot0")}
+        w2_codes = keep.tile([P, N - P], U32, name="w2_codes", tag="plane1_slot", align_bytes=64)
         w2_scales = keep.tile([P, N - P], U8, name="w2_scales", align_bytes=64)
         for cols in (slice(0, P), slice(P, N - P)):
             nc.vector.quantize_mx(
@@ -189,7 +189,6 @@ def tile_picked_headmod_gelu_p_kernel(tc, x_words, x_scales, w1, wt, w2, offs, t
         w2_blocks.extend((w2_codes[:, b * P : (b + 1) * P], w2_scales[:, b * P : (b + 1) * P]) for b in range(3))
 
         out_view = out.rearrange("(b p) s -> p b s", p=P)
-        z_mx = {}
         groups = [((0,), 0, 1, True), ((0,), 1, 1, False), ((0,), 2, 2, False), ((1,), 0, 2, True), ((1,), 2, 2, False)]
         groups.extend(((2, 3), b, 1, b % 2 == 0) for b in range(4))
         for bank, (parts, b0, blocks, on_vector) in enumerate(groups):

@@ -31,10 +31,10 @@ def tile_picked_headmod_gelu_p_kernel(tc, x_words, x_scales, w1, wt, w2, offs, t
 
         offs_t = keep.tile([P, S // 16], U16, name="offs_t")
         take_t = keep.tile([P, V // 16], U16, name="take_t")
-        xs_win = keep.tile([P, T], U8, name="xs_win", tag="scale_slot", align_bytes=64)
+        head = ctx.enter_context(tc.tile_pool(name="head", bufs=1))
+        xs_win = head.tile([P, T], U8, name="xs_win", offset=2048, align_bytes=64)
         xw_win = keep.tile([P, T], I32, name="xw_win", align_bytes=64)
         w1_raw = keep.tile([P, PACK, H], F32, name="w1_raw")
-        wt_t = keep.tile([P, V], F32, name="wt_t")
 
         nc.vector.memset(xs_win[:].bitcast(I32), 0)
         w1_rows = w1.rearrange("(p j) c -> p j c", j=PACK)
@@ -43,7 +43,7 @@ def tile_picked_headmod_gelu_p_kernel(tc, x_words, x_scales, w1, wt, w2, offs, t
         nc.sync.dma_start(offs_t[:], offs)
         nc.sync.dma_start(out=w1_raw[:, 2:4, :], in_=w1_rows[:, 2:4, :])
         nc.sync.dma_start(out=xw_win[:], in_=x_words[0].rearrange("p c r -> p (c r)").bitcast(I32))
-        xs_spread = keep.tile([P, S], U8, name="xs_spread", align_bytes=64)
+        xs_spread = head.tile([P, S], U8, name="xs_spread", offset=16384, align_bytes=64)
         nc.vector.tensor_copy(xs_spread[:], xs_win[:].indirect(offs_t[:]))
         xs = keep.tile([P, S], U8, name="xs", align_bytes=64)
         nc.vector.memset(xs[:].bitcast(I32), 0)
@@ -52,12 +52,11 @@ def tile_picked_headmod_gelu_p_kernel(tc, x_words, x_scales, w1, wt, w2, offs, t
                 out=xs[32 * q : 32 * q + 4, :].bitcast(I32), in_=xs_spread[32 * q + 4 : 32 * q + 32 : 8, :].bitcast(I32)
             )
         w2_view = w2.rearrange("(p j) c -> p j c", j=PACK)
-        w2_early = keep.tile([P, PACK, P], F32, name="w2_early")
-        nc.sync.dma_start(out=w2_early[:], in_=w2_view[:, :, 0:P])
         nc.sync.dma_start(take_t[:], take)
+        w2_early = head.tile([P, PACK, P], F32, name="w2_early", offset=64, align_bytes=64)
+        nc.sync.dma_start(out=w2_early[:], in_=w2_view[:, :, 0:P])
+        wt_t = head.tile([P, V], F32, name="wt_t", offset=2560, align_bytes=64)
         nc.sync.dma_start(out=wt_t[:], in_=wt.rearrange("(p f) v -> p f v", f=PACK)[:, 0, :])
-        w2_raw = keep.tile([P, PACK, N - P], F32, name="w2_raw")
-        nc.sync.dma_start(out=w2_raw[:], in_=w2_view[:, :, P:N])
 
         warm = keep.tile([P, 8], F32, name="warm")
         warm_out = keep.tile([P, 8], F32, name="warm_out")
@@ -67,7 +66,7 @@ def tile_picked_headmod_gelu_p_kernel(tc, x_words, x_scales, w1, wt, w2, offs, t
 
         w1_view = w1_raw[:].rearrange("p j (m t) -> p m j t", t=PACK)
         w1_grouped = [
-            keep.tile([P, 2, P, PACK], BF16, name="w1_grouped0", tag="scale_slot", align_bytes=64),
+            head.tile([P, 2, P, PACK], BF16, name="w1_grouped0", offset=4096 - 64, align_bytes=64),
             keep.tile([P, 2, P, PACK], BF16, name="w1_grouped1", align_bytes=64),
         ]
         nc.vector.tensor_copy(out=w1_grouped[0][:].rearrange("p e m j -> p m j e"), in_=w1_view[:, :, :, 0:2])
@@ -82,7 +81,9 @@ def tile_picked_headmod_gelu_p_kernel(tc, x_words, x_scales, w1, wt, w2, offs, t
             return codes, scales
 
         w1_mx = [quantize_w1(u) for u in range(2)]
-        xw = keep.tile([P, S], U32, name="xw", align_bytes=64)
+        w2_raw = head.tile([P, PACK, N - P], F32, name="w2_raw", offset=6016, align_bytes=64)
+        nc.sync.dma_start(out=w2_raw[:], in_=w2_view[:, :, P:N])
+        xw = order.tile([P, S], U32, name="xw", offset=12288, align_bytes=64)
         for h in range(2):
             nc.vector.tensor_copy(
                 xw[:, h * HALF : (h + 1) * HALF],
@@ -108,11 +109,12 @@ def tile_picked_headmod_gelu_p_kernel(tc, x_words, x_scales, w1, wt, w2, offs, t
         whole = slice(0, S)
         rows = [keep.tile([P, S], F32, name=f"rows{t}") for t in range(PACK)]
         gelu_rows = [
-            keep.tile([P, S], F32, name="gelu_rows0", tag="plane0_slot"),
+            keep.tile([P, S], F32, name="gelu_rows0"),
             order.tile([P, S], F32, name="gelu_rows1", offset=2048, align_bytes=64),
         ]
         dense = []
-        passes = [(t, cols) for cols in halves for t in (2, 0)] + [(3, whole), (1, whole)]
+        passes = [(2, halves[0]), (3, halves[0]), (2, slice(HALF, HALF + QUARTER)), (2, slice(HALF + QUARTER, S))]
+        passes += [(3, halves[1]), (0, whole), (1, whole)]
         for bank, (t, cols) in enumerate(passes):
             acc = first_layer(t, cols, bank)
             if t < 2:
@@ -140,6 +142,7 @@ def tile_picked_headmod_gelu_p_kernel(tc, x_words, x_scales, w1, wt, w2, offs, t
         routed = [keep.tile([P, V], F32, name=f"routed{t}") for t in range(2)]
         for t in range(2):
             nc.vector.tensor_copy(picked[:, t, :], rows[t + 2][:].indirect(take_t[:]))
+        for t in range(2):
             nc.vector.tensor_tensor(routed[t][:], gelu_rows[t][:].indirect(take_t[:]), wt_t[:], MULT)
         for t in range(2):
             nc.scalar.activation(act[:, t, :], picked[:, t, :], GELU)
@@ -147,10 +150,10 @@ def tile_picked_headmod_gelu_p_kernel(tc, x_words, x_scales, w1, wt, w2, offs, t
             nc.scalar.copy(out=rows[t][:, cols], in_=acc[:])
 
         placed = [
-            keep.tile([P, S], F32, name="placed0", tag="plane0_slot"),
-            keep.tile([P, S], F32, name="placed1", tag="plane1_slot", align_bytes=64),
+            order.tile([P, S], F32, name="placed0", offset=12288 + 2048 - 64, align_bytes=64),
+            order.tile([P, S], F32, name="placed1", offset=12288 - 2048 + 64, align_bytes=64),
         ]
-        for t in range(2):
+        for t in (1, 0):
             nc.gpsimd.memset(placed[t][:], 0.0)
 
         w2_late = order.tile([P, N - P, PACK], BF16, name="w2_late", offset=0, align_bytes=64)
@@ -167,8 +170,10 @@ def tile_picked_headmod_gelu_p_kernel(tc, x_words, x_scales, w1, wt, w2, offs, t
             nc.vector.tensor_copy(placed[t][:].indirect(take_t[:]), routed[t][:])
         weighted = order.tile([P, 2, V], F32, name="weighted", offset=3072, align_bytes=64)
         summed = keep.tile([P, 2, V], F32, name="summed")
-        nc.gpsimd.tensor_tensor(weighted[:], act[:], wt_t[:].unsqueeze(1).to_broadcast([P, 2, V]), MULT)
-        nc.gpsimd.tensor_tensor(summed[:], weighted[:], picked[:], ADD)
+        for t in range(2):
+            nc.gpsimd.tensor_tensor(weighted[:, t, :], act[:, t, :], wt_t[:], MULT)
+        for t in range(2):
+            nc.gpsimd.tensor_tensor(summed[:, t, :], weighted[:, t, :], picked[:, t, :], ADD)
         for t in range(2):
             nc.gpsimd.tensor_tensor(z_all[:, :, t], rows[t][:], placed[t][:], ADD)
         nc.vector.tensor_copy(rows[2][:].indirect(take_t[:]), summed[:, 0, :])
@@ -178,7 +183,7 @@ def tile_picked_headmod_gelu_p_kernel(tc, x_words, x_scales, w1, wt, w2, offs, t
             nc.scalar.copy(out=piece[:, :, 3], in_=rows[3][:, cols])
 
         z_mx = {0: quantize("z0", z[0], QUARTER, "z_codes_slot0")}
-        w2_codes = keep.tile([P, N - P], U32, name="w2_codes", tag="plane1_slot", align_bytes=64)
+        w2_codes = order.tile([P, N - P], U32, name="w2_codes", offset=12288 - 2048 + 64, align_bytes=64)
         w2_scales = keep.tile([P, N - P], U8, name="w2_scales", align_bytes=64)
         for cols in (slice(0, P), slice(P, N - P)):
             nc.vector.quantize_mx(
@@ -193,7 +198,7 @@ def tile_picked_headmod_gelu_p_kernel(tc, x_words, x_scales, w1, wt, w2, offs, t
         groups.extend(((2, 3), b, 1, b % 2 == 0) for b in range(4))
         for bank, (parts, b0, blocks, on_vector) in enumerate(groups):
             first, last = pieces[parts[0]].start, pieces[parts[-1]].stop
-            acc = psum.tile([P, blocks, last - first], F32, name=f"out_acc{bank}", tag=f"bank{(6 + bank) % 8}")
+            acc = psum.tile([P, blocks, last - first], F32, name=f"out_acc{bank}", tag=f"bank{(7 + bank) % 8}")
             for i in range(blocks):
                 w2_codes, w2_scales = w2_blocks[b0 + i]
                 for n in parts:

@@ -161,64 +161,102 @@ def tile_picked_headmod_gelu_p_kernel(tc, x_words, x_scales, w1, wt, w2, offs, t
             cols = slice(b * P, (b + 1) * P)
             nc.scalar.copy(*four_at_a_time(w2_late[:, cols, :], w2_raw[:, :, cols]))
 
-        bounds = list(range(0, S + 1, QUARTER))
+        bounds = [0, QUARTER // 2] + list(range(QUARTER, S + 1, QUARTER))
         pieces = [slice(a, b) for a, b in zip(bounds, bounds[1:])]
         z_all = order.tile([P, S, PACK], BF16, name="z_all", offset=4096, align_bytes=64)
-        z = [z_all[:, c, :] for c in pieces]
 
         for t in range(2):
             nc.vector.tensor_copy(placed[t][:].indirect(take_t[:]), routed[t][:])
         weighted = order.tile([P, 2, V], F32, name="weighted", offset=3072, align_bytes=64)
         summed = keep.tile([P, 2, V], F32, name="summed")
-        for t in range(2):
-            nc.gpsimd.tensor_tensor(weighted[:, t, :], act[:, t, :], wt_t[:], MULT)
-        for t in range(2):
-            nc.gpsimd.tensor_tensor(summed[:, t, :], weighted[:, t, :], picked[:, t, :], ADD)
+        nc.gpsimd.tensor_tensor(weighted[:], act[:], wt_t[:].unsqueeze(1).to_broadcast([P, 2, V]), MULT)
+        nc.gpsimd.tensor_tensor(summed[:], weighted[:], picked[:], ADD)
         for t in range(2):
             nc.gpsimd.tensor_tensor(z_all[:, :, t], rows[t][:], placed[t][:], ADD)
         nc.vector.tensor_copy(rows[2][:].indirect(take_t[:]), summed[:, 0, :])
         nc.scalar.copy(out=z_all[:, :, 2], in_=rows[2][:])
         nc.vector.tensor_copy(rows[3][:].indirect(take_t[:]), summed[:, 1, :])
-        for piece, cols in zip(z, pieces):
-            nc.scalar.copy(out=piece[:, :, 3], in_=rows[3][:, cols])
+        for cols in pieces:
+            nc.scalar.copy(out=z_all[:, cols, 3], in_=rows[3][:, cols])
 
-        z_mx = {0: quantize("z0", z[0], QUARTER, "z_codes_slot0")}
         w2_codes = order.tile([P, N - P], U32, name="w2_codes", offset=12288 - 2048 + 64, align_bytes=64)
         w2_scales = keep.tile([P, N - P], U8, name="w2_scales", align_bytes=64)
-        for cols in (slice(0, P), slice(P, N - P)):
+
+        def quantize_w2(b):
+            cols = slice(b * P, (b + 1) * P)
             nc.vector.quantize_mx(
                 out=w2_codes[:, cols].bitcast(FP8X4),
                 scales=w2_scales[:, cols],
                 in_=w2_late[:, cols, :].rearrange("p c j -> p (c j)"),
             )
-        w2_blocks.extend((w2_codes[:, b * P : (b + 1) * P], w2_scales[:, b * P : (b + 1) * P]) for b in range(3))
+            w2_blocks.append((w2_codes[:, cols], w2_scales[:, cols]))
+
+        quantize_w2(0)
+        quantize_w2(1)
+
+        z_scales = keep.tile([P, S], U8, name="z_scales", align_bytes=64)
+
+        def quantize_z(name, first, last, slot):
+            codes = keep.tile([P, last - first], U32, name=name, tag=slot, align_bytes=64)
+            for cols in pieces:
+                if first <= cols.start < last:
+                    nc.vector.quantize_mx(
+                        out=codes[:, cols.start - first : cols.stop - first].bitcast(FP8X4),
+                        scales=z_scales[:, cols],
+                        in_=z_all[:, cols, :].rearrange("p c j -> p (c j)"),
+                    )
+            return codes, first
+
+        def second_layer(acc, block, cols, z_mx):
+            codes, first = z_mx
+            w2_codes, w2_scales = w2_blocks[block]
+            nc.tensor.matmul_mx(
+                out=acc,
+                lhsT=w2_codes.bitcast(FP8X4),
+                lhsT_scale=w2_scales,
+                rhs=codes[:, cols.start - first : cols.stop - first].bitcast(FP8X4),
+                rhs_scale=z_scales[:, cols],
+                start=True,
+                stop=True,
+            )
 
         out_view = out.rearrange("(b p) s -> p b s", p=P)
-        groups = [((0,), 0, 1, True), ((0,), 1, 1, False), ((0,), 2, 2, False), ((1,), 0, 2, True), ((1,), 2, 2, False)]
-        groups.extend(((2, 3), b, 1, b % 2 == 0) for b in range(4))
-        for bank, (parts, b0, blocks, on_vector) in enumerate(groups):
-            first, last = pieces[parts[0]].start, pieces[parts[-1]].stop
-            acc = psum.tile([P, blocks, last - first], F32, name=f"out_acc{bank}", tag=f"bank{(7 + bank) % 8}")
-            for i in range(blocks):
-                w2_codes, w2_scales = w2_blocks[b0 + i]
-                for n in parts:
-                    cols = pieces[n]
-                    if n not in z_mx:
-                        slot = f"z_codes_slot{n % 3}"
-                        z_mx[n] = quantize(f"z{n}", z[n], cols.stop - cols.start, slot)
-                    codes, scales = z_mx[n]
-                    nc.tensor.matmul_mx(
-                        out=acc[:, i, cols.start - first : cols.stop - first],
-                        lhsT=w2_codes.bitcast(FP8X4),
-                        lhsT_scale=w2_scales,
-                        rhs=codes[:].bitcast(FP8X4),
-                        rhs_scale=scales[:],
-                        start=True,
-                        stop=True,
-                    )
-            res = keep.tile([P, blocks, last - first], F32, name=f"res{bank}")
+
+        def bank(n, blocks, width):
+            return psum.tile([P, blocks, width], F32, name=f"out_acc{n}", tag=f"bank{(7 + n) % 8}")
+
+        def store(n, acc, b0, blocks, cols, on_vector):
+            res = keep.tile([P, blocks, cols.stop - cols.start], F32, name=f"res{n}")
             if on_vector:
                 nc.vector.tensor_copy(out=res[:], in_=acc[:])
             else:
                 nc.scalar.copy(out=res[:], in_=acc[:])
-            nc.sync.dma_start(out=out_view[:, b0 : b0 + blocks, first:last], in_=res[:])
+            nc.sync.dma_start(out=out_view[:, b0 : b0 + blocks, cols], in_=res[:])
+
+        eighth = QUARTER // 2
+        z0 = quantize_z("z0_codes", 0, QUARTER, "z_slot0")
+        quantize_w2(2)
+        for b in range(2):
+            acc = bank(b, 1, eighth)
+            second_layer(acc[:, 0, :], b, pieces[0], z0)
+            store(b, acc, b, 1, pieces[0], True)
+        acc = bank(2, 2, QUARTER)
+        for b in range(2):
+            second_layer(acc[:, b, :], 2 + b, slice(0, QUARTER), z0)
+        store(2, acc, 2, 2, slice(0, QUARTER), False)
+        acc = bank(3, 2, HALF - eighth)
+        for b in range(2):
+            second_layer(acc[:, b, 0:eighth], b, pieces[1], z0)
+        z1 = quantize_z("z1_codes", QUARTER, HALF, "z_slot1")
+        for b in range(2):
+            second_layer(acc[:, b, eighth:], b, pieces[2], z1)
+        store(3, acc, 0, 2, slice(eighth, HALF), True)
+        acc = bank(4, 2, QUARTER)
+        for b in range(2):
+            second_layer(acc[:, b, :], 2 + b, pieces[2], z1)
+        store(4, acc, 2, 2, pieces[2], False)
+        z2 = quantize_z("z2_codes", HALF, S, "z_slot0")
+        for b in range(4):
+            acc = bank(5 + b, 1, HALF)
+            second_layer(acc[:, 0, :], b, halves[1], z2)
+            store(5 + b, acc, b, 1, halves[1], b % 2 == 0)

@@ -161,7 +161,7 @@ def tile_picked_headmod_gelu_p_kernel(tc, x_words, x_scales, w1, wt, w2, offs, t
             cols = slice(b * P, (b + 1) * P)
             nc.scalar.copy(*four_at_a_time(w2_late[:, cols, :], w2_raw[:, :, cols]))
 
-        bounds = [0, QUARTER // 2] + list(range(QUARTER, S + 1, QUARTER))
+        bounds = list(range(0, S + 1, QUARTER))
         pieces = [slice(a, b) for a, b in zip(bounds, bounds[1:])]
         z_all = order.tile([P, S, PACK], BF16, name="z_all", offset=4096, align_bytes=64)
 
@@ -194,69 +194,62 @@ def tile_picked_headmod_gelu_p_kernel(tc, x_words, x_scales, w1, wt, w2, offs, t
         quantize_w2(0)
         quantize_w2(1)
 
+        z_codes = keep.tile([P, S], U32, name="z_codes", align_bytes=64)
         z_scales = keep.tile([P, S], U8, name="z_scales", align_bytes=64)
 
-        def quantize_z(name, first, last, slot):
-            codes = keep.tile([P, last - first], U32, name=name, tag=slot, align_bytes=64)
-            for cols in pieces:
-                if first <= cols.start < last:
-                    nc.vector.quantize_mx(
-                        out=codes[:, cols.start - first : cols.stop - first].bitcast(FP8X4),
-                        scales=z_scales[:, cols],
-                        in_=z_all[:, cols, :].rearrange("p c j -> p (c j)"),
-                    )
-            return codes, first
-
-        def second_layer(acc, block, cols, z_mx):
-            codes, first = z_mx
-            w2_codes, w2_scales = w2_blocks[block]
-            nc.tensor.matmul_mx(
-                out=acc,
-                lhsT=w2_codes.bitcast(FP8X4),
-                lhsT_scale=w2_scales,
-                rhs=codes[:, cols.start - first : cols.stop - first].bitcast(FP8X4),
-                rhs_scale=z_scales[:, cols],
-                start=True,
-                stop=True,
+        def quantize_z(cols):
+            nc.vector.quantize_mx(
+                out=z_codes[:, cols].bitcast(FP8X4),
+                scales=z_scales[:, cols],
+                in_=z_all[:, cols, :].rearrange("p c j -> p (c j)"),
             )
 
+        results = keep.tile([P, PACK, S], F32, name="results")
         out_view = out.rearrange("(b p) s -> p b s", p=P)
 
-        def bank(n, blocks, width):
-            return psum.tile([P, blocks, width], F32, name=f"out_acc{n}", tag=f"bank{(7 + n) % 8}")
-
-        def store(n, acc, b0, blocks, cols, on_vector):
-            res = keep.tile([P, blocks, cols.stop - cols.start], F32, name=f"res{n}")
+        def product(bank, block, passes, on_vector):
+            first, last = passes[0].start, passes[-1].stop
+            acc = psum.tile([P, last - first], F32, name=f"out_acc{bank}", tag=f"bank{(7 + bank) % 8}")
+            w2_codes, w2_scales = w2_blocks[block]
+            for cols in passes:
+                nc.tensor.matmul_mx(
+                    out=acc[:, cols.start - first : cols.stop - first],
+                    lhsT=w2_codes.bitcast(FP8X4),
+                    lhsT_scale=w2_scales,
+                    rhs=z_codes[:, cols].bitcast(FP8X4),
+                    rhs_scale=z_scales[:, cols],
+                    start=True,
+                    stop=True,
+                )
             if on_vector:
-                nc.vector.tensor_copy(out=res[:], in_=acc[:])
+                nc.vector.tensor_copy(out=results[:, block, first:last], in_=acc[:])
             else:
-                nc.scalar.copy(out=res[:], in_=acc[:])
-            nc.sync.dma_start(out=out_view[:, b0 : b0 + blocks, cols], in_=res[:])
+                nc.scalar.copy(out=results[:, block, first:last], in_=acc[:])
 
-        eighth = QUARTER // 2
-        z0 = quantize_z("z0_codes", 0, QUARTER, "z_slot0")
+        def store(block, cols):
+            nc.sync.dma_start(out=out_view[:, block, cols], in_=results[:, block, cols])
+
+        rest = slice(QUARTER, S)
+        quantize_z(pieces[0])
         quantize_w2(2)
-        for b in range(2):
-            acc = bank(b, 1, eighth)
-            second_layer(acc[:, 0, :], b, pieces[0], z0)
-            store(b, acc, b, 1, pieces[0], True)
-        acc = bank(2, 2, QUARTER)
-        for b in range(2):
-            second_layer(acc[:, b, :], 2 + b, slice(0, QUARTER), z0)
-        store(2, acc, 2, 2, slice(0, QUARTER), False)
-        acc = bank(3, 2, HALF - eighth)
-        for b in range(2):
-            second_layer(acc[:, b, 0:eighth], b, pieces[1], z0)
-        z1 = quantize_z("z1_codes", QUARTER, HALF, "z_slot1")
-        for b in range(2):
-            second_layer(acc[:, b, eighth:], b, pieces[2], z1)
-        store(3, acc, 0, 2, slice(eighth, HALF), True)
-        acc = bank(4, 2, QUARTER)
-        for b in range(2):
-            second_layer(acc[:, b, :], 2 + b, pieces[2], z1)
-        store(4, acc, 2, 2, pieces[2], False)
-        z2 = quantize_z("z2_codes", HALF, S, "z_slot0")
-        for b in range(4):
-            acc = bank(5 + b, 1, HALF)
-            second_layer(acc[:, 0, :], b, halves[1], z2)
-            store(5 + b, acc, b, 1, halves[1], b % 2 == 0)
+        quantize_z(pieces[1])
+        product(0, 0, pieces[0:1], True)
+        store(0, pieces[0])
+        product(1, 1, pieces[0:1], False)
+        store(1, pieces[0])
+        product(2, 2, pieces[0:2], False)
+        store(2, halves[0])
+        quantize_z(pieces[2])
+        quantize_z(pieces[3])
+        product(3, 3, halves[0:1], True)
+        store(3, halves[0])
+        product(4, 0, pieces[1:3], False)
+        product(5, 0, pieces[3:4], True)
+        store(0, rest)
+        product(6, 1, pieces[1:2], False)
+        product(7, 1, halves[1:2], True)
+        store(1, rest)
+        product(8, 2, halves[1:2], False)
+        store(2, halves[1])
+        product(9, 3, halves[1:2], True)
+        store(3, halves[1])

@@ -43,7 +43,7 @@ def tile_picked_headmod_gelu_p_kernel(tc, x_words, x_scales, w1, wt, w2, offs, t
         nc.sync.dma_start(offs_t[:], offs)
         nc.sync.dma_start(out=w1_raw[:, 2:4, :], in_=w1_rows[:, 2:4, :])
         nc.sync.dma_start(out=xw_win[:], in_=x_words[0].rearrange("p c r -> p (c r)").bitcast(I32))
-        xs_spread = head.tile([P, S], U8, name="xs_spread", offset=16384, align_bytes=64)
+        xs_spread = head.tile([P, S], U8, name="xs_spread", offset=20480, align_bytes=64)
         nc.vector.tensor_copy(xs_spread[:], xs_win[:].indirect(offs_t[:]))
         xs = keep.tile([P, S], U8, name="xs", align_bytes=64)
         nc.vector.memset(xs[:].bitcast(I32), 0)
@@ -65,23 +65,16 @@ def tile_picked_headmod_gelu_p_kernel(tc, x_words, x_scales, w1, wt, w2, offs, t
 
 
         w1_view = w1_raw[:].rearrange("p j (m t) -> p m j t", t=PACK)
-        w1_grouped = [
-            head.tile([P, 2, P, PACK], BF16, name="w1_grouped0", offset=4096 - 64, align_bytes=64),
-            keep.tile([P, 2, P, PACK], BF16, name="w1_grouped1", align_bytes=64),
-        ]
-        nc.vector.tensor_copy(out=w1_grouped[0][:].rearrange("p e m j -> p m j e"), in_=w1_view[:, :, :, 0:2])
-        nc.scalar.copy(out=w1_grouped[1][:].rearrange("p e m j -> p m j e"), in_=w1_view[:, :, :, 2:4])
-
-        def quantize_w1(u):
-            codes = keep.tile([P, 2 * P], U32, name=f"w1_codes{u}", align_bytes=64)
-            scales = keep.tile([P, 2 * P], U8, name=f"w1_scales{u}", align_bytes=64)
-            nc.vector.quantize_mx(
-                out=codes[:].bitcast(FP8X4), scales=scales[:], in_=w1_grouped[u][:].rearrange("p e m j -> p (e m j)")
-            )
-            return codes, scales
-
-        w1_mx = [quantize_w1(u) for u in range(2)]
-        w2_raw = head.tile([P, PACK, N - P], F32, name="w2_raw", offset=6016, align_bytes=64)
+        w1_grouped = head.tile([P, PACK, P, PACK], BF16, name="w1_grouped", offset=6144, align_bytes=64)
+        w1_dealt = w1_grouped[:].rearrange("p t m j -> p m j t")
+        nc.vector.tensor_copy(out=w1_dealt[:, 0:80], in_=w1_view[:, 0:80])
+        nc.scalar.copy(out=w1_dealt[:, 80:P], in_=w1_view[:, 80:P])
+        w1_codes = head.tile([P, H], U32, name="w1_codes", offset=4096 - 64, align_bytes=64)
+        w1_scales = keep.tile([P, H], U8, name="w1_scales", align_bytes=64)
+        nc.vector.quantize_mx(
+            out=w1_codes[:].bitcast(FP8X4), scales=w1_scales[:], in_=w1_grouped[:].rearrange("p t m j -> p (t m j)")
+        )
+        w2_raw = head.tile([P, PACK, N - P], F32, name="w2_raw", offset=10176, align_bytes=64)
         nc.sync.dma_start(out=w2_raw[:], in_=w2_view[:, :, P:N])
         xw = order.tile([P, S], U32, name="xw", offset=12288, align_bytes=64)
         for h in range(2):
@@ -92,12 +85,11 @@ def tile_picked_headmod_gelu_p_kernel(tc, x_words, x_scales, w1, wt, w2, offs, t
 
         def first_layer(t, cols, bank):
             acc = psum.tile([P, cols.stop - cols.start], F32, name=f"y_acc{bank}", tag=f"bank{bank}")
-            codes, scales = w1_mx[t // 2]
-            stat = slice((t % 2) * P, (t % 2 + 1) * P)
+            stat = slice(t * P, (t + 1) * P)
             nc.tensor.matmul_mx(
                 out=acc[:],
-                lhsT=codes[:, stat].bitcast(FP8X4),
-                lhsT_scale=scales[:, stat],
+                lhsT=w1_codes[:, stat].bitcast(FP8X4),
+                lhsT_scale=w1_scales[:, stat],
                 rhs=xw[:, cols].bitcast(FP8X4),
                 rhs_scale=xs[:, cols],
                 start=True,

@@ -18,8 +18,29 @@ MULT = mybir.AluOpType.mult
 
 P = 128
 PACK = 4
+GROUP = 16
+BANKS = 8
 HALF = S // 2
 QUARTER = S // 4
+
+VECTOR_GROUPS = 80
+
+ROW = 4 * S
+EDGE = 64
+XS_WIN_AT = ROW
+W2_EARLY_AT = XS_WIN_AT - ROW + EDGE
+WT_AT = XS_WIN_AT + ROW // 4
+W1_CODES_AT = XS_WIN_AT + ROW - EDGE
+W1_GROUPED_AT = 3 * ROW
+W2_RAW_AT = W1_GROUPED_AT + 2 * ROW - EDGE
+XS_SPREAD_AT = 10 * ROW
+W2_LATE_AT = 0
+GELU_LAST_AT = ROW
+WEIGHTED_AT = 3 * ROW // 2
+Z_AT = 2 * ROW
+XW_AT = 6 * ROW
+PLACED_AT = (XW_AT + ROW - EDGE, XW_AT - ROW + EDGE)
+W2_CODES_AT = PLACED_AT[1]
 
 
 def tile_picked_headmod_gelu_p_kernel(tc, x_words, x_scales, w1, wt, w2, offs, take, out):
@@ -29,11 +50,11 @@ def tile_picked_headmod_gelu_p_kernel(tc, x_words, x_scales, w1, wt, w2, offs, t
         order = ctx.enter_context(tc.tile_pool(name="order", bufs=1))
         psum = ctx.enter_context(tc.psum_pool(name="psum", bufs=1))
 
-        offs_t = keep.tile([P, S // 16], U16, name="offs_t")
-        take_t = keep.tile([P, V // 16], U16, name="take_t")
+        offs_t = keep.tile([P, S // GROUP], U16, name="offs_t")
+        take_t = keep.tile([P, V // GROUP], U16, name="take_t")
         head = ctx.enter_context(tc.tile_pool(name="head", bufs=1))
-        xs_win = head.tile([P, T], U8, name="xs_win", offset=2048, align_bytes=64)
-        xw_win = keep.tile([P, T], I32, name="xw_win", align_bytes=64)
+        xs_win = head.tile([P, T], U8, name="xs_win", offset=XS_WIN_AT, align_bytes=EDGE)
+        xw_win = keep.tile([P, T], I32, name="xw_win", align_bytes=EDGE)
         w1_raw = keep.tile([P, PACK, H], F32, name="w1_raw")
 
         nc.vector.memset(xs_win[:].bitcast(I32), 0)
@@ -43,19 +64,21 @@ def tile_picked_headmod_gelu_p_kernel(tc, x_words, x_scales, w1, wt, w2, offs, t
         nc.sync.dma_start(offs_t[:], offs)
         nc.sync.dma_start(out=w1_raw[:, 2:4, :], in_=w1_rows[:, 2:4, :])
         nc.sync.dma_start(out=xw_win[:], in_=x_words[0].rearrange("p c r -> p (c r)").bitcast(I32))
-        xs_spread = head.tile([P, S], U8, name="xs_spread", offset=20480, align_bytes=64)
+
+        xs_spread = head.tile([P, S], U8, name="xs_spread", offset=XS_SPREAD_AT, align_bytes=EDGE)
         nc.vector.tensor_copy(xs_spread[:], xs_win[:].indirect(offs_t[:]))
-        xs = keep.tile([P, S], U8, name="xs", align_bytes=64)
+        xs = keep.tile([P, S], U8, name="xs", align_bytes=EDGE)
         nc.vector.memset(xs[:].bitcast(I32), 0)
         for q in range(4):
             nc.sync.dma_start(
                 out=xs[32 * q : 32 * q + 4, :].bitcast(I32), in_=xs_spread[32 * q + 4 : 32 * q + 32 : 8, :].bitcast(I32)
             )
-        w2_view = w2.rearrange("(p j) c -> p j c", j=PACK)
+
+        w2_rows = w2.rearrange("(p j) c -> p j c", j=PACK)
         nc.sync.dma_start(take_t[:], take)
-        w2_early = head.tile([P, PACK, P], F32, name="w2_early", offset=64, align_bytes=64)
-        nc.sync.dma_start(out=w2_early[:], in_=w2_view[:, :, 0:P])
-        wt_t = head.tile([P, V], F32, name="wt_t", offset=2560, align_bytes=64)
+        w2_early = head.tile([P, PACK, P], F32, name="w2_early", offset=W2_EARLY_AT, align_bytes=EDGE)
+        nc.sync.dma_start(out=w2_early[:], in_=w2_rows[:, :, 0:P])
+        wt_t = head.tile([P, V], F32, name="wt_t", offset=WT_AT, align_bytes=EDGE)
         nc.sync.dma_start(out=wt_t[:], in_=wt.rearrange("(p f) v -> p f v", f=PACK)[:, 0, :])
 
         warm = keep.tile([P, 8], F32, name="warm")
@@ -63,24 +86,24 @@ def tile_picked_headmod_gelu_p_kernel(tc, x_words, x_scales, w1, wt, w2, offs, t
         nc.vector.memset(warm[:], 0.0)
         nc.scalar.activation(warm_out[:], warm[:], GELU)
 
-
         w1_view = w1_raw[:].rearrange("p j (m t) -> p m j t", t=PACK)
-        w1_grouped = head.tile([P, PACK, P, PACK], BF16, name="w1_grouped", offset=6144, align_bytes=64)
+        w1_grouped = head.tile([P, PACK, P, PACK], BF16, name="w1_grouped", offset=W1_GROUPED_AT, align_bytes=EDGE)
         w1_dealt = w1_grouped[:].rearrange("p t m j -> p m j t")
-        nc.vector.tensor_copy(out=w1_dealt[:, 0:80], in_=w1_view[:, 0:80])
-        nc.scalar.copy(out=w1_dealt[:, 80:P], in_=w1_view[:, 80:P])
-        w1_codes = head.tile([P, H], U32, name="w1_codes", offset=4096 - 64, align_bytes=64)
-        w1_scales = keep.tile([P, H], U8, name="w1_scales", align_bytes=64)
+        nc.vector.tensor_copy(out=w1_dealt[:, 0:VECTOR_GROUPS], in_=w1_view[:, 0:VECTOR_GROUPS])
+        nc.scalar.copy(out=w1_dealt[:, VECTOR_GROUPS:P], in_=w1_view[:, VECTOR_GROUPS:P])
+        w1_codes = head.tile([P, H], U32, name="w1_codes", offset=W1_CODES_AT, align_bytes=EDGE)
+        w1_scales = keep.tile([P, H], U8, name="w1_scales", align_bytes=EDGE)
         nc.vector.quantize_mx(
             out=w1_codes[:].bitcast(FP8X4), scales=w1_scales[:], in_=w1_grouped[:].rearrange("p t m j -> p (t m j)")
         )
-        w2_raw = head.tile([P, PACK, N - P], F32, name="w2_raw", offset=10176, align_bytes=64)
-        nc.sync.dma_start(out=w2_raw[:], in_=w2_view[:, :, P:N])
-        xw = order.tile([P, S], U32, name="xw", offset=12288, align_bytes=64)
+        w2_raw = head.tile([P, PACK, N - P], F32, name="w2_raw", offset=W2_RAW_AT, align_bytes=EDGE)
+        nc.sync.dma_start(out=w2_raw[:], in_=w2_rows[:, :, P:N])
+
+        xw = order.tile([P, S], U32, name="xw", offset=XW_AT, align_bytes=EDGE)
         for h in range(2):
             nc.vector.tensor_copy(
                 xw[:, h * HALF : (h + 1) * HALF],
-                xw_win[:].bitcast(U32).indirect(offs_t[:, h * HALF // 16 : (h + 1) * HALF // 16]),
+                xw_win[:].bitcast(U32).indirect(offs_t[:, h * HALF // GROUP : (h + 1) * HALF // GROUP]),
             )
 
         def first_layer(t, cols, bank):
@@ -98,16 +121,17 @@ def tile_picked_headmod_gelu_p_kernel(tc, x_words, x_scales, w1, wt, w2, offs, t
             return acc
 
         halves = [slice(0, HALF), slice(HALF, S)]
+        quarters = [slice(a, a + QUARTER) for a in range(0, S, QUARTER)]
         whole = slice(0, S)
         rows = [keep.tile([P, S], F32, name=f"rows{t}") for t in range(PACK)]
         gelu_rows = [
             keep.tile([P, S], F32, name="gelu_rows0"),
-            order.tile([P, S], F32, name="gelu_rows1", offset=2048, align_bytes=64),
+            order.tile([P, S], F32, name="gelu_rows1", offset=GELU_LAST_AT, align_bytes=EDGE),
         ]
+        y_passes = [(2, halves[0]), (3, halves[0]), (2, quarters[2]), (2, quarters[3])]
+        y_passes += [(3, halves[1]), (0, whole), (1, whole)]
         dense = []
-        passes = [(2, halves[0]), (3, halves[0]), (2, slice(HALF, HALF + QUARTER)), (2, slice(HALF + QUARTER, S))]
-        passes += [(3, halves[1]), (0, whole), (1, whole)]
-        for bank, (t, cols) in enumerate(passes):
+        for bank, (t, cols) in enumerate(y_passes):
             acc = first_layer(t, cols, bank)
             if t < 2:
                 dense.append((t, cols, acc))
@@ -118,18 +142,18 @@ def tile_picked_headmod_gelu_p_kernel(tc, x_words, x_scales, w1, wt, w2, offs, t
         def four_at_a_time(grouped, raw):
             return grouped.rearrange("p (c i) j -> p c j i", i=4), raw.rearrange("p j (c i) -> p c j i", i=4)
 
-        def quantize(name, grouped, width, slot):
-            codes = keep.tile([P, width], U32, name=f"{name}_codes", tag=slot, align_bytes=64)
-            scales = keep.tile([P, width], U8, name=f"{name}_scales", align_bytes=64)
-            nc.vector.quantize_mx(out=codes[:].bitcast(FP8X4), scales=scales[:], in_=grouped.rearrange("p c j -> p (c j)"))
-            return codes, scales
-
-        w2_first = keep.tile([P, P, PACK], BF16, name="w2_first", tag="w2_first_slot", align_bytes=64)
+        w2_first = keep.tile([P, P, PACK], BF16, name="w2_first", tag="w2_first_slot", align_bytes=EDGE)
         nc.vector.tensor_copy(*four_at_a_time(w2_first[:], w2_early[:]))
-        codes, scales = quantize("w2_first", w2_first[:], P, "w2_first_codes")
-        w2_blocks = [(codes[:], scales[:])]
+        w2_first_codes = keep.tile([P, P], U32, name="w2_first_codes", align_bytes=EDGE)
+        w2_first_scales = keep.tile([P, P], U8, name="w2_first_scales", align_bytes=EDGE)
+        nc.vector.quantize_mx(
+            out=w2_first_codes[:].bitcast(FP8X4),
+            scales=w2_first_scales[:],
+            in_=w2_first[:].rearrange("p c j -> p (c j)"),
+        )
+        w2_blocks = [(w2_first_codes[:], w2_first_scales[:])]
 
-        picked = keep.tile([P, 2, V], F32, name="picked", tag="w2_first_slot", align_bytes=64)
+        picked = keep.tile([P, 2, V], F32, name="picked", tag="w2_first_slot", align_bytes=EDGE)
         act = keep.tile([P, 2, V], F32, name="act")
         routed = [keep.tile([P, V], F32, name=f"routed{t}") for t in range(2)]
         for t in range(2):
@@ -142,24 +166,20 @@ def tile_picked_headmod_gelu_p_kernel(tc, x_words, x_scales, w1, wt, w2, offs, t
             nc.scalar.copy(out=rows[t][:, cols], in_=acc[:])
 
         placed = [
-            order.tile([P, S], F32, name="placed0", offset=12288 + 2048 - 64, align_bytes=64),
-            order.tile([P, S], F32, name="placed1", offset=12288 - 2048 + 64, align_bytes=64),
+            order.tile([P, S], F32, name=f"placed{t}", offset=PLACED_AT[t], align_bytes=EDGE) for t in range(2)
         ]
         for t in (1, 0):
             nc.gpsimd.memset(placed[t][:], 0.0)
 
-        w2_late = order.tile([P, N - P, PACK], BF16, name="w2_late", offset=0, align_bytes=64)
-        for b in range(3):
+        w2_late = order.tile([P, N - P, PACK], BF16, name="w2_late", offset=W2_LATE_AT, align_bytes=EDGE)
+        for b in range(PACK - 1):
             cols = slice(b * P, (b + 1) * P)
             nc.scalar.copy(*four_at_a_time(w2_late[:, cols, :], w2_raw[:, :, cols]))
 
-        bounds = list(range(0, S + 1, QUARTER))
-        pieces = [slice(a, b) for a, b in zip(bounds, bounds[1:])]
-        z_all = order.tile([P, S, PACK], BF16, name="z_all", offset=4096, align_bytes=64)
-
+        z_all = order.tile([P, S, PACK], BF16, name="z_all", offset=Z_AT, align_bytes=EDGE)
         for t in range(2):
             nc.vector.tensor_copy(placed[t][:].indirect(take_t[:]), routed[t][:])
-        weighted = order.tile([P, 2, V], F32, name="weighted", offset=3072, align_bytes=64)
+        weighted = order.tile([P, 2, V], F32, name="weighted", offset=WEIGHTED_AT, align_bytes=EDGE)
         summed = keep.tile([P, 2, V], F32, name="summed")
         nc.gpsimd.tensor_tensor(weighted[:], act[:], wt_t[:].unsqueeze(1).to_broadcast([P, 2, V]), MULT)
         nc.gpsimd.tensor_tensor(summed[:], weighted[:], picked[:], ADD)
@@ -168,11 +188,11 @@ def tile_picked_headmod_gelu_p_kernel(tc, x_words, x_scales, w1, wt, w2, offs, t
         nc.vector.tensor_copy(rows[2][:].indirect(take_t[:]), summed[:, 0, :])
         nc.scalar.copy(out=z_all[:, :, 2], in_=rows[2][:])
         nc.vector.tensor_copy(rows[3][:].indirect(take_t[:]), summed[:, 1, :])
-        for cols in pieces:
+        for cols in quarters:
             nc.scalar.copy(out=z_all[:, cols, 3], in_=rows[3][:, cols])
 
-        w2_codes = order.tile([P, N - P], U32, name="w2_codes", offset=12288 - 2048 + 64, align_bytes=64)
-        w2_scales = keep.tile([P, N - P], U8, name="w2_scales", align_bytes=64)
+        w2_codes = order.tile([P, N - P], U32, name="w2_codes", offset=W2_CODES_AT, align_bytes=EDGE)
+        w2_scales = keep.tile([P, N - P], U8, name="w2_scales", align_bytes=EDGE)
 
         def quantize_w2(b):
             cols = slice(b * P, (b + 1) * P)
@@ -186,8 +206,8 @@ def tile_picked_headmod_gelu_p_kernel(tc, x_words, x_scales, w1, wt, w2, offs, t
         quantize_w2(0)
         quantize_w2(1)
 
-        z_codes = keep.tile([P, S], U32, name="z_codes", align_bytes=64)
-        z_scales = keep.tile([P, S], U8, name="z_scales", align_bytes=64)
+        z_codes = keep.tile([P, S], U32, name="z_codes", align_bytes=EDGE)
+        z_scales = keep.tile([P, S], U8, name="z_scales", align_bytes=EDGE)
 
         def quantize_z(cols):
             nc.vector.quantize_mx(
@@ -199,15 +219,16 @@ def tile_picked_headmod_gelu_p_kernel(tc, x_words, x_scales, w1, wt, w2, offs, t
         results = keep.tile([P, PACK, S], F32, name="results")
         out_view = out.rearrange("(b p) s -> p b s", p=P)
 
-        def product(bank, block, passes, on_vector):
+        def product(n, block, passes, on_vector):
             first, last = passes[0].start, passes[-1].stop
-            acc = psum.tile([P, last - first], F32, name=f"out_acc{bank}", tag=f"bank{(7 + bank) % 8}")
-            w2_codes, w2_scales = w2_blocks[block]
+            bank = (len(y_passes) + n) % BANKS
+            acc = psum.tile([P, last - first], F32, name=f"out_acc{n}", tag=f"bank{bank}")
+            block_codes, block_scales = w2_blocks[block]
             for cols in passes:
                 nc.tensor.matmul_mx(
                     out=acc[:, cols.start - first : cols.stop - first],
-                    lhsT=w2_codes.bitcast(FP8X4),
-                    lhsT_scale=w2_scales,
+                    lhsT=block_codes.bitcast(FP8X4),
+                    lhsT_scale=block_scales,
                     rhs=z_codes[:, cols].bitcast(FP8X4),
                     rhs_scale=z_scales[:, cols],
                     start=True,
@@ -221,27 +242,24 @@ def tile_picked_headmod_gelu_p_kernel(tc, x_words, x_scales, w1, wt, w2, offs, t
         def store(block, cols):
             nc.sync.dma_start(out=out_view[:, block, cols], in_=results[:, block, cols])
 
-        rest = slice(QUARTER, S)
-        quantize_z(pieces[0])
+        quantize_z(quarters[0])
         quantize_w2(2)
-        quantize_z(pieces[1])
-        product(0, 0, pieces[0:1], True)
-        store(0, pieces[0])
-        product(1, 1, pieces[0:1], False)
-        store(1, pieces[0])
-        product(2, 2, pieces[0:2], False)
+        quantize_z(quarters[1])
+        product(0, 0, quarters[0:1], True)
+        store(0, quarters[0])
+        product(1, 1, quarters[0:1], False)
+        product(2, 2, quarters[0:1], False)
+        product(3, 1, quarters[1:2], False)
+        store(1, halves[0])
+        product(4, 2, quarters[1:2], True)
         store(2, halves[0])
-        quantize_z(pieces[2])
-        quantize_z(pieces[3])
-        product(3, 3, halves[0:1], True)
+        quantize_z(quarters[2])
+        quantize_z(quarters[3])
+        product(5, 3, halves[0:1], False)
         store(3, halves[0])
-        product(4, 0, pieces[1:3], False)
-        product(5, 0, pieces[3:4], True)
-        store(0, rest)
-        product(6, 1, pieces[1:2], False)
-        product(7, 1, halves[1:2], True)
-        store(1, rest)
-        product(8, 2, halves[1:2], False)
-        store(2, halves[1])
-        product(9, 3, halves[1:2], True)
-        store(3, halves[1])
+        product(6, 0, quarters[1:3], False)
+        product(7, 0, quarters[3:4], True)
+        store(0, slice(QUARTER, S))
+        for block in range(1, PACK):
+            product(7 + block, block, halves[1:2], block % 2 == 0)
+            store(block, halves[1])

@@ -12,6 +12,7 @@ U32 = mybir.dt.uint32
 U16 = mybir.dt.uint16
 U8 = mybir.dt.uint8
 FP8X4 = mybir.dt.float8_e4m3fn_x4
+COPY = mybir.ActivationFunctionType.Copy
 GELU = mybir.ActivationFunctionType.Gelu_apprx_tanh
 ADD = mybir.AluOpType.add
 MULT = mybir.AluOpType.mult
@@ -28,18 +29,19 @@ VECTOR_GROUPS = 80
 ROW = 4 * S
 EDGE = 64
 XS_WIN_AT = ROW
-W2_EARLY_AT = XS_WIN_AT - ROW + EDGE
 WT_AT = XS_WIN_AT + ROW // 4
 W1_CODES_AT = XS_WIN_AT + ROW - EDGE
 W1_GROUPED_AT = 3 * ROW
 W2_RAW_AT = W1_GROUPED_AT + 2 * ROW - EDGE
 XS_SPREAD_AT = 10 * ROW
 W2_LATE_AT = 0
-GELU_LAST_AT = ROW
-WEIGHTED_AT = 3 * ROW // 2
-Z_AT = 2 * ROW
+WEIGHTED_FIRST_AT = 3 * ROW // 2 - EDGE
+W2_FIRST_AT = 14 * ROW
+ROUTED_AT = (W2_FIRST_AT + EDGE, W2_FIRST_AT + ROW // 2 + EDGE)
+WEIGHTED_AT = WEIGHTED_FIRST_AT + ROW // 2 - EDGE
+Z_AT = WEIGHTED_AT + ROW // 2 - EDGE
 XW_AT = 6 * ROW
-PLACED_AT = (XW_AT + ROW - EDGE, XW_AT - ROW + EDGE)
+PLACED_AT = (12 * ROW + EDGE, 8 * ROW)
 W2_CODES_AT = PLACED_AT[1]
 
 
@@ -76,7 +78,7 @@ def tile_picked_headmod_gelu_p_kernel(tc, x_words, x_scales, w1, wt, w2, offs, t
 
         w2_rows = w2.rearrange("(p j) c -> p j c", j=PACK)
         nc.sync.dma_start(take_t[:], take)
-        w2_early = head.tile([P, PACK, P], F32, name="w2_early", offset=W2_EARLY_AT, align_bytes=EDGE)
+        w2_early = keep.tile([P, PACK, P], F32, name="w2_early")
         nc.sync.dma_start(out=w2_early[:], in_=w2_rows[:, :, 0:P])
         wt_t = head.tile([P, V], F32, name="wt_t", offset=WT_AT, align_bytes=EDGE)
         nc.sync.dma_start(out=wt_t[:], in_=wt.rearrange("(p f) v -> p f v", f=PACK)[:, 0, :])
@@ -85,6 +87,9 @@ def tile_picked_headmod_gelu_p_kernel(tc, x_words, x_scales, w1, wt, w2, offs, t
         warm_out = keep.tile([P, 8], F32, name="warm_out")
         nc.vector.memset(warm[:], 0.0)
         nc.scalar.activation(warm_out[:], warm[:], GELU)
+
+        second_window = order.tile([P, 2 * S], F32, name="placed1", offset=PLACED_AT[1], align_bytes=EDGE)
+        nc.vector.memset(second_window[:, 0:S], 0.0)
 
         w1_view = w1_raw[:].rearrange("p j (m t) -> p m j t", t=PACK)
         w1_grouped = head.tile([P, PACK, P, PACK], BF16, name="w1_grouped", offset=W1_GROUPED_AT, align_bytes=EDGE)
@@ -107,7 +112,7 @@ def tile_picked_headmod_gelu_p_kernel(tc, x_words, x_scales, w1, wt, w2, offs, t
             )
 
         def first_layer(t, cols, bank):
-            acc = psum.tile([P, cols.stop - cols.start], F32, name=f"y_acc{bank}", tag=f"bank{bank}")
+            acc = psum.tile([P, cols.stop - cols.start], F32, name=f"y_acc{t}_{cols.start}", tag=f"bank{bank}")
             stat = slice(t * P, (t + 1) * P)
             nc.tensor.matmul_mx(
                 out=acc[:],
@@ -123,53 +128,71 @@ def tile_picked_headmod_gelu_p_kernel(tc, x_words, x_scales, w1, wt, w2, offs, t
         halves = [slice(0, HALF), slice(HALF, S)]
         quarters = [slice(a, a + QUARTER) for a in range(0, S, QUARTER)]
         whole = slice(0, S)
-        rows = [keep.tile([P, S], F32, name=f"rows{t}") for t in range(PACK)]
-        gelu_rows = [
-            keep.tile([P, S], F32, name="gelu_rows0"),
-            order.tile([P, S], F32, name="gelu_rows1", offset=GELU_LAST_AT, align_bytes=EDGE),
-        ]
-        y_passes = [(2, halves[0]), (3, halves[0]), (2, quarters[2]), (2, quarters[3])]
-        y_passes += [(3, halves[1]), (0, whole), (1, whole)]
+        rows = {t: keep.tile([P, S], F32, name=f"rows{t}") for t in (2, 3)}
+        gelu_rows = [keep.tile([P, S], F32, name=f"gelu_rows{t}") for t in range(2)]
+        y_passes = [(0, halves[0]), (1, halves[0]), (0, quarters[2]), (0, quarters[3])]
+        y_passes += [(1, halves[1]), (2, halves[0]), (2, halves[1]), (3, halves[0])]
         dense = []
+        late = []
         for bank, (t, cols) in enumerate(y_passes):
             acc = first_layer(t, cols, bank)
             if t < 2:
                 dense.append((t, cols, acc))
                 nc.scalar.activation(gelu_rows[t][:, cols], acc[:], GELU)
             else:
-                nc.scalar.copy(out=rows[t][:, cols], in_=acc[:])
+                late.append((t, cols, acc))
 
         def four_at_a_time(grouped, raw):
             return grouped.rearrange("p (c i) j -> p c j i", i=4), raw.rearrange("p j (c i) -> p c j i", i=4)
 
-        w2_first = keep.tile([P, P, PACK], BF16, name="w2_first", tag="w2_first_slot", align_bytes=EDGE)
-        nc.vector.tensor_copy(*four_at_a_time(w2_first[:], w2_early[:]))
+        def keep_y(copy, entry):
+            t, cols, acc = entry
+            copy(out=placed[1 - t][:, S + cols.start : S + cols.stop], in_=acc[:])
+
+        w2_first_room = order.tile([P, P + 16, PACK], BF16, name="w2_first", offset=W2_FIRST_AT, align_bytes=EDGE)
+        w2_first = w2_first_room[:, 0:P, :]
+        nc.vector.tensor_copy(*four_at_a_time(w2_first, w2_early[:]))
         w2_first_codes = keep.tile([P, P], U32, name="w2_first_codes", align_bytes=EDGE)
         w2_first_scales = keep.tile([P, P], U8, name="w2_first_scales", align_bytes=EDGE)
         nc.vector.quantize_mx(
             out=w2_first_codes[:].bitcast(FP8X4),
             scales=w2_first_scales[:],
-            in_=w2_first[:].rearrange("p c j -> p (c j)"),
+            in_=w2_first.rearrange("p c j -> p (c j)"),
         )
+        first_window = order.tile([P, 2 * S], F32, name="placed0", offset=PLACED_AT[0], align_bytes=EDGE)
+        placed = [first_window, second_window]
+        keep_y(nc.vector.tensor_copy, dense[1])
+        nc.gpsimd.memset(placed[0][:, 0:S], 0.0)
         w2_blocks = [(w2_first_codes[:], w2_first_scales[:])]
 
-        picked = keep.tile([P, 2, V], F32, name="picked", tag="w2_first_slot", align_bytes=EDGE)
-        act = keep.tile([P, 2, V], F32, name="act")
-        routed = [keep.tile([P, V], F32, name=f"routed{t}") for t in range(2)]
-        for t in range(2):
-            nc.vector.tensor_copy(picked[:, t, :], rows[t + 2][:].indirect(take_t[:]))
+        routed = [
+            order.tile([P, V], F32, name=f"routed{t}", offset=ROUTED_AT[t], align_bytes=EDGE) for t in range(2)
+        ]
         for t in range(2):
             nc.vector.tensor_tensor(routed[t][:], gelu_rows[t][:].indirect(take_t[:]), wt_t[:], MULT)
-        for t in range(2):
-            nc.scalar.activation(act[:, t, :], picked[:, t, :], GELU)
-        for t, cols, acc in dense:
+        picked = [keep.tile([P, V], F32, name=f"picked{t}") for t in range(2)]
+        act = [keep.tile([P, V], F32, name=f"act{t}") for t in range(2)]
+        for t, cols, acc in late[0:2]:
             nc.scalar.copy(out=rows[t][:, cols], in_=acc[:])
-
-        placed = [
-            order.tile([P, S], F32, name=f"placed{t}", offset=PLACED_AT[t], align_bytes=EDGE) for t in range(2)
+        late.append((3, halves[1], first_layer(3, halves[1], 5)))
+        keep_y(nc.scalar.copy, dense[4])
+        nc.scalar.activation(picked[0][:], rows[2][:].indirect(take_t[:]), COPY)
+        keep_y(nc.scalar.copy, dense[0])
+        nc.scalar.activation(act[0][:], picked[0][:], GELU)
+        for t, cols, acc in late[2:4]:
+            nc.scalar.copy(out=rows[t][:, cols], in_=acc[:])
+        for entry in dense[2:4]:
+            keep_y(nc.scalar.copy, entry)
+        nc.scalar.activation(picked[1][:], rows[3][:].indirect(take_t[:]), COPY)
+        nc.scalar.activation(act[1][:], picked[1][:], GELU)
+        weighted = [
+            order.tile([P, V], F32, name="weighted0", offset=WEIGHTED_FIRST_AT, align_bytes=EDGE),
+            order.tile([P, V], F32, name="weighted1", offset=WEIGHTED_AT, align_bytes=EDGE),
         ]
-        for t in (1, 0):
-            nc.gpsimd.memset(placed[t][:], 0.0)
+        summed = keep.tile([P, 2, V], F32, name="summed")
+        for t in range(2):
+            nc.gpsimd.tensor_tensor(weighted[t][:], act[t][:], wt_t[:], MULT)
+            nc.gpsimd.tensor_tensor(summed[:, t, :], weighted[t][:], picked[t][:], ADD)
 
         w2_late = order.tile([P, N - P, PACK], BF16, name="w2_late", offset=W2_LATE_AT, align_bytes=EDGE)
         for b in range(PACK - 1):
@@ -179,12 +202,15 @@ def tile_picked_headmod_gelu_p_kernel(tc, x_words, x_scales, w1, wt, w2, offs, t
         z_all = order.tile([P, S, PACK], BF16, name="z_all", offset=Z_AT, align_bytes=EDGE)
         for t in range(2):
             nc.vector.tensor_copy(placed[t][:].indirect(take_t[:]), routed[t][:])
-        weighted = order.tile([P, 2, V], F32, name="weighted", offset=WEIGHTED_AT, align_bytes=EDGE)
-        summed = keep.tile([P, 2, V], F32, name="summed")
-        nc.gpsimd.tensor_tensor(weighted[:], act[:], wt_t[:].unsqueeze(1).to_broadcast([P, 2, V]), MULT)
-        nc.gpsimd.tensor_tensor(summed[:], weighted[:], picked[:], ADD)
-        for t in range(2):
-            nc.gpsimd.tensor_tensor(z_all[:, :, t], rows[t][:], placed[t][:], ADD)
+        forward = placed[0][:].rearrange("p (t s) -> p t s", t=2)
+        backward = placed[1][:].rearrange("p (t s) -> p t s", t=2)[:, ::-1, :]
+        for cols in halves:
+            nc.gpsimd.tensor_tensor(
+                z_all[:, cols, 0:2].rearrange("p (c i) t -> p c t i", i=2),
+                forward[:, :, cols].rearrange("p t (c i) -> p c t i", i=2),
+                backward[:, :, cols].rearrange("p t (c i) -> p c t i", i=2),
+                ADD,
+            )
         nc.vector.tensor_copy(rows[2][:].indirect(take_t[:]), summed[:, 0, :])
         nc.scalar.copy(out=z_all[:, :, 2], in_=rows[2][:])
         nc.vector.tensor_copy(rows[3][:].indirect(take_t[:]), summed[:, 1, :])

@@ -25,24 +25,28 @@ HALF = S // 2
 QUARTER = S // 4
 
 VECTOR_GROUPS = 80
+NEXT = 64
 
 ROW = 4 * S
 EDGE = 64
 XS_WIN_AT = ROW
 WT_AT = XS_WIN_AT + ROW // 4
+W2_NEXT_AT = XS_WIN_AT - ROW // 2 + EDGE
 W1_CODES_AT = XS_WIN_AT + ROW - EDGE
 W1_GROUPED_AT = 3 * ROW
 W2_RAW_AT = W1_GROUPED_AT + 2 * ROW - EDGE
 XS_SPREAD_AT = 10 * ROW
-W2_LATE_AT = 0
-WEIGHTED_FIRST_AT = 3 * ROW // 2 - EDGE
-W2_FIRST_AT = 14 * ROW
-ROUTED_AT = (W2_FIRST_AT + EDGE, W2_FIRST_AT + ROW // 2 + EDGE)
-WEIGHTED_AT = WEIGHTED_FIRST_AT + ROW // 2 - EDGE
-Z_AT = WEIGHTED_AT + ROW // 2 - EDGE
-XW_AT = 6 * ROW
-PLACED_AT = (12 * ROW + EDGE, 8 * ROW)
+W2_LATE_AT = ROW // 4
+WEIGHTED_AT = (3 * ROW // 2 - EDGE, 3 * ROW)
+ACT_AT = (WEIGHTED_AT[1] + ROW // 2 - EDGE, 4 * ROW + EDGE)
+Z_AT = ACT_AT[1] + ROW // 2 - EDGE
+XW_AT = 7 * ROW
+W2_EARLY_AT = 10 * ROW
+ROUTED_AT = (W2_EARLY_AT + EDGE, W2_EARLY_AT + ROW // 2 + EDGE)
+PLACED_AT = (W2_EARLY_AT - 2 * ROW + EDGE, W2_EARLY_AT + ROW + EDGE)
 W2_CODES_AT = PLACED_AT[1]
+GELU_LAST_AT = 14 * ROW
+W2_SECOND_AT = GELU_LAST_AT + ROW - EDGE
 
 
 def tile_picked_headmod_gelu_p_kernel(tc, x_words, x_scales, w1, wt, w2, offs, take, out):
@@ -78,18 +82,19 @@ def tile_picked_headmod_gelu_p_kernel(tc, x_words, x_scales, w1, wt, w2, offs, t
 
         w2_rows = w2.rearrange("(p j) c -> p j c", j=PACK)
         nc.sync.dma_start(take_t[:], take)
-        w2_early = keep.tile([P, PACK, P], F32, name="w2_early")
-        nc.sync.dma_start(out=w2_early[:], in_=w2_rows[:, :, 0:P])
+        w2_early_room = order.tile([P, PACK * P + 32], F32, name="w2_early", offset=W2_EARLY_AT, align_bytes=EDGE)
+        w2_early = w2_early_room[:, 0 : PACK * P].rearrange("p (j c) -> p j c", j=PACK)
+        nc.sync.dma_start(out=w2_early, in_=w2_rows[:, :, 0:P])
         wt_t = head.tile([P, V], F32, name="wt_t", offset=WT_AT, align_bytes=EDGE)
         nc.sync.dma_start(out=wt_t[:], in_=wt.rearrange("(p f) v -> p f v", f=PACK)[:, 0, :])
+
+        w2_next = head.tile([P, PACK, NEXT], F32, name="w2_next", offset=W2_NEXT_AT, align_bytes=EDGE)
+        nc.sync.dma_start(out=w2_next[:], in_=w2_rows[:, :, P : P + NEXT])
 
         warm = keep.tile([P, 8], F32, name="warm")
         warm_out = keep.tile([P, 8], F32, name="warm_out")
         nc.vector.memset(warm[:], 0.0)
         nc.scalar.activation(warm_out[:], warm[:], GELU)
-
-        second_window = order.tile([P, 2 * S], F32, name="placed1", offset=PLACED_AT[1], align_bytes=EDGE)
-        nc.vector.memset(second_window[:, 0:S], 0.0)
 
         w1_view = w1_raw[:].rearrange("p j (m t) -> p m j t", t=PACK)
         w1_grouped = head.tile([P, PACK, P, PACK], BF16, name="w1_grouped", offset=W1_GROUPED_AT, align_bytes=EDGE)
@@ -101,8 +106,8 @@ def tile_picked_headmod_gelu_p_kernel(tc, x_words, x_scales, w1, wt, w2, offs, t
         nc.vector.quantize_mx(
             out=w1_codes[:].bitcast(FP8X4), scales=w1_scales[:], in_=w1_grouped[:].rearrange("p t m j -> p (t m j)")
         )
-        w2_raw = head.tile([P, PACK, N - P], F32, name="w2_raw", offset=W2_RAW_AT, align_bytes=EDGE)
-        nc.sync.dma_start(out=w2_raw[:], in_=w2_rows[:, :, P:N])
+        w2_raw = head.tile([P, PACK, N - P - NEXT], F32, name="w2_raw", offset=W2_RAW_AT, align_bytes=EDGE)
+        nc.sync.dma_start(out=w2_raw[:], in_=w2_rows[:, :, P + NEXT : N])
 
         xw = order.tile([P, S], U32, name="xw", offset=XW_AT, align_bytes=EDGE)
         for h in range(2):
@@ -112,7 +117,7 @@ def tile_picked_headmod_gelu_p_kernel(tc, x_words, x_scales, w1, wt, w2, offs, t
             )
 
         def first_layer(t, cols, bank):
-            acc = psum.tile([P, cols.stop - cols.start], F32, name=f"y_acc{t}_{cols.start}", tag=f"bank{bank}")
+            acc = psum.tile([P, cols.stop - cols.start], F32, name=f"y_acc{t}_{cols.start}_{bank}", tag=f"bank{bank}")
             stat = slice(t * P, (t + 1) * P)
             nc.tensor.matmul_mx(
                 out=acc[:],
@@ -129,7 +134,10 @@ def tile_picked_headmod_gelu_p_kernel(tc, x_words, x_scales, w1, wt, w2, offs, t
         quarters = [slice(a, a + QUARTER) for a in range(0, S, QUARTER)]
         whole = slice(0, S)
         rows = {t: keep.tile([P, S], F32, name=f"rows{t}") for t in (2, 3)}
-        gelu_rows = [keep.tile([P, S], F32, name=f"gelu_rows{t}") for t in range(2)]
+        gelu_rows = [
+            keep.tile([P, S], F32, name="gelu_rows0"),
+            order.tile([P, S], F32, name="gelu_rows1", offset=GELU_LAST_AT, align_bytes=EDGE),
+        ]
         y_passes = [(0, halves[0]), (1, halves[0]), (0, quarters[2]), (0, quarters[3])]
         y_passes += [(1, halves[1]), (2, halves[0]), (2, halves[1]), (3, halves[0])]
         dense = []
@@ -149,97 +157,98 @@ def tile_picked_headmod_gelu_p_kernel(tc, x_words, x_scales, w1, wt, w2, offs, t
             t, cols, acc = entry
             copy(out=placed[1 - t][:, S + cols.start : S + cols.stop], in_=acc[:])
 
-        w2_first_room = order.tile([P, P + 16, PACK], BF16, name="w2_first", offset=W2_FIRST_AT, align_bytes=EDGE)
-        w2_first = w2_first_room[:, 0:P, :]
-        nc.vector.tensor_copy(*four_at_a_time(w2_first, w2_early[:]))
-        w2_first_codes = keep.tile([P, P], U32, name="w2_first_codes", align_bytes=EDGE)
-        w2_first_scales = keep.tile([P, P], U8, name="w2_first_scales", align_bytes=EDGE)
-        nc.vector.quantize_mx(
-            out=w2_first_codes[:].bitcast(FP8X4),
-            scales=w2_first_scales[:],
-            in_=w2_first.rearrange("p c j -> p (c j)"),
-        )
-        first_window = order.tile([P, 2 * S], F32, name="placed0", offset=PLACED_AT[0], align_bytes=EDGE)
-        placed = [first_window, second_window]
-        keep_y(nc.vector.tensor_copy, dense[1])
-        nc.gpsimd.memset(placed[0][:, 0:S], 0.0)
-        w2_blocks = [(w2_first_codes[:], w2_first_scales[:])]
+        w2_first = keep.tile([P, P, PACK], BF16, name="w2_first", align_bytes=EDGE)
+        nc.vector.tensor_copy(*four_at_a_time(w2_first[:], w2_early))
+        placed = [
+            order.tile([P, 2 * S], F32, name=f"placed{t}", offset=PLACED_AT[t], align_bytes=EDGE) for t in range(2)
+        ]
+        for entry in dense[0:2]:
+            keep_y(nc.vector.tensor_copy, entry)
+        for t in range(2):
+            nc.gpsimd.memset(placed[t][:, 0:S], 0.0)
 
         routed = [
             order.tile([P, V], F32, name=f"routed{t}", offset=ROUTED_AT[t], align_bytes=EDGE) for t in range(2)
         ]
         for t in range(2):
             nc.vector.tensor_tensor(routed[t][:], gelu_rows[t][:].indirect(take_t[:]), wt_t[:], MULT)
+        w2_second = order.tile([P, NEXT, PACK], BF16, name="w2_second", offset=W2_SECOND_AT, align_bytes=EDGE)
+        nc.gpsimd.tensor_scalar(*four_at_a_time(w2_second[:], w2_next[:]), 1.0, 0.0, MULT, ADD)
         picked = [keep.tile([P, V], F32, name=f"picked{t}") for t in range(2)]
-        act = [keep.tile([P, V], F32, name=f"act{t}") for t in range(2)]
-        for t, cols, acc in late[0:2]:
+        act = [order.tile([P, V], F32, name=f"act{t}", offset=ACT_AT[t], align_bytes=EDGE) for t in range(2)]
+
+        def keep_row(entry):
+            t, cols, acc = entry
             nc.scalar.copy(out=rows[t][:, cols], in_=acc[:])
+
+        keep_row(late[0])
+        keep_row(late[1])
         late.append((3, halves[1], first_layer(3, halves[1], 5)))
-        keep_y(nc.scalar.copy, dense[4])
         nc.scalar.activation(picked[0][:], rows[2][:].indirect(take_t[:]), COPY)
-        keep_y(nc.scalar.copy, dense[0])
         nc.scalar.activation(act[0][:], picked[0][:], GELU)
-        for t, cols, acc in late[2:4]:
-            nc.scalar.copy(out=rows[t][:, cols], in_=acc[:])
-        for entry in dense[2:4]:
-            keep_y(nc.scalar.copy, entry)
+        keep_row(late[2])
+        keep_row(late[3])
         nc.scalar.activation(picked[1][:], rows[3][:].indirect(take_t[:]), COPY)
         nc.scalar.activation(act[1][:], picked[1][:], GELU)
         weighted = [
-            order.tile([P, V], F32, name="weighted0", offset=WEIGHTED_FIRST_AT, align_bytes=EDGE),
-            order.tile([P, V], F32, name="weighted1", offset=WEIGHTED_AT, align_bytes=EDGE),
+            order.tile([P, V], F32, name=f"weighted{t}", offset=WEIGHTED_AT[t], align_bytes=EDGE) for t in range(2)
         ]
-        summed = keep.tile([P, 2, V], F32, name="summed")
+        summed = [
+            keep.tile([P, V], F32, name="summed0"),
+            keep.tile([P, V], F32, name="summed1"),
+        ]
         for t in range(2):
             nc.gpsimd.tensor_tensor(weighted[t][:], act[t][:], wt_t[:], MULT)
-            nc.gpsimd.tensor_tensor(summed[:, t, :], weighted[t][:], picked[t][:], ADD)
-
-        w2_late = order.tile([P, N - P, PACK], BF16, name="w2_late", offset=W2_LATE_AT, align_bytes=EDGE)
-        for b in range(PACK - 1):
-            cols = slice(b * P, (b + 1) * P)
-            nc.scalar.copy(*four_at_a_time(w2_late[:, cols, :], w2_raw[:, :, cols]))
+            nc.gpsimd.tensor_tensor(summed[t][:], weighted[t][:], picked[t][:], ADD)
 
         z_all = order.tile([P, S, PACK], BF16, name="z_all", offset=Z_AT, align_bytes=EDGE)
         for t in range(2):
             nc.vector.tensor_copy(placed[t][:].indirect(take_t[:]), routed[t][:])
+            keep_y(nc.scalar.copy, (1 - t, halves[1], first_layer(1 - t, halves[1], 5)))
+        w2_late = order.tile([P, N - P - NEXT, PACK], BF16, name="w2_late", offset=W2_LATE_AT, align_bytes=EDGE)
+        late_pieces = [slice(0, NEXT), slice(NEXT, P + NEXT), slice(P + NEXT, N - P - NEXT)]
+        for cols in late_pieces:
+            nc.scalar.copy(*four_at_a_time(w2_late[:, cols, :], w2_raw[:, :, cols]))
+
         forward = placed[0][:].rearrange("p (t s) -> p t s", t=2)
         backward = placed[1][:].rearrange("p (t s) -> p t s", t=2)[:, ::-1, :]
-        for cols in halves:
+        for cols in [whole]:
             nc.gpsimd.tensor_tensor(
                 z_all[:, cols, 0:2].rearrange("p (c i) t -> p c t i", i=2),
                 forward[:, :, cols].rearrange("p t (c i) -> p c t i", i=2),
                 backward[:, :, cols].rearrange("p t (c i) -> p c t i", i=2),
                 ADD,
             )
-        nc.vector.tensor_copy(rows[2][:].indirect(take_t[:]), summed[:, 0, :])
+        nc.vector.tensor_copy(rows[2][:].indirect(take_t[:]), summed[0][:])
         nc.scalar.copy(out=z_all[:, :, 2], in_=rows[2][:])
-        nc.vector.tensor_copy(rows[3][:].indirect(take_t[:]), summed[:, 1, :])
+        nc.vector.tensor_copy(rows[3][:].indirect(take_t[:]), summed[1][:])
         for cols in quarters:
             nc.scalar.copy(out=z_all[:, cols, 3], in_=rows[3][:, cols])
 
-        w2_codes = order.tile([P, N - P], U32, name="w2_codes", offset=W2_CODES_AT, align_bytes=EDGE)
-        w2_scales = keep.tile([P, N - P], U8, name="w2_scales", align_bytes=EDGE)
+        w2_codes = order.tile([P, N], U32, name="w2_codes", offset=W2_CODES_AT, align_bytes=EDGE)
+        w2_scales = keep.tile([P, N], U8, name="w2_scales", align_bytes=EDGE)
+        w2_blocks = [(w2_codes[:, b * P : (b + 1) * P], w2_scales[:, b * P : (b + 1) * P]) for b in range(PACK)]
 
-        def quantize_w2(b):
-            cols = slice(b * P, (b + 1) * P)
+        def quantize_w2(first, grouped):
+            cols = slice(first, first + grouped.shape[1])
             nc.vector.quantize_mx(
                 out=w2_codes[:, cols].bitcast(FP8X4),
                 scales=w2_scales[:, cols],
-                in_=w2_late[:, cols, :].rearrange("p c j -> p (c j)"),
+                in_=grouped.rearrange("p c j -> p (c j)"),
             )
-            w2_blocks.append((w2_codes[:, cols], w2_scales[:, cols]))
 
-        quantize_w2(0)
-        quantize_w2(1)
+        quantize_w2(0, w2_first[:])
+        quantize_w2(P, w2_second[:])
+        quantize_w2(P + NEXT, w2_late[:, 0:NEXT, :])
 
         z_codes = keep.tile([P, S], U32, name="z_codes", align_bytes=EDGE)
         z_scales = keep.tile([P, S], U8, name="z_scales", align_bytes=EDGE)
 
-        def quantize_z(cols):
+        def quantize_z(cols, grouped):
             nc.vector.quantize_mx(
                 out=z_codes[:, cols].bitcast(FP8X4),
                 scales=z_scales[:, cols],
-                in_=z_all[:, cols, :].rearrange("p c j -> p (c j)"),
+                in_=grouped.rearrange("p c j -> p (c j)"),
             )
 
         results = keep.tile([P, PACK, S], F32, name="results")
@@ -268,9 +277,9 @@ def tile_picked_headmod_gelu_p_kernel(tc, x_words, x_scales, w1, wt, w2, offs, t
         def store(block, cols):
             nc.sync.dma_start(out=out_view[:, block, cols], in_=results[:, block, cols])
 
-        quantize_z(quarters[0])
-        quantize_w2(2)
-        quantize_z(quarters[1])
+        quantize_z(quarters[0], z_all[:, quarters[0], :])
+        quantize_w2(2 * P, w2_late[:, NEXT : P + NEXT, :])
+        quantize_z(quarters[1], z_all[:, quarters[1], :])
         product(0, 0, quarters[0:1], True)
         store(0, quarters[0])
         product(1, 1, quarters[0:1], False)
@@ -279,8 +288,9 @@ def tile_picked_headmod_gelu_p_kernel(tc, x_words, x_scales, w1, wt, w2, offs, t
         store(1, halves[0])
         product(4, 2, quarters[1:2], True)
         store(2, halves[0])
-        quantize_z(quarters[2])
-        quantize_z(quarters[3])
+        quantize_w2(3 * P, w2_late[:, P + NEXT : N - P - NEXT, :])
+        quantize_z(quarters[2], z_all[:, quarters[2], :])
+        quantize_z(quarters[3], z_all[:, quarters[3], :])
         product(5, 3, halves[0:1], False)
         store(3, halves[0])
         product(6, 0, quarters[1:3], False)

@@ -25,7 +25,8 @@ HALF = S // 2
 QUARTER = S // 4
 
 VECTOR_GROUPS = 80
-NEXT = 64
+GPSIMD_COLUMNS = 64
+LATE_START = P + GPSIMD_COLUMNS
 
 ROW = 4 * S
 EDGE = 64
@@ -42,11 +43,13 @@ ACT_AT = (WEIGHTED_AT[1] + ROW // 2 - EDGE, 4 * ROW + EDGE)
 Z_AT = ACT_AT[1] + ROW // 2 - EDGE
 XW_AT = 7 * ROW
 W2_EARLY_AT = 10 * ROW
+W2_EARLY_BYTES = ROW + 2 * EDGE
 ROUTED_AT = (W2_EARLY_AT + EDGE, W2_EARLY_AT + ROW // 2 + EDGE)
-PLACED_AT = (W2_EARLY_AT - 2 * ROW + EDGE, W2_EARLY_AT + ROW + EDGE)
-W2_CODES_AT = PLACED_AT[1]
+WINDOW_AT = (W2_EARLY_AT - 2 * ROW + EDGE, W2_EARLY_AT + ROW + EDGE)
+W2_CODES_AT = WINDOW_AT[1]
 GELU_LAST_AT = 14 * ROW
 W2_SECOND_AT = GELU_LAST_AT + ROW - EDGE
+LATE_BANK = 5
 
 
 def tile_picked_headmod_gelu_p_kernel(tc, x_words, x_scales, w1, wt, w2, offs, take, out):
@@ -82,14 +85,13 @@ def tile_picked_headmod_gelu_p_kernel(tc, x_words, x_scales, w1, wt, w2, offs, t
 
         w2_rows = w2.rearrange("(p j) c -> p j c", j=PACK)
         nc.sync.dma_start(take_t[:], take)
-        w2_early_room = order.tile([P, PACK * P + 32], F32, name="w2_early", offset=W2_EARLY_AT, align_bytes=EDGE)
+        w2_early_room = order.tile([P, W2_EARLY_BYTES // 4], F32, name="w2_early", offset=W2_EARLY_AT, align_bytes=EDGE)
         w2_early = w2_early_room[:, 0 : PACK * P].rearrange("p (j c) -> p j c", j=PACK)
         nc.sync.dma_start(out=w2_early, in_=w2_rows[:, :, 0:P])
         wt_t = head.tile([P, V], F32, name="wt_t", offset=WT_AT, align_bytes=EDGE)
         nc.sync.dma_start(out=wt_t[:], in_=wt.rearrange("(p f) v -> p f v", f=PACK)[:, 0, :])
-
-        w2_next = head.tile([P, PACK, NEXT], F32, name="w2_next", offset=W2_NEXT_AT, align_bytes=EDGE)
-        nc.sync.dma_start(out=w2_next[:], in_=w2_rows[:, :, P : P + NEXT])
+        w2_next = head.tile([P, PACK, GPSIMD_COLUMNS], F32, name="w2_next", offset=W2_NEXT_AT, align_bytes=EDGE)
+        nc.sync.dma_start(out=w2_next[:], in_=w2_rows[:, :, P:LATE_START])
 
         warm = keep.tile([P, 8], F32, name="warm")
         warm_out = keep.tile([P, 8], F32, name="warm_out")
@@ -106,8 +108,8 @@ def tile_picked_headmod_gelu_p_kernel(tc, x_words, x_scales, w1, wt, w2, offs, t
         nc.vector.quantize_mx(
             out=w1_codes[:].bitcast(FP8X4), scales=w1_scales[:], in_=w1_grouped[:].rearrange("p t m j -> p (t m j)")
         )
-        w2_raw = head.tile([P, PACK, N - P - NEXT], F32, name="w2_raw", offset=W2_RAW_AT, align_bytes=EDGE)
-        nc.sync.dma_start(out=w2_raw[:], in_=w2_rows[:, :, P + NEXT : N])
+        w2_raw = head.tile([P, PACK, N - LATE_START], F32, name="w2_raw", offset=W2_RAW_AT, align_bytes=EDGE)
+        nc.sync.dma_start(out=w2_raw[:], in_=w2_rows[:, :, LATE_START:N])
 
         xw = order.tile([P, S], U32, name="xw", offset=XW_AT, align_bytes=EDGE)
         for h in range(2):
@@ -132,7 +134,6 @@ def tile_picked_headmod_gelu_p_kernel(tc, x_words, x_scales, w1, wt, w2, offs, t
 
         halves = [slice(0, HALF), slice(HALF, S)]
         quarters = [slice(a, a + QUARTER) for a in range(0, S, QUARTER)]
-        whole = slice(0, S)
         rows = {t: keep.tile([P, S], F32, name=f"rows{t}") for t in (2, 3)}
         gelu_rows = [
             keep.tile([P, S], F32, name="gelu_rows0"),
@@ -140,85 +141,70 @@ def tile_picked_headmod_gelu_p_kernel(tc, x_words, x_scales, w1, wt, w2, offs, t
         ]
         y_passes = [(0, halves[0]), (1, halves[0]), (0, quarters[2]), (0, quarters[3])]
         y_passes += [(1, halves[1]), (2, halves[0]), (2, halves[1]), (3, halves[0])]
-        dense = []
-        late = []
+        y_banks = []
         for bank, (t, cols) in enumerate(y_passes):
-            acc = first_layer(t, cols, bank)
+            y_banks.append(first_layer(t, cols, bank))
             if t < 2:
-                dense.append((t, cols, acc))
-                nc.scalar.activation(gelu_rows[t][:, cols], acc[:], GELU)
-            else:
-                late.append((t, cols, acc))
+                nc.scalar.activation(gelu_rows[t][:, cols], y_banks[bank][:], GELU)
 
         def four_at_a_time(grouped, raw):
             return grouped.rearrange("p (c i) j -> p c j i", i=4), raw.rearrange("p j (c i) -> p c j i", i=4)
 
-        def keep_y(copy, entry):
-            t, cols, acc = entry
-            copy(out=placed[1 - t][:, S + cols.start : S + cols.stop], in_=acc[:])
-
         w2_first = keep.tile([P, P, PACK], BF16, name="w2_first", align_bytes=EDGE)
         nc.vector.tensor_copy(*four_at_a_time(w2_first[:], w2_early))
-        placed = [
-            order.tile([P, 2 * S], F32, name=f"placed{t}", offset=PLACED_AT[t], align_bytes=EDGE) for t in range(2)
+        windows = [
+            order.tile([P, 2 * S], F32, name=f"window{t}", offset=WINDOW_AT[t], align_bytes=EDGE) for t in range(2)
         ]
-        for entry in dense[0:2]:
-            keep_y(nc.vector.tensor_copy, entry)
         for t in range(2):
-            nc.gpsimd.memset(placed[t][:, 0:S], 0.0)
+            nc.vector.tensor_copy(out=windows[1 - t][:, S : S + HALF], in_=y_banks[t][:])
+        for t in range(2):
+            nc.gpsimd.memset(windows[t][:, 0:S], 0.0)
 
         routed = [
             order.tile([P, V], F32, name=f"routed{t}", offset=ROUTED_AT[t], align_bytes=EDGE) for t in range(2)
         ]
         for t in range(2):
             nc.vector.tensor_tensor(routed[t][:], gelu_rows[t][:].indirect(take_t[:]), wt_t[:], MULT)
-        w2_second = order.tile([P, NEXT, PACK], BF16, name="w2_second", offset=W2_SECOND_AT, align_bytes=EDGE)
+        w2_second = order.tile([P, GPSIMD_COLUMNS, PACK], BF16, name="w2_second", offset=W2_SECOND_AT, align_bytes=EDGE)
         nc.gpsimd.tensor_scalar(*four_at_a_time(w2_second[:], w2_next[:]), 1.0, 0.0, MULT, ADD)
         picked = [keep.tile([P, V], F32, name=f"picked{t}") for t in range(2)]
         act = [order.tile([P, V], F32, name=f"act{t}", offset=ACT_AT[t], align_bytes=EDGE) for t in range(2)]
-
-        def keep_row(entry):
-            t, cols, acc = entry
-            nc.scalar.copy(out=rows[t][:, cols], in_=acc[:])
-
-        keep_row(late[0])
-        keep_row(late[1])
-        late.append((3, halves[1], first_layer(3, halves[1], 5)))
+        for bank in (5, 6):
+            nc.scalar.copy(out=rows[2][:, y_passes[bank][1]], in_=y_banks[bank][:])
+        y_last = first_layer(3, halves[1], LATE_BANK)
         nc.scalar.activation(picked[0][:], rows[2][:].indirect(take_t[:]), COPY)
         nc.scalar.activation(act[0][:], picked[0][:], GELU)
-        keep_row(late[2])
-        keep_row(late[3])
+        nc.scalar.copy(out=rows[3][:, halves[0]], in_=y_banks[7][:])
+        nc.scalar.copy(out=rows[3][:, halves[1]], in_=y_last[:])
         nc.scalar.activation(picked[1][:], rows[3][:].indirect(take_t[:]), COPY)
         nc.scalar.activation(act[1][:], picked[1][:], GELU)
         weighted = [
             order.tile([P, V], F32, name=f"weighted{t}", offset=WEIGHTED_AT[t], align_bytes=EDGE) for t in range(2)
         ]
-        summed = [
-            keep.tile([P, V], F32, name="summed0"),
-            keep.tile([P, V], F32, name="summed1"),
-        ]
+        summed = [keep.tile([P, V], F32, name=f"summed{t}") for t in range(2)]
         for t in range(2):
             nc.gpsimd.tensor_tensor(weighted[t][:], act[t][:], wt_t[:], MULT)
             nc.gpsimd.tensor_tensor(summed[t][:], weighted[t][:], picked[t][:], ADD)
 
         z_all = order.tile([P, S, PACK], BF16, name="z_all", offset=Z_AT, align_bytes=EDGE)
         for t in range(2):
-            nc.vector.tensor_copy(placed[t][:].indirect(take_t[:]), routed[t][:])
-            keep_y(nc.scalar.copy, (1 - t, halves[1], first_layer(1 - t, halves[1], 5)))
-        w2_late = order.tile([P, N - P - NEXT, PACK], BF16, name="w2_late", offset=W2_LATE_AT, align_bytes=EDGE)
-        late_pieces = [slice(0, NEXT), slice(NEXT, P + NEXT), slice(P + NEXT, N - P - NEXT)]
+            nc.vector.tensor_copy(windows[t][:].indirect(take_t[:]), routed[t][:])
+            y_again = first_layer(1 - t, halves[1], LATE_BANK)
+            nc.scalar.copy(out=windows[t][:, S + HALF : 2 * S], in_=y_again[:])
+        w2_late = order.tile([P, N - LATE_START, PACK], BF16, name="w2_late", offset=W2_LATE_AT, align_bytes=EDGE)
+        late_cuts = [LATE_START, 2 * P, 3 * P, N]
+        late_pieces = [slice(a - LATE_START, b - LATE_START) for a, b in zip(late_cuts, late_cuts[1:])]
         for cols in late_pieces:
             nc.scalar.copy(*four_at_a_time(w2_late[:, cols, :], w2_raw[:, :, cols]))
 
-        forward = placed[0][:].rearrange("p (t s) -> p t s", t=2)
-        backward = placed[1][:].rearrange("p (t s) -> p t s", t=2)[:, ::-1, :]
-        for cols in [whole]:
-            nc.gpsimd.tensor_tensor(
-                z_all[:, cols, 0:2].rearrange("p (c i) t -> p c t i", i=2),
-                forward[:, :, cols].rearrange("p t (c i) -> p c t i", i=2),
-                backward[:, :, cols].rearrange("p t (c i) -> p c t i", i=2),
-                ADD,
-            )
+        forward = windows[0][:].rearrange("p (t s) -> p t s", t=2)
+        backward = windows[1][:].rearrange("p (t s) -> p t s", t=2)[:, ::-1, :]
+        nc.gpsimd.tensor_tensor(
+            z_all[:, :, 0:2].rearrange("p (c i) t -> p c t i", i=4),
+            forward.rearrange("p t (c i) -> p c t i", i=4),
+            backward.rearrange("p t (c i) -> p c t i", i=4),
+            ADD,
+        )
         nc.vector.tensor_copy(rows[2][:].indirect(take_t[:]), summed[0][:])
         nc.scalar.copy(out=z_all[:, :, 2], in_=rows[2][:])
         nc.vector.tensor_copy(rows[3][:].indirect(take_t[:]), summed[1][:])
@@ -227,7 +213,6 @@ def tile_picked_headmod_gelu_p_kernel(tc, x_words, x_scales, w1, wt, w2, offs, t
 
         w2_codes = order.tile([P, N], U32, name="w2_codes", offset=W2_CODES_AT, align_bytes=EDGE)
         w2_scales = keep.tile([P, N], U8, name="w2_scales", align_bytes=EDGE)
-        w2_blocks = [(w2_codes[:, b * P : (b + 1) * P], w2_scales[:, b * P : (b + 1) * P]) for b in range(PACK)]
 
         def quantize_w2(first, grouped):
             cols = slice(first, first + grouped.shape[1])
@@ -237,18 +222,14 @@ def tile_picked_headmod_gelu_p_kernel(tc, x_words, x_scales, w1, wt, w2, offs, t
                 in_=grouped.rearrange("p c j -> p (c j)"),
             )
 
-        quantize_w2(0, w2_first[:])
-        quantize_w2(P, w2_second[:])
-        quantize_w2(P + NEXT, w2_late[:, 0:NEXT, :])
-
         z_codes = keep.tile([P, S], U32, name="z_codes", align_bytes=EDGE)
         z_scales = keep.tile([P, S], U8, name="z_scales", align_bytes=EDGE)
 
-        def quantize_z(cols, grouped):
+        def quantize_z(cols):
             nc.vector.quantize_mx(
                 out=z_codes[:, cols].bitcast(FP8X4),
                 scales=z_scales[:, cols],
-                in_=grouped.rearrange("p c j -> p (c j)"),
+                in_=z_all[:, cols, :].rearrange("p c j -> p (c j)"),
             )
 
         results = keep.tile([P, PACK, S], F32, name="results")
@@ -256,14 +237,13 @@ def tile_picked_headmod_gelu_p_kernel(tc, x_words, x_scales, w1, wt, w2, offs, t
 
         def product(n, block, passes, on_vector):
             first, last = passes[0].start, passes[-1].stop
-            bank = (len(y_passes) + n) % BANKS
-            acc = psum.tile([P, last - first], F32, name=f"out_acc{n}", tag=f"bank{bank}")
-            block_codes, block_scales = w2_blocks[block]
+            acc = psum.tile([P, last - first], F32, name=f"out_acc{n}", tag=f"bank{n % BANKS}")
+            stat = slice(block * P, (block + 1) * P)
             for cols in passes:
                 nc.tensor.matmul_mx(
                     out=acc[:, cols.start - first : cols.stop - first],
-                    lhsT=block_codes.bitcast(FP8X4),
-                    lhsT_scale=block_scales,
+                    lhsT=w2_codes[:, stat].bitcast(FP8X4),
+                    lhsT_scale=w2_scales[:, stat],
                     rhs=z_codes[:, cols].bitcast(FP8X4),
                     rhs_scale=z_scales[:, cols],
                     start=True,
@@ -277,24 +257,28 @@ def tile_picked_headmod_gelu_p_kernel(tc, x_words, x_scales, w1, wt, w2, offs, t
         def store(block, cols):
             nc.sync.dma_start(out=out_view[:, block, cols], in_=results[:, block, cols])
 
-        quantize_z(quarters[0], z_all[:, quarters[0], :])
-        quantize_w2(2 * P, w2_late[:, NEXT : P + NEXT, :])
-        quantize_z(quarters[1], z_all[:, quarters[1], :])
-        product(0, 0, quarters[0:1], True)
+        quantize_w2(0, w2_first[:])
+        quantize_z(quarters[0])
+        quantize_w2(P, w2_second[:])
+        quantize_w2(late_cuts[0], w2_late[:, late_pieces[0], :])
+        quantize_w2(late_cuts[1], w2_late[:, late_pieces[1], :])
+        quantize_z(quarters[1])
+        quantize_w2(late_cuts[2], w2_late[:, late_pieces[2], :])
+        quantize_z(quarters[2])
+        quantize_z(quarters[3])
+
+        product(0, 0, quarters[0:1], False)
         store(0, quarters[0])
         product(1, 1, quarters[0:1], False)
-        product(2, 2, quarters[0:1], False)
+        product(2, 2, quarters[0:1], True)
         product(3, 1, quarters[1:2], False)
         store(1, halves[0])
         product(4, 2, quarters[1:2], True)
         store(2, halves[0])
-        quantize_w2(3 * P, w2_late[:, P + NEXT : N - P - NEXT, :])
-        quantize_z(quarters[2], z_all[:, quarters[2], :])
-        quantize_z(quarters[3], z_all[:, quarters[3], :])
         product(5, 3, halves[0:1], False)
         store(3, halves[0])
-        product(6, 0, quarters[1:3], False)
-        product(7, 0, quarters[3:4], True)
+        product(6, 0, quarters[1:3], True)
+        product(7, 0, quarters[3:4], False)
         store(0, slice(QUARTER, S))
         for block in range(1, PACK):
             product(7 + block, block, halves[1:2], block % 2 == 0)

@@ -200,9 +200,9 @@ def tile_picked_headmod_gelu_p_kernel(tc, x_words, x_scales, w1, wt, w2, offs, t
         forward = windows[0][:].rearrange("p (t s) -> p t s", t=2)
         backward = windows[1][:].rearrange("p (t s) -> p t s", t=2)[:, ::-1, :]
         nc.gpsimd.tensor_tensor(
-            z_all[:, :, 0:2].rearrange("p (c i) t -> p c t i", i=4),
-            forward.rearrange("p t (c i) -> p c t i", i=4),
-            backward.rearrange("p t (c i) -> p c t i", i=4),
+            z_all[:, :, 0:2].rearrange("p (c i) t -> p c t i", i=8),
+            forward.rearrange("p t (c i) -> p c t i", i=8),
+            backward.rearrange("p t (c i) -> p c t i", i=8),
             ADD,
         )
         nc.vector.tensor_copy(rows[2][:].indirect(take_t[:]), summed[0][:])

@@ -25,31 +25,29 @@ HALF = S // 2
 QUARTER = S // 4
 
 VECTOR_GROUPS = 80
-GPSIMD_COLUMNS = 64
-LATE_START = P + GPSIMD_COLUMNS
+SCALAR_START = 320
 
 ROW = 4 * S
 EDGE = 64
 XS_WIN_AT = ROW
 WT_AT = XS_WIN_AT + ROW // 4
-W2_NEXT_AT = XS_WIN_AT - ROW // 2 + EDGE
 W1_CODES_AT = XS_WIN_AT + ROW - EDGE
 W1_GROUPED_AT = 3 * ROW
 W2_RAW_AT = W1_GROUPED_AT + 2 * ROW - EDGE
 XS_SPREAD_AT = 10 * ROW
-W2_LATE_AT = ROW // 4
-WEIGHTED_AT = (3 * ROW // 2 - EDGE, 3 * ROW)
-ACT_AT = (WEIGHTED_AT[1] + ROW // 2 - EDGE, 4 * ROW + EDGE)
-Z_AT = ACT_AT[1] + ROW // 2 - EDGE
-XW_AT = 7 * ROW
-W2_EARLY_AT = 10 * ROW
-W2_EARLY_BYTES = ROW + 2 * EDGE
-ROUTED_AT = (W2_EARLY_AT + EDGE, W2_EARLY_AT + ROW // 2 + EDGE)
-WINDOW_AT = (W2_EARLY_AT - 2 * ROW + EDGE, W2_EARLY_AT + ROW + EDGE)
-W2_CODES_AT = WINDOW_AT[1]
-GELU_LAST_AT = 14 * ROW
-W2_SECOND_AT = GELU_LAST_AT + ROW - EDGE
-LATE_BANK = 5
+GELU2_AT = ROW
+ZEROS_AT = {3: GELU2_AT - ROW + EDGE, 2: GELU2_AT + ROW - EDGE}
+GELU3_AT = 4 * ROW
+W2_MID_AT = GELU3_AT + ROW - EDGE
+ROUTED2_AT = 7 * ROW
+Z_PAIR_AT = ROUTED2_AT - ROW + EDGE
+W2_LATE_AT = ROUTED2_AT + ROW // 2 - EDGE
+W2_FIRST_AT = 12 * ROW
+W2_FIRST_BYTES = ROW + 2 * EDGE
+ROUTED_AT = (W2_FIRST_AT + EDGE, W2_FIRST_AT + ROW // 2 + EDGE)
+WINDOW_AT = (W2_FIRST_AT - 2 * ROW + EDGE, W2_FIRST_AT + ROW + EDGE)
+W2_CODES_AT = WINDOW_AT[1] + 2 * ROW - EDGE
+OUT_BANKS = (0, 1, 2, 3, 4, 6, 5, 7)
 
 
 def tile_picked_headmod_gelu_p_kernel(tc, x_words, x_scales, w1, wt, w2, offs, take, out):
@@ -85,13 +83,10 @@ def tile_picked_headmod_gelu_p_kernel(tc, x_words, x_scales, w1, wt, w2, offs, t
 
         w2_rows = w2.rearrange("(p j) c -> p j c", j=PACK)
         nc.sync.dma_start(take_t[:], take)
-        w2_early_room = order.tile([P, W2_EARLY_BYTES // 4], F32, name="w2_early", offset=W2_EARLY_AT, align_bytes=EDGE)
-        w2_early = w2_early_room[:, 0 : PACK * P].rearrange("p (j c) -> p j c", j=PACK)
-        nc.sync.dma_start(out=w2_early, in_=w2_rows[:, :, 0:P])
+        w2_early = keep.tile([P, PACK, P], F32, name="w2_early")
+        nc.sync.dma_start(out=w2_early[:], in_=w2_rows[:, :, 0:P])
         wt_t = head.tile([P, V], F32, name="wt_t", offset=WT_AT, align_bytes=EDGE)
         nc.sync.dma_start(out=wt_t[:], in_=wt.rearrange("(p f) v -> p f v", f=PACK)[:, 0, :])
-        w2_next = head.tile([P, PACK, GPSIMD_COLUMNS], F32, name="w2_next", offset=W2_NEXT_AT, align_bytes=EDGE)
-        nc.sync.dma_start(out=w2_next[:], in_=w2_rows[:, :, P:LATE_START])
 
         warm = keep.tile([P, 8], F32, name="warm")
         warm_out = keep.tile([P, 8], F32, name="warm_out")
@@ -108,18 +103,18 @@ def tile_picked_headmod_gelu_p_kernel(tc, x_words, x_scales, w1, wt, w2, offs, t
         nc.vector.quantize_mx(
             out=w1_codes[:].bitcast(FP8X4), scales=w1_scales[:], in_=w1_grouped[:].rearrange("p t m j -> p (t m j)")
         )
-        w2_raw = head.tile([P, PACK, N - LATE_START], F32, name="w2_raw", offset=W2_RAW_AT, align_bytes=EDGE)
-        nc.sync.dma_start(out=w2_raw[:], in_=w2_rows[:, :, LATE_START:N])
+        w2_raw = head.tile([P, PACK, N - P], F32, name="w2_raw", offset=W2_RAW_AT, align_bytes=EDGE)
+        nc.sync.dma_start(out=w2_raw[:], in_=w2_rows[:, :, P:N])
 
-        xw = order.tile([P, S], U32, name="xw", offset=XW_AT, align_bytes=EDGE)
+        xw = keep.tile([P, S], U32, name="xw", align_bytes=EDGE)
         for h in range(2):
             nc.vector.tensor_copy(
                 xw[:, h * HALF : (h + 1) * HALF],
                 xw_win[:].bitcast(U32).indirect(offs_t[:, h * HALF // GROUP : (h + 1) * HALF // GROUP]),
             )
 
-        def first_layer(t, cols, bank):
-            acc = psum.tile([P, cols.stop - cols.start], F32, name=f"y_acc{t}_{cols.start}_{bank}", tag=f"bank{bank}")
+        def first_layer(t, cols, bank, again=0):
+            acc = psum.tile([P, cols.stop - cols.start], F32, name=f"y_acc{t}_{cols.start}_{bank}_{again}", tag=f"bank{bank}")
             stat = slice(t * P, (t + 1) * P)
             nc.tensor.matmul_mx(
                 out=acc[:],
@@ -134,69 +129,69 @@ def tile_picked_headmod_gelu_p_kernel(tc, x_words, x_scales, w1, wt, w2, offs, t
 
         halves = [slice(0, HALF), slice(HALF, S)]
         quarters = [slice(a, a + QUARTER) for a in range(0, S, QUARTER)]
-        rows = {t: keep.tile([P, S], F32, name=f"rows{t}") for t in (2, 3)}
         gelu_rows = [
             keep.tile([P, S], F32, name="gelu_rows0"),
-            order.tile([P, S], F32, name="gelu_rows1", offset=GELU_LAST_AT, align_bytes=EDGE),
+            keep.tile([P, S], F32, name="gelu_rows1"),
+            order.tile([P, S], F32, name="gelu_rows2", offset=GELU2_AT, align_bytes=EDGE),
+            order.tile([P, S], F32, name="gelu_rows3", offset=GELU3_AT, align_bytes=EDGE),
         ]
-        y_passes = [(0, halves[0]), (1, halves[0]), (0, quarters[2]), (0, quarters[3])]
-        y_passes += [(1, halves[1]), (2, halves[0]), (2, halves[1]), (3, halves[0])]
-        y_banks = []
-        for bank, (t, cols) in enumerate(y_passes):
-            y_banks.append(first_layer(t, cols, bank))
-            if t < 2:
-                nc.scalar.activation(gelu_rows[t][:, cols], y_banks[bank][:], GELU)
 
         def four_at_a_time(grouped, raw):
             return grouped.rearrange("p (c i) j -> p c j i", i=4), raw.rearrange("p j (c i) -> p c j i", i=4)
 
-        w2_first = keep.tile([P, P, PACK], BF16, name="w2_first", align_bytes=EDGE)
-        nc.vector.tensor_copy(*four_at_a_time(w2_first[:], w2_early))
+        y_passes = [(0, halves[0]), (1, halves[0]), (0, halves[1]), (1, halves[1])]
+        y_passes += [(t, cols) for t in (2, 3) for cols in halves]
+        y_banks = {}
+
+        def first_layer_gelu(t, cols, bank):
+            y_banks[t, cols.start] = first_layer(t, cols, bank)
+            nc.scalar.activation(gelu_rows[t][:, cols], y_banks[t, cols.start][:], GELU)
+
+        for bank, (t, cols) in enumerate(y_passes):
+            first_layer_gelu(t, cols, bank)
+
+        w2_first_room = order.tile([P, W2_FIRST_BYTES // 2], BF16, name="w2_first", offset=W2_FIRST_AT, align_bytes=EDGE)
+        w2_first = w2_first_room[:, 0 : PACK * P]
+        nc.vector.tensor_copy(*four_at_a_time(w2_first.rearrange("p (c j) -> p c j", j=PACK), w2_early[:]))
+        first_codes = keep.tile([P, P], U32, name="first_codes", align_bytes=EDGE)
+        w2_scales = keep.tile([P, N], U8, name="w2_scales", align_bytes=EDGE)
+        first_scales = keep.tile([P, P], U8, name="first_scales", align_bytes=EDGE)
+        nc.vector.quantize_mx(
+            out=first_codes[:].bitcast(FP8X4), scales=first_scales[:], in_=w2_first
+        )
         windows = [
             order.tile([P, 2 * S], F32, name=f"window{t}", offset=WINDOW_AT[t], align_bytes=EDGE) for t in range(2)
         ]
         for t in range(2):
-            nc.vector.tensor_copy(out=windows[1 - t][:, S : S + HALF], in_=y_banks[t][:])
+            nc.vector.tensor_copy(out=windows[1 - t][:, S : S + HALF], in_=y_banks[t, 0][:])
         for t in range(2):
             nc.gpsimd.memset(windows[t][:, 0:S], 0.0)
 
         routed = [
-            order.tile([P, V], F32, name=f"routed{t}", offset=ROUTED_AT[t], align_bytes=EDGE) for t in range(2)
+            order.tile([P, V], F32, name="routed0", offset=ROUTED_AT[0], align_bytes=EDGE),
+            order.tile([P, V], F32, name="routed1", offset=ROUTED_AT[1], align_bytes=EDGE),
+            order.tile([P, V], F32, name="routed2", offset=ROUTED2_AT, align_bytes=EDGE),
+            keep.tile([P, V], F32, name="routed3"),
         ]
-        for t in range(2):
+        for t in range(PACK):
             nc.vector.tensor_tensor(routed[t][:], gelu_rows[t][:].indirect(take_t[:]), wt_t[:], MULT)
-        w2_second = order.tile([P, GPSIMD_COLUMNS, PACK], BF16, name="w2_second", offset=W2_SECOND_AT, align_bytes=EDGE)
-        nc.gpsimd.tensor_scalar(*four_at_a_time(w2_second[:], w2_next[:]), 1.0, 0.0, MULT, ADD)
-        picked = [keep.tile([P, V], F32, name=f"picked{t}") for t in range(2)]
-        act = [order.tile([P, V], F32, name=f"act{t}", offset=ACT_AT[t], align_bytes=EDGE) for t in range(2)]
-        for bank in (5, 6):
-            nc.scalar.copy(out=rows[2][:, y_passes[bank][1]], in_=y_banks[bank][:])
-        y_last = first_layer(3, halves[1], LATE_BANK)
-        nc.scalar.activation(picked[0][:], rows[2][:].indirect(take_t[:]), COPY)
-        nc.scalar.activation(act[0][:], picked[0][:], GELU)
-        nc.scalar.copy(out=rows[3][:, halves[0]], in_=y_banks[7][:])
-        nc.scalar.copy(out=rows[3][:, halves[1]], in_=y_last[:])
-        nc.scalar.activation(picked[1][:], rows[3][:].indirect(take_t[:]), COPY)
-        nc.scalar.activation(act[1][:], picked[1][:], GELU)
-        weighted = [
-            order.tile([P, V], F32, name=f"weighted{t}", offset=WEIGHTED_AT[t], align_bytes=EDGE) for t in range(2)
-        ]
-        summed = [keep.tile([P, V], F32, name=f"summed{t}") for t in range(2)]
-        for t in range(2):
-            nc.gpsimd.tensor_tensor(weighted[t][:], act[t][:], wt_t[:], MULT)
-            nc.gpsimd.tensor_tensor(summed[t][:], weighted[t][:], picked[t][:], ADD)
 
-        z_all = order.tile([P, S, PACK], BF16, name="z_all", offset=Z_AT, align_bytes=EDGE)
         for t in range(2):
-            nc.vector.tensor_copy(windows[t][:].indirect(take_t[:]), routed[t][:])
-            y_again = first_layer(1 - t, halves[1], LATE_BANK)
-            nc.scalar.copy(out=windows[t][:, S + HALF : 2 * S], in_=y_again[:])
-        w2_late = order.tile([P, N - LATE_START, PACK], BF16, name="w2_late", offset=W2_LATE_AT, align_bytes=EDGE)
-        late_cuts = [LATE_START, 2 * P, 3 * P, N]
-        late_pieces = [slice(a - LATE_START, b - LATE_START) for a, b in zip(late_cuts, late_cuts[1:])]
-        for cols in late_pieces:
-            nc.scalar.copy(*four_at_a_time(w2_late[:, cols, :], w2_raw[:, :, cols]))
+            y_again = first_layer(t, halves[1], t, 1)
+            nc.scalar.copy(out=windows[1 - t][:, S + HALF : 2 * S], in_=y_again[:])
+        zeros = {t: order.tile([P, S], F32, name=f"zeros{t}", offset=ZEROS_AT[t], align_bytes=EDGE) for t in (3, 2)}
+        for t in (3, 2):
+            nc.gpsimd.memset(zeros[t][:], 0.0)
+        w2_mid = order.tile([P, SCALAR_START - P, PACK], BF16, name="w2_mid", offset=W2_MID_AT, align_bytes=EDGE)
+        mid_rows = w2_raw[:, :, 0 : SCALAR_START - P].rearrange("p j c -> p c j")
+        nc.gpsimd.tensor_scalar(w2_mid[:], mid_rows, 1.0, 0.0, MULT, ADD)
 
+        nc.scalar.activation(windows[0][:].indirect(take_t[:]), routed[0][:], COPY)
+        nc.vector.tensor_copy(windows[1][:].indirect(take_t[:]), routed[1][:])
+        nc.scalar.activation(zeros[2][:].indirect(take_t[:]), routed[2][:], COPY)
+        nc.vector.tensor_copy(zeros[3][:].indirect(take_t[:]), routed[3][:])
+
+        z_all = keep.tile([P, S, PACK], BF16, name="z_all", align_bytes=EDGE)
         forward = windows[0][:].rearrange("p (t s) -> p t s", t=2)
         backward = windows[1][:].rearrange("p (t s) -> p t s", t=2)[:, ::-1, :]
         nc.gpsimd.tensor_tensor(
@@ -205,20 +200,24 @@ def tile_picked_headmod_gelu_p_kernel(tc, x_words, x_scales, w1, wt, w2, offs, t
             backward.rearrange("p t (c i) -> p c t i", i=8),
             ADD,
         )
-        nc.vector.tensor_copy(rows[2][:].indirect(take_t[:]), summed[0][:])
-        nc.scalar.copy(out=z_all[:, :, 2], in_=rows[2][:])
-        nc.vector.tensor_copy(rows[3][:].indirect(take_t[:]), summed[1][:])
-        for cols in quarters:
-            nc.scalar.copy(out=z_all[:, cols, 3], in_=rows[3][:, cols])
+        w2_late = order.tile([P, N - SCALAR_START, PACK], BF16, name="w2_late", offset=W2_LATE_AT, align_bytes=EDGE)
+        nc.scalar.copy(*four_at_a_time(w2_late[:], w2_raw[:, :, SCALAR_START - P : N - P]))
 
-        w2_codes = order.tile([P, N], U32, name="w2_codes", offset=W2_CODES_AT, align_bytes=EDGE)
-        w2_scales = keep.tile([P, N], U8, name="w2_scales", align_bytes=EDGE)
+        z_pair = order.tile([P, 2, S], BF16, name="z_pair", offset=Z_PAIR_AT, align_bytes=EDGE)
+        for t, cols in ((2, halves[0]), (3, quarters[0]), (3, quarters[1]), (2, halves[1]), (3, halves[1])):
+            first = cols.start // HALF * HALF
+            y_part = y_banks[t, first][:, cols.start - first : cols.stop - first]
+            nc.vector.tensor_tensor(z_pair[:, t - 2, cols], zeros[t][:, cols], y_part, ADD)
+        for cols in quarters:
+            nc.scalar.copy(out=z_all[:, cols, 2:4], in_=z_pair[:, :, cols].rearrange("p t s -> p s t"))
+
+        w2_codes = order.tile([P, N - P], U32, name="w2_codes", offset=W2_CODES_AT, align_bytes=EDGE)
 
         def quantize_w2(first, grouped):
-            cols = slice(first, first + grouped.shape[1])
+            last = first + grouped.shape[1]
             nc.vector.quantize_mx(
-                out=w2_codes[:, cols].bitcast(FP8X4),
-                scales=w2_scales[:, cols],
+                out=w2_codes[:, first - P : last - P].bitcast(FP8X4),
+                scales=w2_scales[:, first:last],
                 in_=grouped.rearrange("p c j -> p (c j)"),
             )
 
@@ -237,13 +236,14 @@ def tile_picked_headmod_gelu_p_kernel(tc, x_words, x_scales, w1, wt, w2, offs, t
 
         def product(n, block, passes, on_vector):
             first, last = passes[0].start, passes[-1].stop
-            acc = psum.tile([P, last - first], F32, name=f"out_acc{n}", tag=f"bank{n % BANKS}")
-            stat = slice(block * P, (block + 1) * P)
+            acc = psum.tile([P, last - first], F32, name=f"out_acc{n}", tag=f"bank{OUT_BANKS[n % BANKS]}")
+            codes = w2_codes[:, (block - 1) * P : block * P] if block else first_codes[:]
+            scales = w2_scales[:, block * P : (block + 1) * P] if block else first_scales[:]
             for cols in passes:
                 nc.tensor.matmul_mx(
                     out=acc[:, cols.start - first : cols.stop - first],
-                    lhsT=w2_codes[:, stat].bitcast(FP8X4),
-                    lhsT_scale=w2_scales[:, stat],
+                    lhsT=codes.bitcast(FP8X4),
+                    lhsT_scale=scales,
                     rhs=z_codes[:, cols].bitcast(FP8X4),
                     rhs_scale=z_scales[:, cols],
                     start=True,
@@ -257,13 +257,12 @@ def tile_picked_headmod_gelu_p_kernel(tc, x_words, x_scales, w1, wt, w2, offs, t
         def store(block, cols):
             nc.sync.dma_start(out=out_view[:, block, cols], in_=results[:, block, cols])
 
-        quantize_w2(0, w2_first[:])
         quantize_z(quarters[0])
-        quantize_w2(P, w2_second[:])
-        quantize_w2(late_cuts[0], w2_late[:, late_pieces[0], :])
-        quantize_w2(late_cuts[1], w2_late[:, late_pieces[1], :])
+        quantize_w2(P, w2_mid[:, 0:P, :])
+        quantize_w2(2 * P, w2_mid[:, P:, :])
+        quantize_w2(SCALAR_START, w2_late[:, 0 : 3 * P - SCALAR_START, :])
         quantize_z(quarters[1])
-        quantize_w2(late_cuts[2], w2_late[:, late_pieces[2], :])
+        quantize_w2(3 * P, w2_late[:, 3 * P - SCALAR_START :, :])
         quantize_z(quarters[2])
         quantize_z(quarters[3])
 

@@ -25,7 +25,7 @@ HALF = S // 2
 QUARTER = S // 4
 
 VECTOR_GROUPS = 80
-SCALAR_START = 320
+SCALAR_START = 256
 
 ROW = 4 * S
 EDGE = 64
@@ -36,7 +36,7 @@ W1_GROUPED_AT = 3 * ROW
 W2_RAW_AT = W1_GROUPED_AT + 2 * ROW - EDGE
 XS_SPREAD_AT = 10 * ROW
 GELU2_AT = ROW
-ZEROS_AT = {3: GELU2_AT - ROW + EDGE, 2: GELU2_AT + ROW - EDGE}
+ZEROS2_AT = GELU2_AT - ROW + EDGE
 GELU3_AT = 4 * ROW
 W2_MID_AT = GELU3_AT + ROW - EDGE
 ROUTED2_AT = 7 * ROW
@@ -46,7 +46,9 @@ W2_FIRST_AT = 12 * ROW
 W2_FIRST_BYTES = ROW + 2 * EDGE
 ROUTED_AT = (W2_FIRST_AT + EDGE, W2_FIRST_AT + ROW // 2 + EDGE)
 WINDOW_AT = (W2_FIRST_AT - 2 * ROW + EDGE, W2_FIRST_AT + ROW + EDGE)
-W2_CODES_AT = WINDOW_AT[1] + 2 * ROW - EDGE
+Z_FIRST_AT = 17 * ROW
+Z_LAST_AT = Z_FIRST_AT - ROW // 2 + EDGE
+W2_CODES_AT = Z_FIRST_AT + ROW // 2 - EDGE
 OUT_BANKS = (0, 1, 2, 3, 4, 6, 5, 7)
 
 
@@ -87,6 +89,9 @@ def tile_picked_headmod_gelu_p_kernel(tc, x_words, x_scales, w1, wt, w2, offs, t
         nc.sync.dma_start(out=w2_early[:], in_=w2_rows[:, :, 0:P])
         wt_t = head.tile([P, V], F32, name="wt_t", offset=WT_AT, align_bytes=EDGE)
         nc.sync.dma_start(out=wt_t[:], in_=wt.rearrange("(p f) v -> p f v", f=PACK)[:, 0, :])
+
+        zeros = {3: keep.tile([P, S], F32, name="zeros3")}
+        nc.vector.memset(zeros[3][:], 0.0)
 
         warm = keep.tile([P, 8], F32, name="warm")
         warm_out = keep.tile([P, 8], F32, name="warm_out")
@@ -179,27 +184,32 @@ def tile_picked_headmod_gelu_p_kernel(tc, x_words, x_scales, w1, wt, w2, offs, t
         for t in range(2):
             y_again = first_layer(t, halves[1], t, 1)
             nc.scalar.copy(out=windows[1 - t][:, S + HALF : 2 * S], in_=y_again[:])
-        zeros = {t: order.tile([P, S], F32, name=f"zeros{t}", offset=ZEROS_AT[t], align_bytes=EDGE) for t in (3, 2)}
-        for t in (3, 2):
-            nc.gpsimd.memset(zeros[t][:], 0.0)
+        zeros[2] = order.tile([P, S], F32, name="zeros2", offset=ZEROS2_AT, align_bytes=EDGE)
+        nc.gpsimd.memset(zeros[2][:], 0.0)
         w2_mid = order.tile([P, SCALAR_START - P, PACK], BF16, name="w2_mid", offset=W2_MID_AT, align_bytes=EDGE)
-        mid_rows = w2_raw[:, :, 0 : SCALAR_START - P].rearrange("p j c -> p c j")
-        nc.gpsimd.tensor_scalar(w2_mid[:], mid_rows, 1.0, 0.0, MULT, ADD)
+        nc.gpsimd.tensor_scalar(*four_at_a_time(w2_mid[:], w2_raw[:, :, 0 : SCALAR_START - P]), 1.0, 0.0, MULT, ADD)
 
         nc.scalar.activation(windows[0][:].indirect(take_t[:]), routed[0][:], COPY)
         nc.vector.tensor_copy(windows[1][:].indirect(take_t[:]), routed[1][:])
         nc.scalar.activation(zeros[2][:].indirect(take_t[:]), routed[2][:], COPY)
         nc.vector.tensor_copy(zeros[3][:].indirect(take_t[:]), routed[3][:])
 
-        z_all = keep.tile([P, S, PACK], BF16, name="z_all", align_bytes=EDGE)
+        z_first = order.tile([P, QUARTER, PACK], BF16, name="z_first", offset=Z_FIRST_AT, align_bytes=EDGE)
+        z_mid = keep.tile([P, HALF, PACK], BF16, name="z_mid", align_bytes=EDGE)
+        z_last = order.tile([P, QUARTER, PACK], BF16, name="z_last", offset=Z_LAST_AT, align_bytes=EDGE)
+        z_parts = [z_first[:], z_mid[:, 0:QUARTER, :], z_mid[:, QUARTER:HALF, :], z_last[:]]
         forward = windows[0][:].rearrange("p (t s) -> p t s", t=2)
         backward = windows[1][:].rearrange("p (t s) -> p t s", t=2)[:, ::-1, :]
-        nc.gpsimd.tensor_tensor(
-            z_all[:, :, 0:2].rearrange("p (c i) t -> p c t i", i=8),
-            forward.rearrange("p t (c i) -> p c t i", i=8),
-            backward.rearrange("p t (c i) -> p c t i", i=8),
-            ADD,
-        )
+
+        def pair_sum(engine, z_part, cols):
+            engine.tensor_tensor(
+                z_part[:, :, 0:2].rearrange("p (c i) t -> p c t i", i=8),
+                forward[:, :, cols].rearrange("p t (c i) -> p c t i", i=8),
+                backward[:, :, cols].rearrange("p t (c i) -> p c t i", i=8),
+                ADD,
+            )
+
+        pair_sum(nc.gpsimd, z_mid[:], slice(QUARTER, S - QUARTER))
         w2_late = order.tile([P, N - SCALAR_START, PACK], BF16, name="w2_late", offset=W2_LATE_AT, align_bytes=EDGE)
         nc.scalar.copy(*four_at_a_time(w2_late[:], w2_raw[:, :, SCALAR_START - P : N - P]))
 
@@ -208,10 +218,22 @@ def tile_picked_headmod_gelu_p_kernel(tc, x_words, x_scales, w1, wt, w2, offs, t
             first = cols.start // HALF * HALF
             y_part = y_banks[t, first][:, cols.start - first : cols.stop - first]
             nc.vector.tensor_tensor(z_pair[:, t - 2, cols], zeros[t][:, cols], y_part, ADD)
-        for cols in quarters:
-            nc.scalar.copy(out=z_all[:, cols, 2:4], in_=z_pair[:, :, cols].rearrange("p t s -> p s t"))
 
-        w2_codes = order.tile([P, N - P], U32, name="w2_codes", offset=W2_CODES_AT, align_bytes=EDGE)
+        def interleave_pair(q):
+            nc.scalar.copy(out=z_parts[q][:, :, 2:4], in_=z_pair[:, :, quarters[q]].rearrange("p t s -> p s t"))
+
+        for q in range(3):
+            interleave_pair(q)
+        pair_sum(nc.gpsimd, z_first[:], quarters[0])
+
+        late_codes = order.tile([P, N - P + S - QUARTER], U32, name="late_codes", offset=W2_CODES_AT, align_bytes=EDGE)
+        w2_codes = late_codes[:, 0 : N - P]
+        z_first_codes = keep.tile([P, QUARTER], U32, name="z_first_codes", align_bytes=EDGE)
+
+        def z_codes(cols):
+            if cols.start == 0:
+                return z_first_codes[:]
+            return late_codes[:, N - P - QUARTER + cols.start : N - P - QUARTER + cols.stop]
 
         def quantize_w2(first, grouped):
             last = first + grouped.shape[1]
@@ -221,14 +243,13 @@ def tile_picked_headmod_gelu_p_kernel(tc, x_words, x_scales, w1, wt, w2, offs, t
                 in_=grouped.rearrange("p c j -> p (c j)"),
             )
 
-        z_codes = keep.tile([P, S], U32, name="z_codes", align_bytes=EDGE)
         z_scales = keep.tile([P, S], U8, name="z_scales", align_bytes=EDGE)
 
-        def quantize_z(cols):
+        def quantize_z(q):
             nc.vector.quantize_mx(
-                out=z_codes[:, cols].bitcast(FP8X4),
-                scales=z_scales[:, cols],
-                in_=z_all[:, cols, :].rearrange("p c j -> p (c j)"),
+                out=z_codes(quarters[q]).bitcast(FP8X4),
+                scales=z_scales[:, quarters[q]],
+                in_=z_parts[q].rearrange("p c j -> p (c j)"),
             )
 
         results = keep.tile([P, PACK, S], F32, name="results")
@@ -244,7 +265,7 @@ def tile_picked_headmod_gelu_p_kernel(tc, x_words, x_scales, w1, wt, w2, offs, t
                     out=acc[:, cols.start - first : cols.stop - first],
                     lhsT=codes.bitcast(FP8X4),
                     lhsT_scale=scales,
-                    rhs=z_codes[:, cols].bitcast(FP8X4),
+                    rhs=z_codes(cols).bitcast(FP8X4),
                     rhs_scale=z_scales[:, cols],
                     start=True,
                     stop=True,
@@ -257,14 +278,15 @@ def tile_picked_headmod_gelu_p_kernel(tc, x_words, x_scales, w1, wt, w2, offs, t
         def store(block, cols):
             nc.sync.dma_start(out=out_view[:, block, cols], in_=results[:, block, cols])
 
-        quantize_z(quarters[0])
-        quantize_w2(P, w2_mid[:, 0:P, :])
-        quantize_w2(2 * P, w2_mid[:, P:, :])
-        quantize_w2(SCALAR_START, w2_late[:, 0 : 3 * P - SCALAR_START, :])
-        quantize_z(quarters[1])
-        quantize_w2(3 * P, w2_late[:, 3 * P - SCALAR_START :, :])
-        quantize_z(quarters[2])
-        quantize_z(quarters[3])
+        quantize_z(0)
+        interleave_pair(3)
+        quantize_w2(P, w2_mid[:])
+        quantize_w2(2 * P, w2_late[:, 0:P, :])
+        quantize_z(1)
+        quantize_w2(3 * P, w2_late[:, P:, :])
+        pair_sum(nc.vector, z_last[:], quarters[3])
+        quantize_z(2)
+        quantize_z(3)
 
         product(0, 0, quarters[0:1], False)
         store(0, quarters[0])
@@ -274,7 +296,7 @@ def tile_picked_headmod_gelu_p_kernel(tc, x_words, x_scales, w1, wt, w2, offs, t
         store(1, halves[0])
         product(4, 2, quarters[1:2], True)
         store(2, halves[0])
-        product(5, 3, halves[0:1], False)
+        product(5, 3, quarters[0:2], False)
         store(3, halves[0])
         product(6, 0, quarters[1:3], True)
         product(7, 0, quarters[3:4], False)

@@ -35,21 +35,19 @@ W1_CODES_AT = XS_WIN_AT + ROW - EDGE
 W1_GROUPED_AT = 3 * ROW
 W2_RAW_AT = W1_GROUPED_AT + 2 * ROW - EDGE
 XS_SPREAD_AT = 10 * ROW
-GELU2_AT = ROW
-ZEROS2_AT = GELU2_AT - ROW + EDGE
-GELU3_AT = 4 * ROW
+GELU3_AT = ROW
 W2_MID_AT = GELU3_AT + ROW - EDGE
-ROUTED2_AT = 7 * ROW
-Z_PAIR_AT = ROUTED2_AT - ROW + EDGE
-W2_LATE_AT = ROUTED2_AT + ROW // 2 - EDGE
-W2_FIRST_AT = 12 * ROW
+W2_LATE_AT = GELU3_AT - ROW + EDGE
+ROUTED_LATE_AT = (4 * ROW, 5 * ROW + ROW // 2 - 2 * EDGE)
+Z_ROWS_LATE_AT = ROUTED_LATE_AT[0] + ROW // 2 - EDGE
+W2_FIRST_AT = 8 * ROW
 W2_FIRST_BYTES = ROW + 2 * EDGE
 ROUTED_AT = (W2_FIRST_AT + EDGE, W2_FIRST_AT + ROW // 2 + EDGE)
-WINDOW_AT = (W2_FIRST_AT - 2 * ROW + EDGE, W2_FIRST_AT + ROW + EDGE)
-Z_FIRST_AT = 17 * ROW
-Z_LAST_AT = Z_FIRST_AT - ROW // 2 + EDGE
-W2_CODES_AT = Z_FIRST_AT + ROW // 2 - EDGE
-OUT_BANKS = (0, 1, 2, 3, 4, 6, 5, 7)
+Y_ROWS_AT = W2_FIRST_AT - ROW + EDGE
+Z_FIRST_AT = 12 * ROW
+LATE_CODES_AT = Z_FIRST_AT + ROW // 2 - EDGE
+OUT_BANKS = (0, 1, 6, 4, 7, 5, 2, 3)
+SCALAR_ENTRIES = 96
 
 
 def tile_picked_headmod_gelu_p_kernel(tc, x_words, x_scales, w1, wt, w2, offs, take, out):
@@ -90,8 +88,9 @@ def tile_picked_headmod_gelu_p_kernel(tc, x_words, x_scales, w1, wt, w2, offs, t
         wt_t = head.tile([P, V], F32, name="wt_t", offset=WT_AT, align_bytes=EDGE)
         nc.sync.dma_start(out=wt_t[:], in_=wt.rearrange("(p f) v -> p f v", f=PACK)[:, 0, :])
 
-        zeros = {3: keep.tile([P, S], F32, name="zeros3")}
-        nc.vector.memset(zeros[3][:], 0.0)
+        windows = [keep.tile([P, S], F32, name=f"window{t}") for t in range(PACK)]
+        for window in windows:
+            nc.vector.memset(window[:], 0.0)
 
         warm = keep.tile([P, 8], F32, name="warm")
         warm_out = keep.tile([P, 8], F32, name="warm_out")
@@ -137,7 +136,7 @@ def tile_picked_headmod_gelu_p_kernel(tc, x_words, x_scales, w1, wt, w2, offs, t
         gelu_rows = [
             keep.tile([P, S], F32, name="gelu_rows0"),
             keep.tile([P, S], F32, name="gelu_rows1"),
-            order.tile([P, S], F32, name="gelu_rows2", offset=GELU2_AT, align_bytes=EDGE),
+            keep.tile([P, S], F32, name="gelu_rows2"),
             order.tile([P, S], F32, name="gelu_rows3", offset=GELU3_AT, align_bytes=EDGE),
         ]
 
@@ -164,69 +163,54 @@ def tile_picked_headmod_gelu_p_kernel(tc, x_words, x_scales, w1, wt, w2, offs, t
         nc.vector.quantize_mx(
             out=first_codes[:].bitcast(FP8X4), scales=first_scales[:], in_=w2_first
         )
-        windows = [
-            order.tile([P, 2 * S], F32, name=f"window{t}", offset=WINDOW_AT[t], align_bytes=EDGE) for t in range(2)
-        ]
+        y_rows = order.tile([P, 2, HALF], F32, name="y_rows", offset=Y_ROWS_AT, align_bytes=EDGE)
         for t in range(2):
-            nc.vector.tensor_copy(out=windows[1 - t][:, S : S + HALF], in_=y_banks[t, 0][:])
-        for t in range(2):
-            nc.gpsimd.memset(windows[t][:, 0:S], 0.0)
+            nc.vector.tensor_copy(out=y_rows[:, t, :], in_=y_banks[t, 0][:])
 
         routed = [
-            order.tile([P, V], F32, name="routed0", offset=ROUTED_AT[0], align_bytes=EDGE),
-            order.tile([P, V], F32, name="routed1", offset=ROUTED_AT[1], align_bytes=EDGE),
-            order.tile([P, V], F32, name="routed2", offset=ROUTED2_AT, align_bytes=EDGE),
-            keep.tile([P, V], F32, name="routed3"),
+            order.tile([P, V], F32, name=f"routed{t}", offset=at, align_bytes=EDGE)
+            for t, at in enumerate(ROUTED_AT + ROUTED_LATE_AT)
         ]
         for t in range(PACK):
             nc.vector.tensor_tensor(routed[t][:], gelu_rows[t][:].indirect(take_t[:]), wt_t[:], MULT)
 
-        for t in range(2):
-            y_again = first_layer(t, halves[1], t, 1)
-            nc.scalar.copy(out=windows[1 - t][:, S + HALF : 2 * S], in_=y_again[:])
-        zeros[2] = order.tile([P, S], F32, name="zeros2", offset=ZEROS2_AT, align_bytes=EDGE)
-        nc.gpsimd.memset(zeros[2][:], 0.0)
         w2_mid = order.tile([P, SCALAR_START - P, PACK], BF16, name="w2_mid", offset=W2_MID_AT, align_bytes=EDGE)
-        nc.gpsimd.tensor_scalar(*four_at_a_time(w2_mid[:], w2_raw[:, :, 0 : SCALAR_START - P]), 1.0, 0.0, MULT, ADD)
+        mid_rows = w2_raw[:, :, 0 : SCALAR_START - P].rearrange("p j c -> p c j")
+        nc.gpsimd.tensor_scalar(w2_mid[:], mid_rows, 1.0, 0.0, MULT, ADD)
 
+        cut = SCALAR_ENTRIES // GROUP
         nc.scalar.activation(windows[0][:].indirect(take_t[:]), routed[0][:], COPY)
         nc.vector.tensor_copy(windows[1][:].indirect(take_t[:]), routed[1][:])
-        nc.scalar.activation(zeros[2][:].indirect(take_t[:]), routed[2][:], COPY)
-        nc.vector.tensor_copy(zeros[3][:].indirect(take_t[:]), routed[3][:])
+        nc.scalar.activation(windows[2][:].indirect(take_t[:, 0:cut]), routed[2][:, 0:SCALAR_ENTRIES], COPY)
+        nc.vector.tensor_copy(windows[2][:].indirect(take_t[:, cut:]), routed[2][:, SCALAR_ENTRIES:V])
+        nc.scalar.activation(windows[3][:].indirect(take_t[:]), routed[3][:], COPY)
 
-        z_first = order.tile([P, QUARTER, PACK], BF16, name="z_first", offset=Z_FIRST_AT, align_bytes=EDGE)
-        z_mid = keep.tile([P, HALF, PACK], BF16, name="z_mid", align_bytes=EDGE)
-        z_last = order.tile([P, QUARTER, PACK], BF16, name="z_last", offset=Z_LAST_AT, align_bytes=EDGE)
-        z_parts = [z_first[:], z_mid[:, 0:QUARTER, :], z_mid[:, QUARTER:HALF, :], z_last[:]]
-        forward = windows[0][:].rearrange("p (t s) -> p t s", t=2)
-        backward = windows[1][:].rearrange("p (t s) -> p t s", t=2)[:, ::-1, :]
-
-        def pair_sum(engine, z_part, cols):
-            engine.tensor_tensor(
-                z_part[:, :, 0:2].rearrange("p (c i) t -> p c t i", i=8),
-                forward[:, :, cols].rearrange("p t (c i) -> p c t i", i=8),
-                backward[:, :, cols].rearrange("p t (c i) -> p c t i", i=8),
-                ADD,
-            )
-
-        pair_sum(nc.gpsimd, z_mid[:], slice(QUARTER, S - QUARTER))
         w2_late = order.tile([P, N - SCALAR_START, PACK], BF16, name="w2_late", offset=W2_LATE_AT, align_bytes=EDGE)
         nc.scalar.copy(*four_at_a_time(w2_late[:], w2_raw[:, :, SCALAR_START - P : N - P]))
 
-        z_pair = order.tile([P, 2, S], BF16, name="z_pair", offset=Z_PAIR_AT, align_bytes=EDGE)
-        for t, cols in ((2, halves[0]), (3, quarters[0]), (3, quarters[1]), (2, halves[1]), (3, halves[1])):
-            first = cols.start // HALF * HALF
-            y_part = y_banks[t, first][:, cols.start - first : cols.stop - first]
-            nc.vector.tensor_tensor(z_pair[:, t - 2, cols], zeros[t][:, cols], y_part, ADD)
+        z_rows = [
+            keep.tile([P, PACK, HALF], BF16, name="z_rows0"),
+            order.tile([P, PACK, HALF], BF16, name="z_rows1", offset=Z_ROWS_LATE_AT, align_bytes=EDGE),
+        ]
+        for t in range(2):
+            nc.gpsimd.tensor_tensor(z_rows[0][:, t, :], windows[t][:, halves[0]], y_rows[:, t, :], ADD)
+        sums = [(3, halves[0]), (2, quarters[0]), (2, quarters[1])] + [(t, halves[1]) for t in range(PACK)]
+        for t, cols in sums:
+            h = cols.start // HALF
+            part = slice(cols.start - h * HALF, cols.stop - h * HALF)
+            nc.vector.tensor_tensor(z_rows[h][:, t, part], windows[t][:, cols], y_banks[t, h * HALF][:, part], ADD)
 
-        def interleave_pair(q):
-            nc.scalar.copy(out=z_parts[q][:, :, 2:4], in_=z_pair[:, :, quarters[q]].rearrange("p t s -> p s t"))
+        z_first = order.tile([P, QUARTER, PACK], BF16, name="z_first", offset=Z_FIRST_AT, align_bytes=EDGE)
+        z_rest = keep.tile([P, S - QUARTER, PACK], BF16, name="z_rest", align_bytes=EDGE)
+        z_parts = [z_first[:]] + [z_rest[:, a : a + QUARTER, :] for a in range(0, S - QUARTER, QUARTER)]
 
-        for q in range(3):
-            interleave_pair(q)
-        pair_sum(nc.gpsimd, z_first[:], quarters[0])
+        def interleave_z(q, copy):
+            copy(*four_at_a_time(z_parts[q], z_rows[q // 2][:, :, q % 2 * QUARTER : (q % 2 + 1) * QUARTER]))
 
-        late_codes = order.tile([P, N - P + S - QUARTER], U32, name="late_codes", offset=W2_CODES_AT, align_bytes=EDGE)
+        for q in (0, 1, 3):
+            interleave_z(q, nc.scalar.copy)
+
+        late_codes = order.tile([P, N - P + S - QUARTER], U32, name="late_codes", offset=LATE_CODES_AT, align_bytes=EDGE)
         w2_codes = late_codes[:, 0 : N - P]
         z_first_codes = keep.tile([P, QUARTER], U32, name="z_first_codes", align_bytes=EDGE)
 
@@ -279,12 +263,11 @@ def tile_picked_headmod_gelu_p_kernel(tc, x_words, x_scales, w1, wt, w2, offs, t
             nc.sync.dma_start(out=out_view[:, block, cols], in_=results[:, block, cols])
 
         quantize_z(0)
-        interleave_pair(3)
         quantize_w2(P, w2_mid[:])
         quantize_w2(2 * P, w2_late[:, 0:P, :])
+        interleave_z(2, nc.vector.tensor_copy)
         quantize_z(1)
         quantize_w2(3 * P, w2_late[:, P:, :])
-        pair_sum(nc.vector, z_last[:], quarters[3])
         quantize_z(2)
         quantize_z(3)
 

@@ -40,6 +40,7 @@ W2_MID_AT = GELU3_AT + ROW - EDGE
 W2_LATE_AT = GELU3_AT - ROW + EDGE
 ROUTED_LATE_AT = (4 * ROW, 5 * ROW + ROW // 2 - 2 * EDGE)
 Z_ROWS_LATE_AT = ROUTED_LATE_AT[0] + ROW // 2 - EDGE
+FIRST_CODES_AT = ROUTED_LATE_AT[1] + ROW // 2 - EDGE
 W2_FIRST_AT = 8 * ROW
 W2_FIRST_BYTES = ROW + 2 * EDGE
 ROUTED_AT = (W2_FIRST_AT + EDGE, W2_FIRST_AT + ROW // 2 + EDGE)
@@ -83,8 +84,9 @@ def tile_picked_headmod_gelu_p_kernel(tc, x_words, x_scales, w1, wt, w2, offs, t
 
         w2_rows = w2.rearrange("(p j) c -> p j c", j=PACK)
         nc.sync.dma_start(take_t[:], take)
-        w2_early = keep.tile([P, PACK, P], F32, name="w2_early")
-        nc.sync.dma_start(out=w2_early[:], in_=w2_rows[:, :, 0:P])
+        w2_early_room = order.tile([P, W2_FIRST_BYTES // 4], F32, name="w2_early", offset=W2_FIRST_AT, align_bytes=EDGE)
+        w2_early = w2_early_room[:, 0 : PACK * P].rearrange("p (j c) -> p j c", j=PACK)
+        nc.sync.dma_start(out=w2_early, in_=w2_rows[:, :, 0:P])
         wt_t = head.tile([P, V], F32, name="wt_t", offset=WT_AT, align_bytes=EDGE)
         nc.sync.dma_start(out=wt_t[:], in_=wt.rearrange("(p f) v -> p f v", f=PACK)[:, 0, :])
 
@@ -154,15 +156,10 @@ def tile_picked_headmod_gelu_p_kernel(tc, x_words, x_scales, w1, wt, w2, offs, t
         for bank, (t, cols) in enumerate(y_passes):
             first_layer_gelu(t, cols, bank)
 
-        w2_first_room = order.tile([P, W2_FIRST_BYTES // 2], BF16, name="w2_first", offset=W2_FIRST_AT, align_bytes=EDGE)
-        w2_first = w2_first_room[:, 0 : PACK * P]
-        nc.vector.tensor_copy(*four_at_a_time(w2_first.rearrange("p (c j) -> p c j", j=PACK), w2_early[:]))
-        first_codes = keep.tile([P, P], U32, name="first_codes", align_bytes=EDGE)
+        w2_first = keep.tile([P, P, PACK], BF16, name="w2_first", align_bytes=EDGE)
+        nc.vector.tensor_copy(*four_at_a_time(w2_first[:], w2_early))
         w2_scales = keep.tile([P, N], U8, name="w2_scales", align_bytes=EDGE)
         first_scales = keep.tile([P, P], U8, name="first_scales", align_bytes=EDGE)
-        nc.vector.quantize_mx(
-            out=first_codes[:].bitcast(FP8X4), scales=first_scales[:], in_=w2_first
-        )
         y_rows = order.tile([P, 2, HALF], F32, name="y_rows", offset=Y_ROWS_AT, align_bytes=EDGE)
         for t in range(2):
             nc.vector.tensor_copy(out=y_rows[:, t, :], in_=y_banks[t, 0][:])
@@ -262,6 +259,10 @@ def tile_picked_headmod_gelu_p_kernel(tc, x_words, x_scales, w1, wt, w2, offs, t
         def store(block, cols):
             nc.sync.dma_start(out=out_view[:, block, cols], in_=results[:, block, cols])
 
+        first_codes = order.tile([P, P], U32, name="first_codes", offset=FIRST_CODES_AT, align_bytes=EDGE)
+        nc.vector.quantize_mx(
+            out=first_codes[:].bitcast(FP8X4), scales=first_scales[:], in_=w2_first[:].rearrange("p c j -> p (c j)")
+        )
         quantize_z(0)
         quantize_w2(P, w2_mid[:])
         quantize_w2(2 * P, w2_late[:, 0:P, :])

@@ -39,15 +39,16 @@ GELU3_AT = ROW
 W2_MID_AT = GELU3_AT + ROW - EDGE
 W2_LATE_AT = GELU3_AT - ROW + EDGE
 ROUTED_LATE_AT = (4 * ROW, 5 * ROW + ROW // 2 - 2 * EDGE)
-Z_ROWS_LATE_AT = ROUTED_LATE_AT[0] + ROW // 2 - EDGE
 FIRST_CODES_AT = ROUTED_LATE_AT[1] + ROW // 2 - EDGE
 W2_FIRST_AT = 8 * ROW
 W2_FIRST_BYTES = ROW + 2 * EDGE
 ROUTED_AT = (W2_FIRST_AT + EDGE, W2_FIRST_AT + ROW // 2 + EDGE)
+Z_ROWS_LATE_AT = ROUTED_AT[1] + ROW // 2 - EDGE
 Y_ROWS_AT = W2_FIRST_AT - ROW + EDGE
 Z_FIRST_AT = 12 * ROW
+Z_LAST_AT = Z_FIRST_AT - ROW // 2 + EDGE
 LATE_CODES_AT = Z_FIRST_AT + ROW // 2 - EDGE
-OUT_BANKS = (0, 1, 6, 4, 7, 5, 2, 3)
+OUT_BANKS = (0, 1, 2, 4, 6, 3, 5, 7)
 SCALAR_ENTRIES = 96
 
 
@@ -191,20 +192,22 @@ def tile_picked_headmod_gelu_p_kernel(tc, x_words, x_scales, w1, wt, w2, offs, t
         ]
         for t in range(2):
             nc.gpsimd.tensor_tensor(z_rows[0][:, t, :], windows[t][:, halves[0]], y_rows[:, t, :], ADD)
-        sums = [(3, halves[0]), (2, quarters[0]), (2, quarters[1])] + [(t, halves[1]) for t in range(PACK)]
+        sums = [(0, halves[1])] + [(t, cols) for cols in quarters[0:2] for t in (2, 3)]
+        sums += [(t, halves[1]) for t in range(1, PACK)]
         for t, cols in sums:
             h = cols.start // HALF
             part = slice(cols.start - h * HALF, cols.stop - h * HALF)
             nc.vector.tensor_tensor(z_rows[h][:, t, part], windows[t][:, cols], y_banks[t, h * HALF][:, part], ADD)
 
         z_first = order.tile([P, QUARTER, PACK], BF16, name="z_first", offset=Z_FIRST_AT, align_bytes=EDGE)
-        z_rest = keep.tile([P, S - QUARTER, PACK], BF16, name="z_rest", align_bytes=EDGE)
-        z_parts = [z_first[:]] + [z_rest[:, a : a + QUARTER, :] for a in range(0, S - QUARTER, QUARTER)]
+        z_rest = keep.tile([P, 2, QUARTER, PACK], BF16, name="z_rest", align_bytes=EDGE)
+        z_last = order.tile([P, QUARTER, PACK], BF16, name="z_last", offset=Z_LAST_AT, align_bytes=EDGE)
+        z_parts = [z_first[:], z_rest[:, 0], z_rest[:, 1], z_last[:]]
 
         def interleave_z(q, copy):
             copy(*four_at_a_time(z_parts[q], z_rows[q // 2][:, :, q % 2 * QUARTER : (q % 2 + 1) * QUARTER]))
 
-        for q in (0, 1, 3):
+        for q in range(3):
             interleave_z(q, nc.scalar.copy)
 
         late_codes = order.tile([P, N - P + S - QUARTER], U32, name="late_codes", offset=LATE_CODES_AT, align_bytes=EDGE)
@@ -236,25 +239,26 @@ def tile_picked_headmod_gelu_p_kernel(tc, x_words, x_scales, w1, wt, w2, offs, t
         results = keep.tile([P, PACK, S], F32, name="results")
         out_view = out.rearrange("(b p) s -> p b s", p=P)
 
-        def product(n, block, passes, on_vector):
-            first, last = passes[0].start, passes[-1].stop
-            acc = psum.tile([P, last - first], F32, name=f"out_acc{n}", tag=f"bank{OUT_BANKS[n % BANKS]}")
+        def open_group(n, cols):
+            return psum.tile([P, cols.stop - cols.start], F32, name=f"out_acc{n}", tag=f"bank{OUT_BANKS[n % BANKS]}")
+
+        def product(acc, block, cols):
             codes = w2_codes[:, (block - 1) * P : block * P] if block else first_codes[:]
             scales = w2_scales[:, block * P : (block + 1) * P] if block else first_scales[:]
-            for cols in passes:
-                nc.tensor.matmul_mx(
-                    out=acc[:, cols.start - first : cols.stop - first],
-                    lhsT=codes.bitcast(FP8X4),
-                    lhsT_scale=scales,
-                    rhs=z_codes(cols).bitcast(FP8X4),
-                    rhs_scale=z_scales[:, cols],
-                    start=True,
-                    stop=True,
-                )
-            if on_vector:
-                nc.vector.tensor_copy(out=results[:, block, first:last], in_=acc[:])
-            else:
-                nc.scalar.copy(out=results[:, block, first:last], in_=acc[:])
+            nc.tensor.matmul_mx(
+                out=acc,
+                lhsT=codes.bitcast(FP8X4),
+                lhsT_scale=scales,
+                rhs=z_codes(cols).bitcast(FP8X4),
+                rhs_scale=z_scales[:, cols],
+                start=True,
+                stop=True,
+            )
+
+        def whole_group(n, block, cols, copy):
+            acc = open_group(n, cols)
+            product(acc[:], block, cols)
+            copy(out=results[:, block, cols], in_=acc[:])
 
         def store(block, cols):
             nc.sync.dma_start(out=out_view[:, block, cols], in_=results[:, block, cols])
@@ -265,26 +269,36 @@ def tile_picked_headmod_gelu_p_kernel(tc, x_words, x_scales, w1, wt, w2, offs, t
         )
         quantize_z(0)
         quantize_w2(P, w2_mid[:])
-        quantize_w2(2 * P, w2_late[:, 0:P, :])
-        interleave_z(2, nc.vector.tensor_copy)
         quantize_z(1)
+        quantize_w2(2 * P, w2_late[:, 0:P, :])
         quantize_w2(3 * P, w2_late[:, P:, :])
+        interleave_z(3, nc.vector.tensor_copy)
         quantize_z(2)
         quantize_z(3)
 
-        product(0, 0, quarters[0:1], False)
+        whole_group(0, 0, quarters[0], nc.scalar.copy)
         store(0, quarters[0])
-        product(1, 1, quarters[0:1], False)
-        product(2, 2, quarters[0:1], True)
-        product(3, 1, quarters[1:2], False)
+        for q in range(2):
+            whole_group(1 + q, 1, quarters[q], nc.scalar.copy)
         store(1, halves[0])
-        product(4, 2, quarters[1:2], True)
-        store(2, halves[0])
-        product(5, 3, quarters[0:2], False)
-        store(3, halves[0])
-        product(6, 0, quarters[1:3], True)
-        product(7, 0, quarters[3:4], False)
+        middle = slice(QUARTER, S - QUARTER)
+        acc_middle = open_group(3, middle)
+        product(acc_middle[:, quarters[0]], 0, quarters[1])
+        for block in (2, 3):
+            acc = open_group(2 + block, halves[0])
+            for q in range(2):
+                product(acc[:, quarters[q]], block, quarters[q])
+            nc.scalar.copy(out=results[:, block, halves[0]], in_=acc[:])
+            store(block, halves[0])
+        product(acc_middle[:, quarters[1]], 0, quarters[2])
+        nc.vector.tensor_copy(out=results[:, 0, middle], in_=acc_middle[:])
+        acc_late = open_group(6, halves[1])
+        product(acc_late[:, quarters[0]], 1, quarters[2])
+        whole_group(7, 0, quarters[3], nc.scalar.copy)
         store(0, slice(QUARTER, S))
-        for block in range(1, PACK):
-            product(7 + block, block, halves[1:2], block % 2 == 0)
+        product(acc_late[:, quarters[1]], 1, quarters[3])
+        nc.vector.tensor_copy(out=results[:, 1, halves[1]], in_=acc_late[:])
+        store(1, halves[1])
+        for block, copy in ((2, nc.scalar.copy), (3, nc.vector.tensor_copy)):
+            whole_group(6 + block, block, halves[1], copy)
             store(block, halves[1])

@@ -29,10 +29,12 @@ SCALAR_START = 256
 
 ROW = 4 * S
 EDGE = 64
-XS_WIN_AT = ROW
+XS_WIN_AT = 2 * ROW
 WT_AT = XS_WIN_AT + ROW // 4
 W1_CODES_AT = XS_WIN_AT + ROW - EDGE
-W1_GROUPED_AT = 3 * ROW
+W2_NEXT_AT = XS_WIN_AT - ROW + EDGE
+Z_ROWS_EARLY_AT = WT_AT + ROW // 2 - EDGE
+W1_GROUPED_AT = 4 * ROW
 W2_RAW_AT = W1_GROUPED_AT + 2 * ROW - EDGE
 XS_SPREAD_AT = 10 * ROW
 GELU3_AT = ROW
@@ -91,6 +93,9 @@ def tile_picked_headmod_gelu_p_kernel(tc, x_words, x_scales, w1, wt, w2, offs, t
         wt_t = head.tile([P, V], F32, name="wt_t", offset=WT_AT, align_bytes=EDGE)
         nc.sync.dma_start(out=wt_t[:], in_=wt.rearrange("(p f) v -> p f v", f=PACK)[:, 0, :])
 
+        w2_next = head.tile([P, PACK, P], F32, name="w2_next", offset=W2_NEXT_AT, align_bytes=EDGE)
+        nc.sync.dma_start(out=w2_next[:], in_=w2_rows[:, :, P : 2 * P])
+
         windows = [keep.tile([P, S], F32, name=f"window{t}") for t in range(PACK)]
         for window in windows:
             nc.vector.memset(window[:], 0.0)
@@ -110,8 +115,8 @@ def tile_picked_headmod_gelu_p_kernel(tc, x_words, x_scales, w1, wt, w2, offs, t
         nc.vector.quantize_mx(
             out=w1_codes[:].bitcast(FP8X4), scales=w1_scales[:], in_=w1_grouped[:].rearrange("p t m j -> p (t m j)")
         )
-        w2_raw = head.tile([P, PACK, N - P], F32, name="w2_raw", offset=W2_RAW_AT, align_bytes=EDGE)
-        nc.sync.dma_start(out=w2_raw[:], in_=w2_rows[:, :, P:N])
+        w2_raw = head.tile([P, PACK, N - 2 * P], F32, name="w2_raw", offset=W2_RAW_AT, align_bytes=EDGE)
+        nc.sync.dma_start(out=w2_raw[:], in_=w2_rows[:, :, 2 * P : N])
 
         xw = keep.tile([P, S], U32, name="xw", align_bytes=EDGE)
         for h in range(2):
@@ -173,7 +178,7 @@ def tile_picked_headmod_gelu_p_kernel(tc, x_words, x_scales, w1, wt, w2, offs, t
             nc.vector.tensor_tensor(routed[t][:], gelu_rows[t][:].indirect(take_t[:]), wt_t[:], MULT)
 
         w2_mid = order.tile([P, SCALAR_START - P, PACK], BF16, name="w2_mid", offset=W2_MID_AT, align_bytes=EDGE)
-        mid_rows = w2_raw[:, :, 0 : SCALAR_START - P].rearrange("p j c -> p c j")
+        mid_rows = w2_next[:].rearrange("p j c -> p c j")
         nc.gpsimd.tensor_scalar(w2_mid[:], mid_rows, 1.0, 0.0, MULT, ADD)
 
         cut = SCALAR_ENTRIES // GROUP
@@ -184,10 +189,10 @@ def tile_picked_headmod_gelu_p_kernel(tc, x_words, x_scales, w1, wt, w2, offs, t
         nc.scalar.activation(windows[3][:].indirect(take_t[:]), routed[3][:], COPY)
 
         w2_late = order.tile([P, N - SCALAR_START, PACK], BF16, name="w2_late", offset=W2_LATE_AT, align_bytes=EDGE)
-        nc.scalar.copy(*four_at_a_time(w2_late[:], w2_raw[:, :, SCALAR_START - P : N - P]))
+        nc.scalar.copy(*four_at_a_time(w2_late[:], w2_raw[:]))
 
         z_rows = [
-            keep.tile([P, PACK, HALF], BF16, name="z_rows0"),
+            head.tile([P, PACK, HALF], BF16, name="z_rows0", offset=Z_ROWS_EARLY_AT, align_bytes=EDGE),
             order.tile([P, PACK, HALF], BF16, name="z_rows1", offset=Z_ROWS_LATE_AT, align_bytes=EDGE),
         ]
         for t in range(2):

@@ -47,6 +47,7 @@ W2_FIRST_BYTES = ROW + 2 * EDGE
 ROUTED_AT = (W2_FIRST_AT + EDGE, W2_FIRST_AT + ROW // 2 + EDGE)
 Z_ROWS_LATE_AT = ROUTED_AT[1] + ROW // 2 - EDGE
 Y_ROWS_AT = W2_FIRST_AT - ROW + EDGE
+W2_BEHIND_AT = Y_ROWS_AT - ROW // 4 + EDGE
 Z_FIRST_AT = 12 * ROW
 Z_LAST_AT = Z_FIRST_AT - ROW // 2 + EDGE
 LATE_CODES_AT = Z_FIRST_AT + ROW // 2 - EDGE
@@ -177,9 +178,9 @@ def tile_picked_headmod_gelu_p_kernel(tc, x_words, x_scales, w1, wt, w2, offs, t
         for t in range(PACK):
             nc.vector.tensor_tensor(routed[t][:], gelu_rows[t][:].indirect(take_t[:]), wt_t[:], MULT)
 
-        w2_mid = order.tile([P, SCALAR_START - P, PACK], BF16, name="w2_mid", offset=W2_MID_AT, align_bytes=EDGE)
+        w2_mid = order.tile([P, P // 2, PACK], BF16, name="w2_mid", offset=W2_MID_AT, align_bytes=EDGE)
         mid_rows = w2_next[:].rearrange("p j c -> p c j")
-        nc.gpsimd.tensor_scalar(w2_mid[:], mid_rows, 1.0, 0.0, MULT, ADD)
+        nc.gpsimd.tensor_scalar(w2_mid[:], mid_rows[:, 0 : P // 2, :], 1.0, 0.0, MULT, ADD)
 
         cut = SCALAR_ENTRIES // GROUP
         nc.scalar.activation(windows[0][:].indirect(take_t[:]), routed[0][:], COPY)
@@ -197,6 +198,8 @@ def tile_picked_headmod_gelu_p_kernel(tc, x_words, x_scales, w1, wt, w2, offs, t
         ]
         for t in range(2):
             nc.gpsimd.tensor_tensor(z_rows[0][:, t, :], windows[t][:, halves[0]], y_rows[:, t, :], ADD)
+        w2_behind = order.tile([P, P // 2, PACK], BF16, name="w2_behind", offset=W2_BEHIND_AT, align_bytes=EDGE)
+        nc.gpsimd.tensor_scalar(w2_behind[:], mid_rows[:, P // 2 : P, :], 1.0, 0.0, MULT, ADD)
         sums = [(0, halves[1])] + [(t, cols) for cols in quarters[0:2] for t in (2, 3)]
         sums += [(t, halves[1]) for t in range(1, PACK)]
         for t, cols in sums:
@@ -274,6 +277,7 @@ def tile_picked_headmod_gelu_p_kernel(tc, x_words, x_scales, w1, wt, w2, offs, t
         )
         quantize_z(0)
         quantize_w2(P, w2_mid[:])
+        quantize_w2(P + P // 2, w2_behind[:])
         quantize_z(1)
         quantize_w2(2 * P, w2_late[:, 0:P, :])
         quantize_w2(3 * P, w2_late[:, P:, :])

@@ -97,14 +97,15 @@ def tile_picked_headmod_gelu_p_kernel(tc, x_words, x_scales, w1, wt, w2, offs, t
         w2_next = head.tile([P, PACK, P], F32, name="w2_next", offset=W2_NEXT_AT, align_bytes=EDGE)
         nc.sync.dma_start(out=w2_next[:], in_=w2_rows[:, :, P : 2 * P])
 
-        windows = [keep.tile([P, S], F32, name=f"window{t}") for t in range(PACK)]
-        for window in windows:
-            nc.vector.memset(window[:], 0.0)
-
         warm = keep.tile([P, 8], F32, name="warm")
         warm_out = keep.tile([P, 8], F32, name="warm_out")
         nc.vector.memset(warm[:], 0.0)
         nc.scalar.activation(warm_out[:], warm[:], GELU)
+
+        windows = [keep.tile([P, S], F32, name=f"window{t}") for t in range(PACK)]
+        for t in range(2):
+            nc.vector.memset(windows[t][:], 0.0)
+            nc.scalar.copy(out=windows[2 + t][:], in_=windows[t][:])
 
         w1_view = w1_raw[:].rearrange("p j (m t) -> p m j t", t=PACK)
         w1_grouped = head.tile([P, PACK, P, PACK], BF16, name="w1_grouped", offset=W1_GROUPED_AT, align_bytes=EDGE)
@@ -287,27 +288,22 @@ def tile_picked_headmod_gelu_p_kernel(tc, x_words, x_scales, w1, wt, w2, offs, t
 
         whole_group(0, 0, quarters[0], nc.scalar.copy)
         store(0, quarters[0])
-        for q in range(2):
-            whole_group(1 + q, 1, quarters[q], nc.scalar.copy)
-        store(1, halves[0])
-        middle = slice(QUARTER, S - QUARTER)
-        acc_middle = open_group(3, middle)
-        product(acc_middle[:, quarters[0]], 0, quarters[1])
-        for block in (2, 3):
-            acc = open_group(2 + block, halves[0])
+        for block in range(1, PACK):
             for q in range(2):
-                product(acc[:, quarters[q]], block, quarters[q])
-            nc.scalar.copy(out=results[:, block, halves[0]], in_=acc[:])
+                whole_group(2 * block - 1 + q, block, quarters[q], nc.scalar.copy)
             store(block, halves[0])
-        product(acc_middle[:, quarters[1]], 0, quarters[2])
+        middle = slice(QUARTER, S - QUARTER)
+        acc_middle = open_group(7, middle)
+        for q in range(2):
+            product(acc_middle[:, quarters[q]], 0, quarters[1 + q])
         nc.vector.tensor_copy(out=results[:, 0, middle], in_=acc_middle[:])
-        acc_late = open_group(6, halves[1])
+        acc_late = open_group(8, halves[1])
         product(acc_late[:, quarters[0]], 1, quarters[2])
-        whole_group(7, 0, quarters[3], nc.scalar.copy)
+        whole_group(9, 0, quarters[3], nc.scalar.copy)
         store(0, slice(QUARTER, S))
         product(acc_late[:, quarters[1]], 1, quarters[3])
         nc.vector.tensor_copy(out=results[:, 1, halves[1]], in_=acc_late[:])
         store(1, halves[1])
         for block, copy in ((2, nc.scalar.copy), (3, nc.vector.tensor_copy)):
-            whole_group(6 + block, block, halves[1], copy)
+            whole_group(8 + block, block, halves[1], copy)
             store(block, halves[1])

from contextlib import ExitStack

import concourse.mybir as mybir

K, T, S, V, N, H = 512, 2048, 512, 256, 512, 512
FLOPS = 2 * K * H * S + 2 * H * N * S

F32 = mybir.dt.float32
BF16 = mybir.dt.bfloat16
I32 = mybir.dt.int32
U32 = mybir.dt.uint32
U16 = mybir.dt.uint16
U8 = mybir.dt.uint8
FP8X4 = mybir.dt.float8_e4m3fn_x4
COPY = mybir.ActivationFunctionType.Copy
GELU = mybir.ActivationFunctionType.Gelu_apprx_tanh
ADD = mybir.AluOpType.add
MULT = mybir.AluOpType.mult

P = 128
PACK = 4
GROUP = 16
BANKS = 8
HALF = S // 2
QUARTER = S // 4

VECTOR_GROUPS = 80
SCALAR_START = 256

ROW = 4 * S
EDGE = 64
XS_WIN_AT = 2 * ROW
WT_AT = XS_WIN_AT + ROW // 4
W1_CODES_AT = XS_WIN_AT + ROW - EDGE
W2_NEXT_AT = XS_WIN_AT - ROW + EDGE
Z_ROWS_EARLY_AT = WT_AT + ROW // 2 - EDGE
W1_GROUPED_AT = 4 * ROW
W2_RAW_AT = W1_GROUPED_AT + 2 * ROW - EDGE
XS_SPREAD_AT = 10 * ROW
GELU3_AT = ROW
W2_MID_AT = GELU3_AT + ROW - EDGE
W2_LATE_AT = GELU3_AT - ROW + EDGE
ROUTED_LATE_AT = (4 * ROW, 5 * ROW + ROW // 2 - 2 * EDGE)
FIRST_CODES_AT = ROUTED_LATE_AT[1] + ROW // 2 - EDGE
W2_FIRST_AT = 8 * ROW
W2_FIRST_BYTES = ROW + 2 * EDGE
ROUTED_AT = (W2_FIRST_AT + EDGE, W2_FIRST_AT + ROW // 2 + EDGE)
Z_ROWS_LATE_AT = ROUTED_AT[1] + ROW // 2 - EDGE
Y_ROWS_AT = W2_FIRST_AT - ROW + EDGE
W2_BEHIND_AT = Y_ROWS_AT - ROW // 4 + EDGE
Z_FIRST_AT = 12 * ROW
Z_LAST_AT = Z_FIRST_AT - ROW // 2 + EDGE
LATE_CODES_AT = Z_FIRST_AT + ROW // 2 - EDGE
OUT_BANKS = (0, 1, 2, 4, 6, 3, 5, 7)
SCALAR_ENTRIES = 96


def tile_picked_headmod_gelu_p_kernel(tc, x_words, x_scales, w1, wt, w2, offs, take, out):
    nc = tc.nc
    with ExitStack() as ctx:
        keep = ctx.enter_context(tc.tile_pool(name="keep", bufs=1))
        order = ctx.enter_context(tc.tile_pool(name="order", bufs=1))
        psum = ctx.enter_context(tc.psum_pool(name="psum", bufs=1))

        offs_t = keep.tile([P, S // GROUP], U16, name="offs_t")
        take_t = keep.tile([P, V // GROUP], U16, name="take_t")
        head = ctx.enter_context(tc.tile_pool(name="head", bufs=1))
        xs_win = head.tile([P, T], U8, name="xs_win", offset=XS_WIN_AT, align_bytes=EDGE)
        xw_win = keep.tile([P, T], I32, name="xw_win", align_bytes=EDGE)
        w1_raw = keep.tile([P, PACK, H], F32, name="w1_raw")

        nc.vector.memset(xs_win[:].bitcast(I32), 0)
        w1_rows = w1.rearrange("(p j) c -> p j c", j=PACK)
        nc.sync.dma_start(out=w1_raw[:, 0:2, :], in_=w1_rows[:, 0:2, :])
        nc.sync.dma_start(out=xs_win[4:P:8, :].bitcast(I32), in_=x_scales[0].bitcast(I32))
        nc.sync.dma_start(offs_t[:], offs)
        nc.sync.dma_start(out=w1_raw[:, 2:4, :], in_=w1_rows[:, 2:4, :])
        nc.sync.dma_start(out=xw_win[:], in_=x_words[0].rearrange("p c r -> p (c r)").bitcast(I32))

        xs_spread = head.tile([P, S], U8, name="xs_spread", offset=XS_SPREAD_AT, align_bytes=EDGE)
        nc.vector.tensor_copy(xs_spread[:], xs_win[:].indirect(offs_t[:]))
        xs = keep.tile([P, S], U8, name="xs", align_bytes=EDGE)
        nc.vector.memset(xs[:].bitcast(I32), 0)
        for q in range(4):
            nc.sync.dma_start(
                out=xs[32 * q : 32 * q + 4, :].bitcast(I32), in_=xs_spread[32 * q + 4 : 32 * q + 32 : 8, :].bitcast(I32)
            )

        w2_rows = w2.rearrange("(p j) c -> p j c", j=PACK)
        nc.sync.dma_start(take_t[:], take)
        w2_early_room = order.tile([P, W2_FIRST_BYTES // 4], F32, name="w2_early", offset=W2_FIRST_AT, align_bytes=EDGE)
        w2_early = w2_early_room[:, 0 : PACK * P].rearrange("p (j c) -> p j c", j=PACK)
        nc.sync.dma_start(out=w2_early, in_=w2_rows[:, :, 0:P])
        wt_t = head.tile([P, V], F32, name="wt_t", offset=WT_AT, align_bytes=EDGE)
        nc.sync.dma_start(out=wt_t[:], in_=wt.rearrange("(p f) v -> p f v", f=PACK)[:, 0, :])

        w2_next = head.tile([P, PACK, P], F32, name="w2_next", offset=W2_NEXT_AT, align_bytes=EDGE)
        nc.sync.dma_start(out=w2_next[:], in_=w2_rows[:, :, P : 2 * P])

        warm = keep.tile([P, 8], F32, name="warm")
        warm_out = keep.tile([P, 8], F32, name="warm_out")
        nc.vector.memset(warm[:], 0.0)
        nc.scalar.activation(warm_out[:], warm[:], GELU)

        windows = [keep.tile([P, S], F32, name=f"window{t}") for t in range(PACK)]
        for t in range(2):
            nc.vector.memset(windows[t][:], 0.0)
            nc.scalar.copy(out=windows[2 + t][:], in_=windows[t][:])

        w1_view = w1_raw[:].rearrange("p j (m t) -> p m j t", t=PACK)
        w1_grouped = head.tile([P, PACK, P, PACK], BF16, name="w1_grouped", offset=W1_GROUPED_AT, align_bytes=EDGE)
        w1_dealt = w1_grouped[:].rearrange("p t m j -> p m j t")
        nc.vector.tensor_copy(out=w1_dealt[:, 0:VECTOR_GROUPS], in_=w1_view[:, 0:VECTOR_GROUPS])
        nc.scalar.copy(out=w1_dealt[:, VECTOR_GROUPS:P], in_=w1_view[:, VECTOR_GROUPS:P])
        w1_codes = head.tile([P, H], U32, name="w1_codes", offset=W1_CODES_AT, align_bytes=EDGE)
        w1_scales = keep.tile([P, H], U8, name="w1_scales", align_bytes=EDGE)
        nc.vector.quantize_mx(
            out=w1_codes[:].bitcast(FP8X4), scales=w1_scales[:], in_=w1_grouped[:].rearrange("p t m j -> p (t m j)")
        )
        w2_raw = head.tile([P, PACK, N - 2 * P], F32, name="w2_raw", offset=W2_RAW_AT, align_bytes=EDGE)
        nc.sync.dma_start(out=w2_raw[:], in_=w2_rows[:, :, 2 * P : N])

        xw = keep.tile([P, S], U32, name="xw", align_bytes=EDGE)
        for h in range(2):
            nc.vector.tensor_copy(
                xw[:, h * HALF : (h + 1) * HALF],
                xw_win[:].bitcast(U32).indirect(offs_t[:, h * HALF // GROUP : (h + 1) * HALF // GROUP]),
            )

        def first_layer(t, cols, bank, again=0):
            acc = psum.tile([P, cols.stop - cols.start], F32, name=f"y_acc{t}_{cols.start}_{bank}_{again}", tag=f"bank{bank}")
            stat = slice(t * P, (t + 1) * P)
            nc.tensor.matmul_mx(
                out=acc[:],
                lhsT=w1_codes[:, stat].bitcast(FP8X4),
                lhsT_scale=w1_scales[:, stat],
                rhs=xw[:, cols].bitcast(FP8X4),
                rhs_scale=xs[:, cols],
                start=True,
                stop=True,
            )
            return acc

        halves = [slice(0, HALF), slice(HALF, S)]
        quarters = [slice(a, a + QUARTER) for a in range(0, S, QUARTER)]
        gelu_rows = [
            keep.tile([P, S], F32, name="gelu_rows0"),
            keep.tile([P, S], F32, name="gelu_rows1"),
            keep.tile([P, S], F32, name="gelu_rows2"),
            order.tile([P, S], F32, name="gelu_rows3", offset=GELU3_AT, align_bytes=EDGE),
        ]

        def four_at_a_time(grouped, raw):
            return grouped.rearrange("p (c i) j -> p c j i", i=4), raw.rearrange("p j (c i) -> p c j i", i=4)

        y_passes = [(0, halves[0]), (1, halves[0]), (0, halves[1]), (1, halves[1])]
        y_passes += [(t, cols) for t in (2, 3) for cols in halves]
        y_banks = {}

        def first_layer_gelu(t, cols, bank):
            y_banks[t, cols.start] = first_layer(t, cols, bank)
            nc.scalar.activation(gelu_rows[t][:, cols], y_banks[t, cols.start][:], GELU)

        for bank, (t, cols) in enumerate(y_passes):
            first_layer_gelu(t, cols, bank)

        w2_first = keep.tile([P, P, PACK], BF16, name="w2_first", align_bytes=EDGE)
        nc.vector.tensor_copy(*four_at_a_time(w2_first[:], w2_early))
        w2_scales = keep.tile([P, N], U8, name="w2_scales", align_bytes=EDGE)
        first_scales = keep.tile([P, P], U8, name="first_scales", align_bytes=EDGE)
        y_rows = order.tile([P, 2, HALF], F32, name="y_rows", offset=Y_ROWS_AT, align_bytes=EDGE)
        for t in range(2):
            nc.vector.tensor_copy(out=y_rows[:, t, :], in_=y_banks[t, 0][:])

        routed = [
            order.tile([P, V], F32, name=f"routed{t}", offset=at, align_bytes=EDGE)
            for t, at in enumerate(ROUTED_AT + ROUTED_LATE_AT)
        ]
        for t in range(PACK):
            nc.vector.tensor_tensor(routed[t][:], gelu_rows[t][:].indirect(take_t[:]), wt_t[:], MULT)

        w2_mid = order.tile([P, P // 2, PACK], BF16, name="w2_mid", offset=W2_MID_AT, align_bytes=EDGE)
        mid_rows = w2_next[:].rearrange("p j c -> p c j")
        nc.gpsimd.tensor_scalar(w2_mid[:], mid_rows[:, 0 : P // 2, :], 1.0, 0.0, MULT, ADD)

        cut = SCALAR_ENTRIES // GROUP
        nc.scalar.activation(windows[0][:].indirect(take_t[:]), routed[0][:], COPY)
        nc.vector.tensor_copy(windows[1][:].indirect(take_t[:]), routed[1][:])
        nc.scalar.activation(windows[2][:].indirect(take_t[:, 0:cut]), routed[2][:, 0:SCALAR_ENTRIES], COPY)
        nc.vector.tensor_copy(windows[2][:].indirect(take_t[:, cut:]), routed[2][:, SCALAR_ENTRIES:V])
        nc.scalar.activation(windows[3][:].indirect(take_t[:]), routed[3][:], COPY)

        w2_late = order.tile([P, N - SCALAR_START, PACK], BF16, name="w2_late", offset=W2_LATE_AT, align_bytes=EDGE)
        nc.scalar.copy(*four_at_a_time(w2_late[:], w2_raw[:]))

        z_rows = [
            head.tile([P, PACK, HALF], BF16, name="z_rows0", offset=Z_ROWS_EARLY_AT, align_bytes=EDGE),
            order.tile([P, PACK, HALF], BF16, name="z_rows1", offset=Z_ROWS_LATE_AT, align_bytes=EDGE),
        ]
        for t in range(2):
            nc.gpsimd.tensor_tensor(z_rows[0][:, t, :], windows[t][:, halves[0]], y_rows[:, t, :], ADD)
        w2_behind = order.tile([P, P // 2, PACK], BF16, name="w2_behind", offset=W2_BEHIND_AT, align_bytes=EDGE)
        nc.gpsimd.tensor_scalar(w2_behind[:], mid_rows[:, P // 2 : P, :], 1.0, 0.0, MULT, ADD)
        sums = [(0, halves[1])] + [(t, cols) for cols in quarters[0:2] for t in (2, 3)]
        sums += [(t, halves[1]) for t in range(1, PACK)]
        for t, cols in sums:
            h = cols.start // HALF
            part = slice(cols.start - h * HALF, cols.stop - h * HALF)
            nc.vector.tensor_tensor(z_rows[h][:, t, part], windows[t][:, cols], y_banks[t, h * HALF][:, part], ADD)

        z_first = order.tile([P, QUARTER, PACK], BF16, name="z_first", offset=Z_FIRST_AT, align_bytes=EDGE)
        z_rest = keep.tile([P, 2, QUARTER, PACK], BF16, name="z_rest", align_bytes=EDGE)
        z_last = order.tile([P, QUARTER, PACK], BF16, name="z_last", offset=Z_LAST_AT, align_bytes=EDGE)
        z_parts = [z_first[:], z_rest[:, 0], z_rest[:, 1], z_last[:]]

        def interleave_z(q, copy):
            copy(*four_at_a_time(z_parts[q], z_rows[q // 2][:, :, q % 2 * QUARTER : (q % 2 + 1) * QUARTER]))

        for q in range(3):
            interleave_z(q, nc.scalar.copy)

        late_codes = order.tile([P, N - P + S - QUARTER], U32, name="late_codes", offset=LATE_CODES_AT, align_bytes=EDGE)
        w2_codes = late_codes[:, 0 : N - P]
        z_first_codes = keep.tile([P, QUARTER], U32, name="z_first_codes", align_bytes=EDGE)

        def z_codes(cols):
            if cols.start == 0:
                return z_first_codes[:]
            return late_codes[:, N - P - QUARTER + cols.start : N - P - QUARTER + cols.stop]

        def quantize_w2(first, grouped):
            last = first + grouped.shape[1]
            nc.vector.quantize_mx(
                out=w2_codes[:, first - P : last - P].bitcast(FP8X4),
                scales=w2_scales[:, first:last],
                in_=grouped.rearrange("p c j -> p (c j)"),
            )

        z_scales = keep.tile([P, S], U8, name="z_scales", align_bytes=EDGE)

        def quantize_z(q):
            nc.vector.quantize_mx(
                out=z_codes(quarters[q]).bitcast(FP8X4),
                scales=z_scales[:, quarters[q]],
                in_=z_parts[q].rearrange("p c j -> p (c j)"),
            )

        results = keep.tile([P, PACK, S], F32, name="results")
        out_view = out.rearrange("(b p) s -> p b s", p=P)

        def open_group(n, cols):
            return psum.tile([P, cols.stop - cols.start], F32, name=f"out_acc{n}", tag=f"bank{OUT_BANKS[n % BANKS]}")

        def product(acc, block, cols):
            codes = w2_codes[:, (block - 1) * P : block * P] if block else first_codes[:]
            scales = w2_scales[:, block * P : (block + 1) * P] if block else first_scales[:]
            nc.tensor.matmul_mx(
                out=acc,
                lhsT=codes.bitcast(FP8X4),
                lhsT_scale=scales,
                rhs=z_codes(cols).bitcast(FP8X4),
                rhs_scale=z_scales[:, cols],
                start=True,
                stop=True,
            )

        def whole_group(n, block, cols, copy):
            acc = open_group(n, cols)
            product(acc[:], block, cols)
            copy(out=results[:, block, cols], in_=acc[:])

        def store(block, cols):
            nc.sync.dma_start(out=out_view[:, block, cols], in_=results[:, block, cols])

        first_codes = order.tile([P, P], U32, name="first_codes", offset=FIRST_CODES_AT, align_bytes=EDGE)
        nc.vector.quantize_mx(
            out=first_codes[:].bitcast(FP8X4), scales=first_scales[:], in_=w2_first[:].rearrange("p c j -> p (c j)")
        )
        quantize_z(0)
        quantize_w2(P, w2_mid[:])
        quantize_w2(P + P // 2, w2_behind[:])
        quantize_z(1)
        quantize_w2(2 * P, w2_late[:, 0:P, :])
        quantize_w2(3 * P, w2_late[:, P:, :])
        interleave_z(3, nc.vector.tensor_copy)
        quantize_z(2)
        quantize_z(3)

        whole_group(0, 0, quarters[0], nc.scalar.copy)
        store(0, quarters[0])
        for block in range(1, PACK):
            for q in range(2):
                whole_group(2 * block - 1 + q, block, quarters[q], nc.scalar.copy)
            store(block, halves[0])
        middle = slice(QUARTER, S - QUARTER)
        acc_middle = open_group(7, middle)
        for q in range(2):
            product(acc_middle[:, quarters[q]], 0, quarters[1 + q])
        nc.vector.tensor_copy(out=results[:, 0, middle], in_=acc_middle[:])
        acc_late = open_group(8, halves[1])
        product(acc_late[:, quarters[0]], 1, quarters[2])
        whole_group(9, 0, quarters[3], nc.scalar.copy)
        store(0, slice(QUARTER, S))
        product(acc_late[:, quarters[1]], 1, quarters[3])
        nc.vector.tensor_copy(out=results[:, 1, halves[1]], in_=acc_late[:])
        store(1, halves[1])
        for block, copy in ((2, nc.scalar.copy), (3, nc.vector.tensor_copy)):
            whole_group(8 + block, block, halves[1], copy)
            store(block, halves[1])
